import numpy as np
import ml_dtypes


def mxq(x, axis, fmt="e4m3"):
    dtype, down = {"e4m3": (ml_dtypes.float8_e4m3fn, 7), "e5m2": (ml_dtypes.float8_e5m2, 14)}[fmt]
    v = np.moveaxis(np.asarray(x, np.float32).astype(ml_dtypes.bfloat16).astype(np.float64), axis, -1)
    blocks = v.reshape(v.shape[:-1] + (-1, 32))
    amax = np.abs(blocks).max(-1, keepdims=True)
    byte = np.maximum(np.where(amax > 0, np.frexp(amax)[1] - 1 + 127, 0) - down, 1)
    scale = np.exp2(byte - 127.0)
    codes = (blocks / scale).astype(np.float32).astype(dtype).astype(np.float64)
    return np.moveaxis((codes * scale).reshape(v.shape), -1, axis)


WIDE = False


def mx_kscale(k):
    if not WIDE:
        return np.ones(k)
    levels = np.array([10, -10, 5, -5, 0])
    if k % 512:
        return np.exp2(np.random.permutation(np.resize(levels, k // 32))).repeat(32)
    a = np.empty((k // 512, 16))
    for p in range(k // 512):
        a[p, :8] = np.random.permutation(np.resize(levels, 8))
        for g in range(8):
            far = levels[np.abs(levels - a[p, g]) >= 10]
            a[p, g + 8] = far[np.random.randint(len(far))]
    return np.exp2(a.ravel()).repeat(32)


def f64(x):
    return np.asarray(x).astype(np.float64)


def striped(idx):
    return np.tile(idx.reshape(-1, 16).T, (8, 1)).astype(np.uint16)


def unstriped(offs):
    return offs[:16].T.reshape(-1).astype(np.int64)


E2M1 = np.array([0.0, 0.5, 1.0, 1.5, 2.0, 3.0, 4.0, 6.0, -0.0, -0.5, -1.0, -1.5, -2.0, -3.0, -4.0, -6.0])


def pack_weight(w, fmt):
    k, n = w.shape
    w = f64(np.asarray(w, np.float32).astype(ml_dtypes.bfloat16)).reshape(k // 32, 32, n)
    amax = np.abs(w).max(1)
    if fmt == "e4m3":
        byte = np.frexp(amax)[1] - 1 + 127 - 7
    else:
        mant, ex = np.frexp(amax / 6.0)
        byte = np.where(mant > 0.5, ex, ex - 1) + 127
    byte = np.clip(np.where(amax > 0, byte, 1), 1, 254)
    scaled = (w * np.exp2(127.0 - byte)[:, None, :]).reshape(k, n).astype(np.float32)
    by_word = np.ascontiguousarray(scaled.reshape(k // 512, 128, 4, n).transpose(0, 1, 3, 2))
    if fmt == "e4m3":
        words = by_word.astype(ml_dtypes.float8_e4m3fn).view(np.uint8)
    else:
        c = by_word.astype(ml_dtypes.float4_e2m1fn).view(np.uint8) & 0xF
        words = (c[..., 0::2] | (c[..., 1::2] << 4)).reshape(k // 512, 128, 2 * n)
    return np.ascontiguousarray(words), np.ascontiguousarray(byte.astype(np.uint8).reshape(k // 512, 16, n))


def unpack_weight(words, scales, fmt):
    g, _, n = scales.shape
    words = np.ascontiguousarray(words).reshape(g, 128, n, -1)
    if fmt == "e4m3":
        vals = words.view(ml_dtypes.float8_e4m3fn).astype(np.float64)
    else:
        nib = np.empty((g, 128, n, 4), np.uint8)
        nib[..., 0::2] = words & 0xF
        nib[..., 1::2] = words >> 4
        vals = E2M1[nib]
    vals = vals * np.repeat(np.exp2(scales.astype(np.float64) - 127.0), 8, axis=1)[..., None]
    return vals.transpose(0, 1, 3, 2).reshape(g * 512, n)


def d_silu(v):
    s = 1.0 / (1.0 + np.exp(-np.maximum(v, -700.0)))
    return s * (1.0 + v * (1.0 - s))


K, T, E, C, H, N = 256, 1024, 4, 256, 512, 1024


def by_expert(wq, xq):
    return np.concatenate([wq[e].T @ xq[:, e * C:(e + 1) * C] for e in range(E)], axis=1)


def setup_inputs():
    n = np.random.standard_normal
    v = mx_kscale(N)
    u = mx_kscale(H)
    slot_token = np.random.permutation(T)[:E * C]
    w_slot = np.random.uniform(0.2, 1.0, E * C)
    partner = np.random.permutation(T)[:E * C]
    dy = pack_weight(n((N, T)) * v[:, None], "e4m3")
    w2t = [pack_weight(m, "e2m1") for m in n((E, N, H)) / np.sqrt(N) / v[None, :, None] * u]
    w1t = [pack_weight(m, "e2m1") for m in n((E, H, K)) / np.sqrt(H) / u[None, :, None]]
    wpt = [pack_weight(m, "e4m3") for m in n((E, H, K)) / np.sqrt(H) / u[None, :, None]]
    return {
        "dy_words": dy[0],
        "dy_scales": dy[1],
        "w2t_words": np.stack([m[0] for m in w2t]),
        "w2t_scales": np.stack([m[1] for m in w2t]),
        "w1t_words": np.stack([m[0] for m in w1t]),
        "w1t_scales": np.stack([m[1] for m in w1t]),
        "wpt_words": np.stack([m[0] for m in wpt]),
        "wpt_scales": np.stack([m[1] for m in wpt]),
        "a": (n((H, E * C))).astype(np.float32),
        "gate": (np.tile(w_slot, (128, 1))).astype(np.float32),
        "offs": striped(slot_token),
        "offs2": striped(partner),
    }


def reference(dy_words, dy_scales, w2t_words, w2t_scales, w1t_words, w1t_scales, wpt_words, wpt_scales, a, gate, offs, offs2):
    w2t = np.stack([unpack_weight(w2t_words[e], w2t_scales[e], "e2m1") for e in range(E)])
    w1t = np.stack([unpack_weight(w1t_words[e], w1t_scales[e], "e2m1") for e in range(E)])
    wpt = np.stack([unpack_weight(wpt_words[e], wpt_scales[e], "e4m3") for e in range(E)])
    idx, idx2 = unstriped(offs), unstriped(offs2)
    gq = unpack_weight(dy_words, dy_scales, "e4m3")[:, idx]
    dh = f64(gate[:1]) * by_expert(w2t, gq) * d_silu(f64(a))
    dq = mxq(dh, 0, "e4m3")
    out = np.zeros((K, T))
    out[:, idx] = by_expert(w1t, dq)
    out[:, idx2] += by_expert(wpt, dq)
    return out

@@ -1,0 +1,227 @@
+from contextlib import ExitStack
+
+import concourse.mybir as mybir
+from concourse.masks import make_identity
+
+K, T, E, C, H, N = 256, 1024, 4, 256, 512, 1024
+FLOPS = 2 * E * C * (N * H + 2 * H * K)
+
+F32 = mybir.dt.float32
+BF16 = mybir.dt.bfloat16
+I32 = mybir.dt.int32
+U32 = mybir.dt.uint32
+U16 = mybir.dt.uint16
+U8 = mybir.dt.uint8
+FP8X4 = mybir.dt.float8_e4m3fn_x4
+FP4X4 = mybir.dt.float4_e2m1fn_x4
+ACT = mybir.ActivationFunctionType
+ALU = mybir.AluOpType
+
+P = 128
+PASSES = N // 512
+SLOTS = E * C
+GROUP = 16
+HALF = SLOTS // 2
+TILES = SLOTS // P
+TPE = C // P
+KT = K // P
+
+
+def load_scale_rows(queue, plane, rows):
+    m = rows.shape[0]
+    for q in range(4):
+        queue.dma_start(
+            out=plane[32 * q : 32 * q + 4, :].bitcast(I32).rearrange("b (m w) -> b m w", m=m),
+            in_=rows[:, 4 * q : 4 * q + 4, :].bitcast(I32).rearrange("m b w -> b m w"),
+        )
+
+
+def tile_moe_dub_silu_kernel(
+    tc, dy_words, dy_scales, w2t_words, w2t_scales, w1t_words, w1t_scales, wpt_words, wpt_scales, a, gate, offs, offs2, out
+):
+    nc = tc.nc
+    with ExitStack() as ctx:
+        lists = ctx.enter_context(tc.tile_pool(name="lists", bufs=1))
+        keep = ctx.enter_context(tc.tile_pool(name="keep", bufs=1))
+        psum = ctx.enter_context(tc.psum_pool(name="psum", bufs=2))
+
+        token_list = lists.tile([P, SLOTS // GROUP], U16, name="token_list")
+        partner_list = lists.tile([P, SLOTS // GROUP], U16, name="partner_list")
+
+        dy_sc = keep.tile([P, T], U8, name="dy_sc", align_bytes=64)
+        w2_sc = keep.tile([P, E * PASSES * H], U8, name="w2_sc", align_bytes=64)
+        w1_sc = keep.tile([P, E * K], U8, name="w1_sc", align_bytes=64)
+        wp_sc = keep.tile([P, E * K], U8, name="wp_sc", align_bytes=64)
+        g_sc = [keep.tile([P, SLOTS], U8, name=f"g_sc{s}", align_bytes=64) for s in range(PASSES)]
+        for plane in (dy_sc, w2_sc, g_sc[1], w1_sc, wp_sc):
+            nc.vector.memset(plane[:].bitcast(I32), 0)
+
+        ident = keep.tile([P, P], F32, name="ident")
+        gate_rows = keep.tile([P, P], F32, name="gate_rows")
+        nc.gpsimd.memset(gate_rows[:], 0.0)
+        make_identity(nc, ident[:])
+
+        dy_w = [keep.tile([P, T], I32, name=f"dy_w{s}", align_bytes=64) for s in range(PASSES)]
+        a_sb = [keep.tile([P, H // P, C], F32, name=f"a_sb{e}", align_bytes=64) for e in range(E)]
+        w2_w = [keep.tile([P, PASSES, 2 * H], U8, name=f"w2_w{e}", align_bytes=64) for e in range(E)]
+        w1_w = keep.tile([P, E, 2 * K], U8, name="w1_w", align_bytes=64)
+        wp_w = keep.tile([P, E, 4 * K], U8, name="wp_w", align_bytes=64)
+
+        def load_a(e):
+            nc.sync.dma_start(out=a_sb[e][:], in_=a[:, e * C : (e + 1) * C].rearrange("(c p) j -> p c j", p=P))
+
+        def load_w2(e):
+            nc.sync.dma_start(out=w2_w[e][:].bitcast(I32), in_=w2t_words[e].bitcast(I32).rearrange("s p w -> p s w"))
+
+        nc.sync.dma_start(token_list[:], offs)
+        for q in range(4):
+            nc.sync.dma_start(
+                out=dy_sc[32 * q : 32 * q + 4 * PASSES, :].bitcast(I32),
+                in_=dy_scales[:, 4 * q : 4 * q + 4, :].bitcast(I32),
+            )
+        for s in range(PASSES):
+            nc.sync.dma_start(out=dy_w[s][:], in_=dy_words[s].rearrange("p n t -> p (n t)").bitcast(I32))
+        load_a(0)
+        load_a(1)
+        load_scale_rows(nc.sync, w2_sc, w2t_scales.rearrange("e s b w -> (e s) b w"))
+        load_w2(0)
+        nc.sync.dma_start(out=gate_rows[0:TILES, :], in_=gate[0:1, :].rearrange("o (s c) -> (o s) c", c=P))
+        load_w2(1)
+        load_a(2)
+        load_a(3)
+        nc.sync.dma_start(out=w1_w[:].bitcast(I32), in_=w1t_words.bitcast(I32).rearrange("e s p w -> p (e s) w"))
+        nc.sync.dma_start(
+            out=wp_w[:].bitcast(I32), in_=wpt_words.rearrange("e s p k d -> p (e s) (k d)").bitcast(I32)
+        )
+        nc.sync.dma_start(partner_list[:], offs2)
+        load_w2(2)
+        load_w2(3)
+        load_scale_rows(nc.gpsimd, w1_sc, w1t_scales.rearrange("e s b w -> (e s) b w"))
+        load_scale_rows(nc.gpsimd, wp_sc, wpt_scales.rearrange("e s b w -> (e s) b w"))
+
+        g_w = [[keep.tile([P, HALF], U32, name=f"g_w{h}{s}", align_bytes=64) for s in range(PASSES)] for h in range(2)]
+        for h in range(2):
+            entries = token_list[:, h * HALF // GROUP : (h + 1) * HALF // GROUP]
+            nc.vector.tensor_copy(g_sc[0][:, h * HALF : (h + 1) * HALF], dy_sc[:].indirect(entries))
+        for q in range(4):
+            nc.scalar.dma_start(
+                out=g_sc[1][32 * q : 32 * q + 4, :].bitcast(I32),
+                in_=g_sc[0][32 * q + 4 : 32 * q + 8, :].bitcast(I32),
+            )
+        for h in range(2):
+            entries = token_list[:, h * HALF // GROUP : (h + 1) * HALF // GROUP]
+            for s in range(PASSES):
+                nc.vector.tensor_copy(g_w[h][s][:], dy_w[s][:].bitcast(U32).indirect(entries))
+
+        gate_ps = psum.tile([P, P], F32, name="gate_ps", tag="turn")
+        nc.tensor.transpose(gate_ps[:], gate_rows[:], ident[:])
+        neg_gate = keep.tile([P, TILES], F32, name="neg_gate")
+        nc.vector.tensor_scalar(neg_gate[:], gate_ps[:, 0:TILES], -1.0, None, ALU.mult)
+
+        sig = [keep.tile([P, TPE * H], F32, name=f"sig{e}") for e in range(E)]
+        rest = [keep.tile([P, TPE * H], F32, name=f"rest{e}") for e in range(E)]
+
+        def activate(e, dest, func, scale):
+            for u in range(TPE):
+                a_ps = psum.tile([P, H], F32, name="a_ps", tag="a_ps")
+                for c in range(H // P):
+                    nc.tensor.transpose(a_ps[:, c * P : (c + 1) * P], a_sb[e][:, c, u * P : (u + 1) * P], ident[:])
+                nc.scalar.activation(dest[e][:, u * H : (u + 1) * H], a_ps[:], func, scale=scale)
+
+        for e in (0, 1):
+            activate(e, sig, ACT.Sigmoid, 1.0)
+        for e in range(E):
+            activate(e, rest, ACT.Silu, -1.0)
+        for e in (2, 3):
+            activate(e, sig, ACT.Sigmoid, 1.0)
+
+        stage = [keep.tile([P, 2, SLOTS], F32, name=f"stage{kt}") for kt in range(KT)]
+        window = [[keep.tile([P, T], F32, name=f"window{kt}{w}") for w in range(2)] for kt in range(KT)]
+        dh_rows = {}
+        dq = {}
+
+        def make_dh(e):
+            neg_d = keep.tile([P, TPE * H], F32, name=f"neg_d{e}")
+            nc.vector.scalar_tensor_tensor(neg_d[:], rest[e][:], 1.0, sig[e][:], ALU.subtract, ALU.mult)
+            turned = psum.tile([P, TPE, 2, P], F32, name="turned", tag="turn")
+            for u in range(TPE):
+                t = e * TPE + u
+                h, c0 = divmod(t * P, HALF)
+                sums = psum.tile([P, H], F32, name="sums", tag="sums")
+                for s in range(PASSES):
+                    m = e * PASSES + s
+                    nc.tensor.matmul_mx(
+                        out=sums[:],
+                        lhsT=g_w[h][s][:, c0 : c0 + P].bitcast(FP8X4),
+                        lhsT_scale=g_sc[s][:, t * P : (t + 1) * P],
+                        rhs=w2_w[e][:, s, :].bitcast(FP4X4),
+                        rhs_scale=w2_sc[:, m * H : (m + 1) * H],
+                        start=(s == 0),
+                        stop=(s == PASSES - 1),
+                    )
+                dh_t = keep.tile([P, H], BF16, name=f"dh_t{t}", align_bytes=64)
+                nc.vector.scalar_tensor_tensor(
+                    dh_t[:], sums[:], neg_gate[:, t : t + 1], neg_d[:, u * H : (u + 1) * H], ALU.mult, ALU.mult
+                )
+                pairs = dh_t[:].bitcast(F32)
+                for v in range(2):
+                    nc.tensor.transpose(turned[:, u, v, :], pairs[:, v : H // 2 : 2], ident[:])
+            dh_rows[e] = keep.tile([P, C * 4], BF16, name=f"dh_rows{e}", align_bytes=64)
+            nc.scalar.copy(
+                dh_rows[e][:].bitcast(F32).rearrange("p (u j v) -> p u j v", u=TPE, v=2),
+                turned[:].rearrange("p u v j -> p u j v"),
+            )
+
+        def multiply(e):
+            codes = keep.tile([P, C], U32, name=f"dq_w{e}", align_bytes=64)
+            scales = keep.tile([P, C], U8, name=f"dq_sc{e}", align_bytes=64)
+            nc.vector.quantize_mx(out=codes[:].bitcast(FP8X4), scales=scales[:], in_=dh_rows[e][:])
+            for kt in range(KT):
+                both = psum.tile([P, 2, C], F32, name="both", tag="both")
+                cols = slice(e * K + kt * P, e * K + (kt + 1) * P)
+                nc.tensor.matmul_mx(
+                    out=both[:, 0, :],
+                    lhsT=w1_w[:, e, 2 * kt * P : 2 * (kt + 1) * P].bitcast(FP4X4),
+                    lhsT_scale=w1_sc[:, cols],
+                    rhs=codes[:].bitcast(FP8X4),
+                    rhs_scale=scales[:],
+                    start=True,
+                    stop=True,
+                )
+                nc.tensor.matmul_mx(
+                    out=both[:, 1, :],
+                    lhsT=wp_w[:, e, 4 * kt * P : 4 * (kt + 1) * P].bitcast(FP8X4),
+                    lhsT_scale=wp_sc[:, cols],
+                    rhs=codes[:].bitcast(FP8X4),
+                    rhs_scale=scales[:],
+                    start=True,
+                    stop=True,
+                )
+                nc.scalar.copy(stage[kt][:, :, e * C : (e + 1) * C], both[:])
+
+        def scatter(e, kt, w):
+            entries = (token_list, partner_list)[w][:, e * C // GROUP : (e + 1) * C // GROUP]
+            nc.vector.tensor_copy(window[kt][w][:].indirect(entries), stage[kt][:, w, e * C : (e + 1) * C])
+
+        def finish(kt, lo, hi):
+            total = keep.tile([P, hi - lo], F32, name=f"total{kt}_{lo}")
+            nc.vector.tensor_tensor(total[:], window[kt][0][:, lo:hi], window[kt][1][:, lo:hi], ALU.add)
+            nc.sync.dma_start(out=out[kt * P : (kt + 1) * P, lo:hi], in_=total[:])
+
+        make_dh(0)
+        make_dh(1)
+        multiply(0)
+        make_dh(2)
+        multiply(1)
+        for e in range(E):
+            if e + 3 < E:
+                make_dh(e + 3)
+            for kt in range(KT):
+                for w in range(2):
+                    scatter(e, kt, w)
+                    if e == E - 1 and (kt, w) == (1, 0):
+                        finish(0, 0, T)
+            if e + 2 < E:
+                multiply(e + 2)
+        finish(1, 0, T // 2)
+        finish(1, T // 2, T)

@@ -25,6 +25,7 @@ HALF = SLOTS // 2
 TILES = SLOTS // P
 TPE = C // P
 KT = K // P
+OPT = {'sa': (4, 5, 2), 'a0': 1, 'gq': 0, 'loads': 'w2s w20 gate move a1 w10 wp0 w1s wps o2 a23 w2r w1r wpr', 'warm': 0, 'split': (0, 3), 'pool': (), 't31': 'dh_t3', 'first': ((0, 1), (1, 2)), 'g_early': ((0, 4, 0), (0, 4, 1), (4, 8, 0)), 'g_late': ((4, 8, 1, 'dh_t0'),)}
 
 
 def load_scale_rows(queue, plane, rows):
@@ -62,126 +63,181 @@ def tile_moe_dub_silu_kernel(
         make_identity(nc, ident[:])
 
         dy_w = [keep.tile([P, T], I32, name=f"dy_w{s}", align_bytes=64) for s in range(PASSES)]
-        a_sb = [keep.tile([P, H // P, C], F32, name=f"a_sb{e}", align_bytes=64) for e in range(E)]
-        w2_w = [keep.tile([P, PASSES, 2 * H], U8, name=f"w2_w{e}", align_bytes=64) for e in range(E)]
-        w1_w = keep.tile([P, E, 2 * K], U8, name="w1_w", align_bytes=64)
-        wp_w = keep.tile([P, E, 4 * K], U8, name="wp_w", align_bytes=64)
+        a_cuts = ((0, 1), (1, 2), (2, 4))
+        w2_cuts = ((0, 1), (1, 4))
+        a_sb, w2_w = {}, {}
+        w1_w, wp_w = {}, {}
 
-        def load_a(e):
-            nc.sync.dma_start(out=a_sb[e][:], in_=a[:, e * C : (e + 1) * C].rearrange("(c p) j -> p c j", p=P))
+        def load_w1(lo, hi):
+            part = keep.tile([P, hi - lo, 2 * K], U8, name=f"w1_w{lo}", align_bytes=64)
+            nc.sync.dma_start(out=part[:].bitcast(I32), in_=w1t_words[lo:hi].bitcast(I32).rearrange("e s p w -> p (e s) w"))
+            for e in range(lo, hi):
+                w1_w[e] = part[:, e - lo, :]
 
-        def load_w2(e):
-            nc.sync.dma_start(out=w2_w[e][:].bitcast(I32), in_=w2t_words[e].bitcast(I32).rearrange("s p w -> p s w"))
+        def load_wp(lo, hi):
+            part = keep.tile([P, hi - lo, 4 * K], U8, name=f"wp_w{lo}", align_bytes=64)
+            nc.sync.dma_start(
+                out=part[:].bitcast(I32), in_=wpt_words.rearrange("e s p k d -> p (e s) (k d)").bitcast(I32)[:, lo:hi, :]
+            )
+            for e in range(lo, hi):
+                wp_w[e] = part[:, e - lo, :]
 
+        def load_a(lo, hi):
+            part = keep.tile([P, H // P, (hi - lo) * C], F32, name=f"a_sb{lo}", align_bytes=64)
+            nc.sync.dma_start(out=part[:], in_=a[:, lo * C : hi * C].rearrange("(c p) j -> p c j", p=P))
+            for e in range(lo, hi):
+                a_sb[e] = part[:, :, (e - lo) * C : (e - lo + 1) * C]
+
+        def load_w2(lo, hi):
+            part = keep.tile([P, (hi - lo) * PASSES, 2 * H], U8, name=f"w2_w{lo}", align_bytes=64)
+            nc.sync.dma_start(
+                out=part[:].bitcast(I32), in_=w2t_words[lo:hi].bitcast(I32).rearrange("e s p w -> p (e s) w")
+            )
+            for e in range(lo, hi):
+                w2_w[e] = part[:, (e - lo) * PASSES : (e - lo + 1) * PASSES, :]
+
+        if OPT["a0"] == 0:
+            load_a(*a_cuts[0])
         nc.sync.dma_start(token_list[:], offs)
         for q in range(4):
             nc.sync.dma_start(
                 out=dy_sc[32 * q : 32 * q + 4 * PASSES, :].bitcast(I32),
                 in_=dy_scales[:, 4 * q : 4 * q + 4, :].bitcast(I32),
             )
+        if OPT["a0"] == 1:
+            load_a(*a_cuts[0])
         for s in range(PASSES):
             nc.sync.dma_start(out=dy_w[s][:], in_=dy_words[s].rearrange("p n t -> p (n t)").bitcast(I32))
-        load_a(0)
-        load_a(1)
-        load_scale_rows(nc.sync, w2_sc, w2t_scales.rearrange("e s b w -> (e s) b w"))
-        load_w2(0)
-        nc.sync.dma_start(out=gate_rows[0:TILES, :], in_=gate[0:1, :].rearrange("o (s c) -> (o s) c", c=P))
-        load_w2(1)
-        load_a(2)
-        load_a(3)
-        nc.sync.dma_start(out=w1_w[:].bitcast(I32), in_=w1t_words.bitcast(I32).rearrange("e s p w -> p (e s) w"))
-        nc.sync.dma_start(
-            out=wp_w[:].bitcast(I32), in_=wpt_words.rearrange("e s p k d -> p (e s) (k d)").bitcast(I32)
-        )
-        nc.sync.dma_start(partner_list[:], offs2)
-        load_w2(2)
-        load_w2(3)
-        load_scale_rows(nc.gpsimd, w1_sc, w1t_scales.rearrange("e s b w -> (e s) b w"))
-        load_scale_rows(nc.gpsimd, wp_sc, wpt_scales.rearrange("e s b w -> (e s) b w"))
-
-        g_w = [[keep.tile([P, HALF], U32, name=f"g_w{h}{s}", align_bytes=64) for s in range(PASSES)] for h in range(2)]
         for h in range(2):
             entries = token_list[:, h * HALF // GROUP : (h + 1) * HALF // GROUP]
             nc.vector.tensor_copy(g_sc[0][:, h * HALF : (h + 1) * HALF], dy_sc[:].indirect(entries))
-        for q in range(4):
-            nc.scalar.dma_start(
-                out=g_sc[1][32 * q : 32 * q + 4, :].bitcast(I32),
-                in_=g_sc[0][32 * q + 4 : 32 * q + 8, :].bitcast(I32),
-            )
-        for h in range(2):
-            entries = token_list[:, h * HALF // GROUP : (h + 1) * HALF // GROUP]
-            for s in range(PASSES):
-                nc.vector.tensor_copy(g_w[h][s][:], dy_w[s][:].bitcast(U32).indirect(entries))
+        steps = {
+            "w2s": lambda: load_scale_rows(nc.sync, w2_sc, w2t_scales.rearrange("e s b w -> (e s) b w")),
+            "w20": lambda: load_w2(*w2_cuts[0]),
+            "gate": lambda: nc.sync.dma_start(out=gate_rows[0:TILES, :], in_=gate[0:1, :].rearrange("o (s c) -> (o s) c", c=P)),
+            "move": lambda: nc.sync.dma_start(out=g_sc[1][0:112, :].bitcast(I32), in_=g_sc[0][4:116, :].bitcast(I32)),
+            "a1": lambda: load_a(*a_cuts[1]),
+            "w1s": lambda: load_scale_rows(nc.gpsimd if OPT["gq"] > 1 else nc.sync, w1_sc, w1t_scales.rearrange("e s b w -> (e s) b w")),
+            "wps": lambda: load_scale_rows(nc.gpsimd if OPT["gq"] > 0 else nc.sync, wp_sc, wpt_scales.rearrange("e s b w -> (e s) b w")),
+            "w1": lambda: load_w1(0, E),
+            "wp": lambda: load_wp(0, E),
+            "w10": lambda: load_w1(0, 1),
+            "wp0": lambda: load_wp(0, 1),
+            "w1r": lambda: load_w1(1, E),
+            "wpr": lambda: load_wp(1, E),
+            "a2": lambda: load_a(2, 3),
+            "a3": lambda: load_a(3, 4),
+            "w23": lambda: load_w2(3, 4),
+            "w212": lambda: load_w2(1, 3),
+            "o2": lambda: nc.sync.dma_start(partner_list[:], offs2),
+            "a23": lambda: load_a(*a_cuts[2]),
+            "w2r": lambda: load_w2(*w2_cuts[1]),
+        }
+        for step in OPT["loads"].split():
+            steps[step]()
 
-        gate_ps = psum.tile([P, P], F32, name="gate_ps", tag="turn")
-        nc.tensor.transpose(gate_ps[:], gate_rows[:], ident[:])
-        neg_gate = keep.tile([P, TILES], F32, name="neg_gate")
-        nc.vector.tensor_scalar(neg_gate[:], gate_ps[:, 0:TILES], -1.0, None, ALU.mult)
+        g_w = {}
+
+        def gather_words(lo, hi, s, tag=None):
+            part = keep.tile([P, (hi - lo) * P], U32, name=f"g_w{lo}{s}", tag=tag or f"g_w{lo}{s}", align_bytes=64)
+            entries = token_list[:, lo * P // GROUP : hi * P // GROUP]
+            nc.vector.tensor_copy(part[:], dy_w[s][:].bitcast(U32).indirect(entries))
+            for t in range(lo, hi):
+                g_w[t, s] = part[:, (t - lo) * P : (t - lo + 1) * P]
 
         sig = [keep.tile([P, TPE * H], F32, name=f"sig{e}") for e in range(E)]
         rest = [keep.tile([P, TPE * H], F32, name=f"rest{e}") for e in range(E)]
 
-        def activate(e, dest, func, scale):
-            for u in range(TPE):
-                a_ps = psum.tile([P, H], F32, name="a_ps", tag="a_ps")
+        def turn_a(e, halves):
+            banks = {}
+            for u in halves:
+                a_ps = psum.tile([P, H], F32, name="a_ps", tag="a_ps", bufs=3)
                 for c in range(H // P):
                     nc.tensor.transpose(a_ps[:, c * P : (c + 1) * P], a_sb[e][:, c, u * P : (u + 1) * P], ident[:])
-                nc.scalar.activation(dest[e][:, u * H : (u + 1) * H], a_ps[:], func, scale=scale)
+                banks[u] = a_ps
+            return banks
 
-        for e in (0, 1):
-            activate(e, sig, ACT.Sigmoid, 1.0)
-        for e in range(E):
-            activate(e, rest, ACT.Silu, -1.0)
-        for e in (2, 3):
-            activate(e, sig, ACT.Sigmoid, 1.0)
+        def activate(e, banks, dest, func, scale):
+            for u in banks:
+                nc.scalar.activation(dest[e][:, u * H : (u + 1) * H], banks[u][:], func, scale=scale)
 
-        stage = [keep.tile([P, 2, SLOTS], F32, name=f"stage{kt}") for kt in range(KT)]
+        if OPT["warm"]:
+            warm = psum.tile([P, H], F32, name="warm", tag="sums")
+            for c in range(OPT["warm"]):
+                nc.tensor.transpose(warm[:, (c % 4) * P : (c % 4 + 1) * P], ident[:], ident[:])
+        banks = turn_a(0, (0, 1))
+        activate(0, banks, sig, ACT.Sigmoid, 1.0)
+        for lo, hi, s in OPT["g_early"]:
+            gather_words(lo, hi, s)
+        activate(0, banks, rest, ACT.Silu, -1.0)
+        gate_ps = psum.tile([P, P], F32, name="gate_ps", tag="turn", bufs=1)
+        nc.tensor.transpose(gate_ps[:], gate_rows[:], ident[:])
+        neg_gate = keep.tile([P, TILES], F32, name="neg_gate")
+        nc.vector.tensor_scalar(neg_gate[:], gate_ps[:, 0:TILES], -1.0, None, ALU.mult)
+
+        stage = {}
         window = [[keep.tile([P, T], F32, name=f"window{kt}{w}") for w in range(2)] for kt in range(KT)]
-        dh_rows = {}
-        dq = {}
+        dh_rows, neg_ds, dq = {}, {}, {}
 
-        def make_dh(e):
-            neg_d = keep.tile([P, TPE * H], F32, name=f"neg_d{e}")
-            nc.vector.scalar_tensor_tensor(neg_d[:], rest[e][:], 1.0, sig[e][:], ALU.subtract, ALU.mult)
-            turned = psum.tile([P, TPE, 2, P], F32, name="turned", tag="turn")
-            for u in range(TPE):
-                t = e * TPE + u
-                h, c0 = divmod(t * P, HALF)
-                sums = psum.tile([P, H], F32, name="sums", tag="sums")
+        def make_factor(e):
+            neg_ds[e] = keep.tile([P, TPE * H], F32, name=f"neg_d{e}", tag=f"neg_d{e}", align_bytes=64)
+            if e in OPT["pool"]:
+                for u in range(TPE):
+                    cols = slice(u * H, (u + 1) * H)
+                    nc.scalar.activation(rest[e][:, cols], rest[e][:, cols], ACT.Copy, bias=-1.0)
+                    nc.gpsimd.tensor_tensor(neg_ds[e][:, cols], rest[e][:, cols], sig[e][:, cols], ALU.mult)
+            elif e not in OPT["split"]:
+                nc.vector.scalar_tensor_tensor(neg_ds[e][:], rest[e][:], 1.0, sig[e][:], ALU.subtract, ALU.mult)
+
+        def make_dh(lo, hi):
+            e = lo // TPE
+            neg_d = neg_ds[e]
+            turned = psum.tile([P, hi - lo, 2, P], F32, name="turned", tag="turn", bufs=1)
+            for t in range(lo, hi):
+                cols = slice((t % TPE) * H, (t % TPE + 1) * H)
+                if t in OPT["sa"]:
+                    sums = psum.tile([P, H], F32, name="sums", tag="a_ps", bufs=3)
+                else:
+                    sums = psum.tile([P, H], F32, name="sums", tag="sums")
                 for s in range(PASSES):
                     m = e * PASSES + s
                     nc.tensor.matmul_mx(
                         out=sums[:],
-                        lhsT=g_w[h][s][:, c0 : c0 + P].bitcast(FP8X4),
+                        lhsT=g_w[t, s].bitcast(FP8X4),
                         lhsT_scale=g_sc[s][:, t * P : (t + 1) * P],
                         rhs=w2_w[e][:, s, :].bitcast(FP4X4),
                         rhs_scale=w2_sc[:, m * H : (m + 1) * H],
                         start=(s == 0),
                         stop=(s == PASSES - 1),
                     )
-                dh_t = keep.tile([P, H], BF16, name=f"dh_t{t}", align_bytes=64)
-                nc.vector.scalar_tensor_tensor(
-                    dh_t[:], sums[:], neg_gate[:, t : t + 1], neg_d[:, u * H : (u + 1) * H], ALU.mult, ALU.mult
-                )
+                if e in OPT["split"]:
+                    nc.vector.scalar_tensor_tensor(neg_d[:, cols], rest[e][:, cols], 1.0, sig[e][:, cols], ALU.subtract, ALU.mult)
+                dh_t = keep.tile([P, H], BF16, name=f"dh_t{t}", tag=f"dh_t{t}", align_bytes=64)
+                nc.vector.scalar_tensor_tensor(dh_t[:], sums[:], neg_gate[:, t : t + 1], neg_d[:, cols], ALU.mult, ALU.mult)
                 pairs = dh_t[:].bitcast(F32)
                 for v in range(2):
-                    nc.tensor.transpose(turned[:, u, v, :], pairs[:, v : H // 2 : 2], ident[:])
-            dh_rows[e] = keep.tile([P, C * 4], BF16, name=f"dh_rows{e}", align_bytes=64)
+                    nc.tensor.transpose(turned[:, t - lo, v, :], pairs[:, v : H // 2 : 2], ident[:])
+            dh_rows[lo] = keep.tile([P, (hi - lo) * H], BF16, name=f"dh_rows{lo}", tag=f"dh_rows{lo}", align_bytes=64)
             nc.scalar.copy(
-                dh_rows[e][:].bitcast(F32).rearrange("p (u j v) -> p u j v", u=TPE, v=2),
+                dh_rows[lo][:].bitcast(F32).rearrange("p (u j v) -> p u j v", u=hi - lo, v=2),
                 turned[:].rearrange("p u v j -> p u j v"),
             )
 
-        def multiply(e):
-            codes = keep.tile([P, C], U32, name=f"dq_w{e}", align_bytes=64)
-            scales = keep.tile([P, C], U8, name=f"dq_sc{e}", align_bytes=64)
-            nc.vector.quantize_mx(out=codes[:].bitcast(FP8X4), scales=scales[:], in_=dh_rows[e][:])
-            for kt in range(KT):
-                both = psum.tile([P, 2, C], F32, name="both", tag="both")
+        def quantise(lo, hi):
+            codes = keep.tile([P, (hi - lo) * P], U32, name=f"dq_w{lo}", align_bytes=64)
+            scales = keep.tile([P, (hi - lo) * P], U8, name=f"dq_sc{lo}", align_bytes=64)
+            nc.vector.quantize_mx(out=codes[:].bitcast(FP8X4), scales=scales[:], in_=dh_rows[lo][:])
+            dq[lo] = (codes, scales)
+
+        def multiply(lo, hi, kts=(0, 1), tag=None):
+            e = lo // TPE
+            codes, scales = dq[lo]
+            for kt in kts:
+                both = psum.tile([P, 2, (hi - lo) * P], F32, name="both", tag="both")
                 cols = slice(e * K + kt * P, e * K + (kt + 1) * P)
                 nc.tensor.matmul_mx(
                     out=both[:, 0, :],
-                    lhsT=w1_w[:, e, 2 * kt * P : 2 * (kt + 1) * P].bitcast(FP4X4),
+                    lhsT=w1_w[e][:, 2 * kt * P : 2 * (kt + 1) * P].bitcast(FP4X4),
                     lhsT_scale=w1_sc[:, cols],
                     rhs=codes[:].bitcast(FP8X4),
                     rhs_scale=scales[:],
@@ -190,38 +246,62 @@ def tile_moe_dub_silu_kernel(
                 )
                 nc.tensor.matmul_mx(
                     out=both[:, 1, :],
-                    lhsT=wp_w[:, e, 4 * kt * P : 4 * (kt + 1) * P].bitcast(FP8X4),
+                    lhsT=wp_w[e][:, 4 * kt * P : 4 * (kt + 1) * P].bitcast(FP8X4),
                     lhsT_scale=wp_sc[:, cols],
                     rhs=codes[:].bitcast(FP8X4),
                     rhs_scale=scales[:],
                     start=True,
                     stop=True,
                 )
-                nc.scalar.copy(stage[kt][:, :, e * C : (e + 1) * C], both[:])
+                stage[lo, kt] = keep.tile([P, 2, (hi - lo) * P], F32, name=f"stage{lo}{kt}", tag=tag or f"stage{lo}{kt}", align_bytes=64)
+                nc.scalar.copy(stage[lo, kt][:], both[:])
 
-        def scatter(e, kt, w):
-            entries = (token_list, partner_list)[w][:, e * C // GROUP : (e + 1) * C // GROUP]
-            nc.vector.tensor_copy(window[kt][w][:].indirect(entries), stage[kt][:, w, e * C : (e + 1) * C])
+        def scatter(lo, hi, kt, w):
+            entries = (token_list, partner_list)[w][:, lo * P // GROUP : hi * P // GROUP]
+            nc.vector.tensor_copy(window[kt][w][:].indirect(entries), stage[lo, kt][:, w, :])
 
         def finish(kt, lo, hi):
             total = keep.tile([P, hi - lo], F32, name=f"total{kt}_{lo}")
             nc.vector.tensor_tensor(total[:], window[kt][0][:, lo:hi], window[kt][1][:, lo:hi], ALU.add)
             nc.sync.dma_start(out=out[kt * P : (kt + 1) * P, lo:hi], in_=total[:])
 
-        make_dh(0)
-        make_dh(1)
-        multiply(0)
-        make_dh(2)
-        multiply(1)
-        for e in range(E):
-            if e + 3 < E:
-                make_dh(e + 3)
+        make_factor(0)
+        for lo, hi in OPT["first"]:
+            make_dh(lo, hi)
+            quantise(lo, hi)
+            multiply(lo, hi)
+        for lo, hi, s, tag in OPT["g_late"]:
+            gather_words(lo, hi, s, tag)
+        for e in (1, 2, 3):
+            banks = turn_a(e, (0, 1))
+            activate(e, banks, rest, ACT.Silu, -1.0)
+        activate(3, {1: banks[1]}, sig, ACT.Sigmoid, 1.0)
+        activate(3, turn_a(3, (0,)), sig, ACT.Sigmoid, 1.0)
+        make_factor(3)
+        for e in (2, 1):
+            activate(e, turn_a(e, (0, 1)), sig, ACT.Sigmoid, 1.0)
+            make_factor(e)
+        for lo, hi in OPT["first"]:
             for kt in range(KT):
                 for w in range(2):
-                    scatter(e, kt, w)
-                    if e == E - 1 and (kt, w) == (1, 0):
-                        finish(0, 0, T)
-            if e + 2 < E:
-                multiply(e + 2)
+                    scatter(lo, hi, kt, w)
+        make_dh(6, 8)
+        quantise(6, 8)
+        multiply(6, 8, (0,))
+        make_dh(4, 6)
+        quantise(4, 6)
+        make_dh(2, 4)
+        quantise(2, 4)
+        multiply(6, 8, (1,), OPT["t31"])
+        multiply(4, 6)
+        multiply(2, 4)
+        for lo, kt in ((6, 0), (6, 1), (4, 0), (4, 1)):
+            for w in range(2):
+                scatter(lo, lo + 2, kt, w)
+        scatter(2, 4, 0, 0)
+        scatter(2, 4, 0, 1)
+        scatter(2, 4, 1, 0)
+        finish(0, 0, T)
+        scatter(2, 4, 1, 1)
         finish(1, 0, T // 2)
         finish(1, T // 2, T)

@@ -25,7 +25,7 @@ HALF = SLOTS // 2
 TILES = SLOTS // P
 TPE = C // P
 KT = K // P
-OPT = {'sa': (4, 5, 2), 'a0': 1, 'gq': 0, 'loads': 'w2s w20 gate move a1 w10 wp0 w1s wps o2 a23 w2r w1r wpr', 'warm': 0, 'split': (0, 3), 'pool': (), 't31': 'dh_t3', 'first': ((0, 1), (1, 2)), 'g_early': ((0, 4, 0), (0, 4, 1), (4, 8, 0)), 'g_late': ((4, 8, 1, 'dh_t0'),)}
+OPT = dict(zt=dict(), mode='vvph', sa=(4,), sb=(), split=(0, 1), a0=1, gq=0, padd=1, warm=0, g_early=((0, 4, 0), (0, 4, 1), (4, 8, 0)), loads='gate w2s w20 a1 move w1s wp0 wps w10 o2 a3 w21 a2 w1r w2x wpr', prog='F0 D01 D12 Q01 L1 Q12 M011 G481:dh_rows0 U01101 M010 S2 S1h:dq_w0 F1 M120 U12001 D24 M121 U12101:dh_t3 P4 L2b F2 Q24 M241 U2411 M240 U2410:dq_w2 U24001:dh_t1 X01101 D46 Q46 L3 S3b F3:dh_rows4 M461 U01001 D68 U4610 U4611:dh_t7 M460 X12101 U46001 Q68 M680 X24101 U68001 X12001 M681 U68101 X46101 X01001 X24001 X46001 X68001 E0 X68101 E1')
 
 
 def load_scale_rows(queue, plane, rows):
@@ -129,6 +129,8 @@ def tile_moe_dub_silu_kernel(
             "a3": lambda: load_a(3, 4),
             "w23": lambda: load_w2(3, 4),
             "w212": lambda: load_w2(1, 3),
+            "w21": lambda: load_w2(1, 2),
+            "w2x": lambda: load_w2(2, 4),
             "o2": lambda: nc.sync.dma_start(partner_list[:], offs2),
             "a23": lambda: load_a(*a_cuts[2]),
             "w2r": lambda: load_w2(*w2_cuts[1]),
@@ -145,8 +147,7 @@ def tile_moe_dub_silu_kernel(
             for t in range(lo, hi):
                 g_w[t, s] = part[:, (t - lo) * P : (t - lo + 1) * P]
 
-        sig = [keep.tile([P, TPE * H], F32, name=f"sig{e}") for e in range(E)]
-        rest = [keep.tile([P, TPE * H], F32, name=f"rest{e}") for e in range(E)]
+        sig, rest = {}, {}
 
         def turn_a(e, halves):
             banks = {}
@@ -157,7 +158,10 @@ def tile_moe_dub_silu_kernel(
                 banks[u] = a_ps
             return banks
 
-        def activate(e, banks, dest, func, scale):
+        def activate(e, banks, dest, func, scale, tag=None):
+            name = f"sig{e}" if dest is sig else f"rest{e}"
+            if e not in dest:
+                dest[e] = keep.tile([P, TPE * H], F32, name=name, tag=tag or name, align_bytes=64)
             for u in banks:
                 nc.scalar.activation(dest[e][:, u * H : (u + 1) * H], banks[u][:], func, scale=scale)
 
@@ -179,26 +183,26 @@ def tile_moe_dub_silu_kernel(
         window = [[keep.tile([P, T], F32, name=f"window{kt}{w}") for w in range(2)] for kt in range(KT)]
         dh_rows, neg_ds, dq = {}, {}, {}
 
-        def make_factor(e):
-            neg_ds[e] = keep.tile([P, TPE * H], F32, name=f"neg_d{e}", tag=f"neg_d{e}", align_bytes=64)
-            if e in OPT["pool"]:
-                for u in range(TPE):
-                    cols = slice(u * H, (u + 1) * H)
-                    nc.scalar.activation(rest[e][:, cols], rest[e][:, cols], ACT.Copy, bias=-1.0)
-                    nc.gpsimd.tensor_tensor(neg_ds[e][:, cols], rest[e][:, cols], sig[e][:, cols], ALU.mult)
+        def make_factor(e, tag=None):
+            assert e in sig and e in rest
+            neg_ds[e] = keep.tile([P, TPE * H], F32, name=f"neg_d{e}", tag=tag or f"neg_d{e}", align_bytes=64)
+            if OPT["mode"][e] == "p":
+                nc.scalar.activation(neg_ds[e][:], rest[e][:], ACT.Copy, bias=-1.0)
             elif e not in OPT["split"]:
                 nc.vector.scalar_tensor_tensor(neg_ds[e][:], rest[e][:], 1.0, sig[e][:], ALU.subtract, ALU.mult)
 
-        def make_dh(lo, hi):
-            e = lo // TPE
-            neg_d = neg_ds[e]
-            turned = psum.tile([P, hi - lo, 2, P], F32, name="turned", tag="turn", bufs=1)
-            for t in range(lo, hi):
-                cols = slice((t % TPE) * H, (t % TPE + 1) * H)
+        first_sums = {}
+
+        def first_product(t):
+            e = t // TPE
+            if True:
                 if t in OPT["sa"]:
                     sums = psum.tile([P, H], F32, name="sums", tag="a_ps", bufs=3)
+                elif t in OPT["sb"]:
+                    sums = psum.tile([P, H], F32, name="sums", tag="both")
                 else:
                     sums = psum.tile([P, H], F32, name="sums", tag="sums")
+                first_sums[t] = sums
                 for s in range(PASSES):
                     m = e * PASSES + s
                     nc.tensor.matmul_mx(
@@ -210,10 +214,38 @@ def tile_moe_dub_silu_kernel(
                         start=(s == 0),
                         stop=(s == PASSES - 1),
                     )
+
+        gateds = {}
+
+        def gate_sums(t, tag=None):
+            if t not in first_sums:
+                first_product(t)
+            gateds[t] = keep.tile([P, H], F32, name=f"gated{t}", tag=tag or f"gated{t}", align_bytes=64)
+            nc.scalar.activation(gateds[t][:], first_sums[t][:], ACT.Copy, scale=neg_gate[:, t : t + 1])
+
+        def make_dh(lo, hi, tag=None):
+            e = lo // TPE
+            neg_d = neg_ds[e]
+            turned = psum.tile([P, hi - lo, 2, P], F32, name="turned", tag="turn", bufs=1)
+            for t in range(lo, hi):
+                cols = slice((t % TPE) * H, (t % TPE + 1) * H)
+                if t not in first_sums:
+                    first_product(t)
+                sums = first_sums[t]
                 if e in OPT["split"]:
                     nc.vector.scalar_tensor_tensor(neg_d[:, cols], rest[e][:, cols], 1.0, sig[e][:, cols], ALU.subtract, ALU.mult)
-                dh_t = keep.tile([P, H], BF16, name=f"dh_t{t}", tag=f"dh_t{t}", align_bytes=64)
-                nc.vector.scalar_tensor_tensor(dh_t[:], sums[:], neg_gate[:, t : t + 1], neg_d[:, cols], ALU.mult, ALU.mult)
+                dh_t = keep.tile([P, H], BF16, name=f"dh_t{t}", tag=(tag if t == lo and tag and OPT["mode"][e] != "p" else OPT["zt"].get(t, f"dh_t{t}")), align_bytes=64)
+                if OPT["mode"][e] != "v":
+                    if t not in gateds:
+                        gate_sums(t)
+                    gated = gateds[t]
+                    if OPT["mode"][e] == "p":
+                        half = keep.tile([P, H], F32, name=f"half{t}", tag=(tag if t == lo and tag else f"half{t}"), align_bytes=64)
+                        nc.gpsimd.tensor_tensor(half[:], gated[:], sig[e][:, cols], ALU.mult)
+                        gated = half
+                    nc.gpsimd.tensor_tensor(dh_t[:], gated[:], neg_d[:, cols], ALU.mult)
+                else:
+                    nc.vector.scalar_tensor_tensor(dh_t[:], sums[:], neg_gate[:, t : t + 1], neg_d[:, cols], ALU.mult, ALU.mult)
                 pairs = dh_t[:].bitcast(F32)
                 for v in range(2):
                     nc.tensor.transpose(turned[:, t - lo, v, :], pairs[:, v : H // 2 : 2], ident[:])
@@ -223,85 +255,89 @@ def tile_moe_dub_silu_kernel(
                 turned[:].rearrange("p u v j -> p u j v"),
             )
 
-        def quantise(lo, hi):
-            codes = keep.tile([P, (hi - lo) * P], U32, name=f"dq_w{lo}", align_bytes=64)
+        def quantise(lo, hi, tag=None):
+            codes = keep.tile([P, (hi - lo) * P], U32, name=f"dq_w{lo}", tag=tag or f"dq_w{lo}", align_bytes=64)
             scales = keep.tile([P, (hi - lo) * P], U8, name=f"dq_sc{lo}", align_bytes=64)
             nc.vector.quantize_mx(out=codes[:].bitcast(FP8X4), scales=scales[:], in_=dh_rows[lo][:])
             dq[lo] = (codes, scales)
 
-        def multiply(lo, hi, kts=(0, 1), tag=None):
+        banks2 = {}
+
+        def multiply(lo, hi, kt):
             e = lo // TPE
             codes, scales = dq[lo]
-            for kt in kts:
-                both = psum.tile([P, 2, (hi - lo) * P], F32, name="both", tag="both")
-                cols = slice(e * K + kt * P, e * K + (kt + 1) * P)
-                nc.tensor.matmul_mx(
-                    out=both[:, 0, :],
-                    lhsT=w1_w[e][:, 2 * kt * P : 2 * (kt + 1) * P].bitcast(FP4X4),
-                    lhsT_scale=w1_sc[:, cols],
-                    rhs=codes[:].bitcast(FP8X4),
-                    rhs_scale=scales[:],
-                    start=True,
-                    stop=True,
-                )
-                nc.tensor.matmul_mx(
-                    out=both[:, 1, :],
-                    lhsT=wp_w[e][:, 4 * kt * P : 4 * (kt + 1) * P].bitcast(FP8X4),
-                    lhsT_scale=wp_sc[:, cols],
-                    rhs=codes[:].bitcast(FP8X4),
-                    rhs_scale=scales[:],
-                    start=True,
-                    stop=True,
-                )
-                stage[lo, kt] = keep.tile([P, 2, (hi - lo) * P], F32, name=f"stage{lo}{kt}", tag=tag or f"stage{lo}{kt}", align_bytes=64)
-                nc.scalar.copy(stage[lo, kt][:], both[:])
+            both = psum.tile([P, 2, (hi - lo) * P], F32, name="both", tag="both")
+            cols = slice(e * K + kt * P, e * K + (kt + 1) * P)
+            nc.tensor.matmul_mx(
+                out=both[:, 0, :],
+                lhsT=w1_w[e][:, 2 * kt * P : 2 * (kt + 1) * P].bitcast(FP4X4),
+                lhsT_scale=w1_sc[:, cols],
+                rhs=codes[:].bitcast(FP8X4),
+                rhs_scale=scales[:],
+                start=True,
+                stop=True,
+            )
+            nc.tensor.matmul_mx(
+                out=both[:, 1, :],
+                lhsT=wp_w[e][:, 4 * kt * P : 4 * (kt + 1) * P].bitcast(FP8X4),
+                lhsT_scale=wp_sc[:, cols],
+                rhs=codes[:].bitcast(FP8X4),
+                rhs_scale=scales[:],
+                start=True,
+                stop=True,
+            )
+            banks2[lo, kt] = both
+
+        def unload(lo, hi, kt, ws, tag=None):
+            part = keep.tile([P, len(ws), (hi - lo) * P], F32, name=f"stage{lo}{kt}{ws[0]}", tag=tag or f"stage{lo}{kt}{ws[0]}", align_bytes=64)
+            nc.scalar.copy(part[:], banks2[lo, kt][:, ws[0] : ws[-1] + 1, :])
+            for w in ws:
+                stage[lo, kt, w] = part[:, w - ws[0], :]
 
         def scatter(lo, hi, kt, w):
             entries = (token_list, partner_list)[w][:, lo * P // GROUP : hi * P // GROUP]
-            nc.vector.tensor_copy(window[kt][w][:].indirect(entries), stage[lo, kt][:, w, :])
+            nc.vector.tensor_copy(window[kt][w][:].indirect(entries), stage[lo, kt, w])
 
         def finish(kt, lo, hi):
             total = keep.tile([P, hi - lo], F32, name=f"total{kt}_{lo}")
-            nc.vector.tensor_tensor(total[:], window[kt][0][:, lo:hi], window[kt][1][:, lo:hi], ALU.add)
-            nc.sync.dma_start(out=out[kt * P : (kt + 1) * P, lo:hi], in_=total[:])
+            (nc.gpsimd if kt == 0 and OPT["padd"] else nc.vector).tensor_tensor(total[:], window[kt][0][:, lo:hi], window[kt][1][:, lo:hi], ALU.add)
+            (nc.scalar if kt == 0 else nc.sync).dma_start(out=out[kt * P : (kt + 1) * P, lo:hi], in_=total[:])
 
-        make_factor(0)
-        for lo, hi in OPT["first"]:
-            make_dh(lo, hi)
-            quantise(lo, hi)
-            multiply(lo, hi)
-        for lo, hi, s, tag in OPT["g_late"]:
-            gather_words(lo, hi, s, tag)
-        for e in (1, 2, 3):
-            banks = turn_a(e, (0, 1))
-            activate(e, banks, rest, ACT.Silu, -1.0)
-        activate(3, {1: banks[1]}, sig, ACT.Sigmoid, 1.0)
-        activate(3, turn_a(3, (0,)), sig, ACT.Sigmoid, 1.0)
-        make_factor(3)
-        for e in (2, 1):
-            activate(e, turn_a(e, (0, 1)), sig, ACT.Sigmoid, 1.0)
-            make_factor(e)
-        for lo, hi in OPT["first"]:
-            for kt in range(KT):
-                for w in range(2):
-                    scatter(lo, hi, kt, w)
-        make_dh(6, 8)
-        quantise(6, 8)
-        multiply(6, 8, (0,))
-        make_dh(4, 6)
-        quantise(4, 6)
-        make_dh(2, 4)
-        quantise(2, 4)
-        multiply(6, 8, (1,), OPT["t31"])
-        multiply(4, 6)
-        multiply(2, 4)
-        for lo, kt in ((6, 0), (6, 1), (4, 0), (4, 1)):
-            for w in range(2):
-                scatter(lo, lo + 2, kt, w)
-        scatter(2, 4, 0, 0)
-        scatter(2, 4, 0, 1)
-        scatter(2, 4, 1, 0)
-        finish(0, 0, T)
-        scatter(2, 4, 1, 1)
-        finish(1, 0, T // 2)
-        finish(1, T // 2, T)
+        held = {}
+        FUNC = {"S": (sig, ACT.Sigmoid, 1.0), "L": (rest, ACT.Silu, -1.0)}
+        for step in OPT["prog"].split():
+            op, arg, tag = step[0], step[1:].split(":")[0], (step.split(":") + [None])[1]
+            if op in "SL":
+                e = int(arg[0])
+                if arg[1:] == "h":
+                    activate(e, held[e], *FUNC[op], tag)
+                elif arg[1:] == "b":
+                    activate(e, {1: held[e][1]}, *FUNC[op], tag)
+                    activate(e, turn_a(e, (0,)), *FUNC[op], tag)
+                else:
+                    held[e] = turn_a(e, (0, 1))
+                    activate(e, held[e], *FUNC[op], tag)
+            elif op == "G":
+                gather_words(int(arg[0]), int(arg[1]), int(arg[2]), tag)
+            elif op == "F":
+                make_factor(int(arg), tag)
+            elif op == "P":
+                assert int(arg) not in first_sums
+                first_product(int(arg))
+            elif op == "H":
+                assert int(arg) not in gateds and OPT["mode"][int(arg) // TPE] != "v"
+                gate_sums(int(arg), tag)
+            elif op == "D":
+                make_dh(int(arg[0]), int(arg[1]), tag)
+            elif op == "Q":
+                quantise(int(arg[0]), int(arg[1]), tag)
+            elif op == "M":
+                multiply(int(arg[0]), int(arg[1]), int(arg[2]))
+            elif op == "U":
+                unload(int(arg[0]), int(arg[1]), int(arg[2]), [int(w) for w in arg[3:]], tag)
+            elif op == "X":
+                for w in arg[3:]:
+                    scatter(int(arg[0]), int(arg[1]), int(arg[2]), int(w))
+            elif op == "E":
+                finish(int(arg), 0, T // 2)
+                finish(int(arg), T // 2, T)

@@ -20,18 +20,19 @@ ALU = mybir.AluOpType
 P = 128
 PASSES = N // 512
 SLOTS = E * C
-GROUP = 16
-HALF = SLOTS // 2
-TILES = SLOTS // P
-TPE = C // P
-KT = K // P
-OPT = dict(zt=dict(), mode='vvph', sa=(4,), sb=(), split=(0, 1), a0=1, gq=0, padd=1, warm=0, g_early=((0, 4, 0), (0, 4, 1), (4, 8, 0)), loads='gate w2s w20 a1 move w1s wp0 wps w10 o2 a3 w21 a2 w1r w2x wpr', prog='F0 D01 D12 Q01 L1 Q12 M011 G481:dh_rows0 U01101 M010 S2 S1h:dq_w0 F1 M120 U12001 D24 M121 U12101:dh_t3 P4 L2b F2 Q24 M241 U2411 M240 U2410:dq_w2 U24001:dh_t1 X01101 D46 Q46 L3 S3b F3:dh_rows4 M461 U01001 D68 U4610 U4611:dh_t7 M460 X12101 U46001 Q68 M680 X24101 U68001 X12001 M681 U68101 X46101 X01001 X24001 X46001 X68001 E0 X68101 E1')
+GROUPS = SLOTS // P
+PER_EXPERT = C // P
+PER_COLUMN = 16
+QUADRANTS = 4
+MOVED_ROWS = 112
+DX, DP = 0, 1
+A_BANKS = 3
 
 
-def load_scale_rows(queue, plane, rows):
+def load_scale_rows(nc, plane, rows):
     m = rows.shape[0]
-    for q in range(4):
-        queue.dma_start(
+    for q in range(QUADRANTS):
+        nc.sync.dma_start(
             out=plane[32 * q : 32 * q + 4, :].bitcast(I32).rearrange("b (m w) -> b m w", m=m),
             in_=rows[:, 4 * q : 4 * q + 4, :].bitcast(I32).rearrange("m b w -> b m w"),
         )
@@ -46,15 +47,21 @@ def tile_moe_dub_silu_kernel(
         keep = ctx.enter_context(tc.tile_pool(name="keep", bufs=1))
         psum = ctx.enter_context(tc.psum_pool(name="psum", bufs=2))
 
-        token_list = lists.tile([P, SLOTS // GROUP], U16, name="token_list")
-        partner_list = lists.tile([P, SLOTS // GROUP], U16, name="partner_list")
+        def held(shape, dtype, name, after=None):
+            return keep.tile(shape, dtype, name=name, tag=after or name, align_bytes=64)
 
-        dy_sc = keep.tile([P, T], U8, name="dy_sc", align_bytes=64)
-        w2_sc = keep.tile([P, E * PASSES * H], U8, name="w2_sc", align_bytes=64)
-        w1_sc = keep.tile([P, E * K], U8, name="w1_sc", align_bytes=64)
-        wp_sc = keep.tile([P, E * K], U8, name="wp_sc", align_bytes=64)
-        g_sc = [keep.tile([P, SLOTS], U8, name=f"g_sc{s}", align_bytes=64) for s in range(PASSES)]
-        for plane in (dy_sc, w2_sc, g_sc[1], w1_sc, wp_sc):
+        token_list = lists.tile([P, SLOTS // PER_COLUMN], U16, name="token_list")
+        partner_list = lists.tile([P, SLOTS // PER_COLUMN], U16, name="partner_list")
+
+        def entries(which, lo, hi):
+            return (token_list, partner_list)[which][:, lo * P // PER_COLUMN : hi * P // PER_COLUMN]
+
+        dy_sc = held([P, T], U8, "dy_sc")
+        w2_sc = held([P, E * PASSES * H], U8, "w2_sc")
+        w1_sc = held([P, E * K], U8, "w1_sc")
+        wp_sc = held([P, E * K], U8, "wp_sc")
+        slot_sc = [held([P, SLOTS], U8, f"slot_sc{s}") for s in range(PASSES)]
+        for plane in (dy_sc, w2_sc, slot_sc[1], w1_sc, wp_sc):
             nc.vector.memset(plane[:].bitcast(I32), 0)
 
         ident = keep.tile([P, P], F32, name="ident")
@@ -62,215 +69,161 @@ def tile_moe_dub_silu_kernel(
         nc.gpsimd.memset(gate_rows[:], 0.0)
         make_identity(nc, ident[:])
 
-        dy_w = [keep.tile([P, T], I32, name=f"dy_w{s}", align_bytes=64) for s in range(PASSES)]
-        a_cuts = ((0, 1), (1, 2), (2, 4))
-        w2_cuts = ((0, 1), (1, 4))
+        dy_w = [held([P, T], I32, f"dy_w{s}") for s in range(PASSES)]
         a_sb, w2_w = {}, {}
-        w1_w, wp_w = {}, {}
-
-        def load_w1(lo, hi):
-            part = keep.tile([P, hi - lo, 2 * K], U8, name=f"w1_w{lo}", align_bytes=64)
-            nc.sync.dma_start(out=part[:].bitcast(I32), in_=w1t_words[lo:hi].bitcast(I32).rearrange("e s p w -> p (e s) w"))
-            for e in range(lo, hi):
-                w1_w[e] = part[:, e - lo, :]
-
-        def load_wp(lo, hi):
-            part = keep.tile([P, hi - lo, 4 * K], U8, name=f"wp_w{lo}", align_bytes=64)
-            nc.sync.dma_start(
-                out=part[:].bitcast(I32), in_=wpt_words.rearrange("e s p k d -> p (e s) (k d)").bitcast(I32)[:, lo:hi, :]
-            )
-            for e in range(lo, hi):
-                wp_w[e] = part[:, e - lo, :]
 
         def load_a(lo, hi):
-            part = keep.tile([P, H // P, (hi - lo) * C], F32, name=f"a_sb{lo}", align_bytes=64)
+            part = held([P, H // P, (hi - lo) * C], F32, f"a_sb{lo}")
             nc.sync.dma_start(out=part[:], in_=a[:, lo * C : hi * C].rearrange("(c p) j -> p c j", p=P))
             for e in range(lo, hi):
                 a_sb[e] = part[:, :, (e - lo) * C : (e - lo + 1) * C]
 
         def load_w2(lo, hi):
-            part = keep.tile([P, (hi - lo) * PASSES, 2 * H], U8, name=f"w2_w{lo}", align_bytes=64)
+            part = held([P, (hi - lo) * PASSES, 2 * H], U8, f"w2_w{lo}")
             nc.sync.dma_start(
                 out=part[:].bitcast(I32), in_=w2t_words[lo:hi].bitcast(I32).rearrange("e s p w -> p (e s) w")
             )
             for e in range(lo, hi):
                 w2_w[e] = part[:, (e - lo) * PASSES : (e - lo + 1) * PASSES, :]
 
-        if OPT["a0"] == 0:
-            load_a(*a_cuts[0])
         nc.sync.dma_start(token_list[:], offs)
-        for q in range(4):
+        for q in range(QUADRANTS):
             nc.sync.dma_start(
                 out=dy_sc[32 * q : 32 * q + 4 * PASSES, :].bitcast(I32),
                 in_=dy_scales[:, 4 * q : 4 * q + 4, :].bitcast(I32),
             )
-        if OPT["a0"] == 1:
-            load_a(*a_cuts[0])
+        load_a(0, 1)
         for s in range(PASSES):
             nc.sync.dma_start(out=dy_w[s][:], in_=dy_words[s].rearrange("p n t -> p (n t)").bitcast(I32))
-        for h in range(2):
-            entries = token_list[:, h * HALF // GROUP : (h + 1) * HALF // GROUP]
-            nc.vector.tensor_copy(g_sc[0][:, h * HALF : (h + 1) * HALF], dy_sc[:].indirect(entries))
-        steps = {
-            "w2s": lambda: load_scale_rows(nc.sync, w2_sc, w2t_scales.rearrange("e s b w -> (e s) b w")),
-            "w20": lambda: load_w2(*w2_cuts[0]),
-            "gate": lambda: nc.sync.dma_start(out=gate_rows[0:TILES, :], in_=gate[0:1, :].rearrange("o (s c) -> (o s) c", c=P)),
-            "move": lambda: nc.sync.dma_start(out=g_sc[1][0:112, :].bitcast(I32), in_=g_sc[0][4:116, :].bitcast(I32)),
-            "a1": lambda: load_a(*a_cuts[1]),
-            "w1s": lambda: load_scale_rows(nc.gpsimd if OPT["gq"] > 1 else nc.sync, w1_sc, w1t_scales.rearrange("e s b w -> (e s) b w")),
-            "wps": lambda: load_scale_rows(nc.gpsimd if OPT["gq"] > 0 else nc.sync, wp_sc, wpt_scales.rearrange("e s b w -> (e s) b w")),
-            "w1": lambda: load_w1(0, E),
-            "wp": lambda: load_wp(0, E),
-            "w10": lambda: load_w1(0, 1),
-            "wp0": lambda: load_wp(0, 1),
-            "w1r": lambda: load_w1(1, E),
-            "wpr": lambda: load_wp(1, E),
-            "a2": lambda: load_a(2, 3),
-            "a3": lambda: load_a(3, 4),
-            "w23": lambda: load_w2(3, 4),
-            "w212": lambda: load_w2(1, 3),
-            "w21": lambda: load_w2(1, 2),
-            "w2x": lambda: load_w2(2, 4),
-            "o2": lambda: nc.sync.dma_start(partner_list[:], offs2),
-            "a23": lambda: load_a(*a_cuts[2]),
-            "w2r": lambda: load_w2(*w2_cuts[1]),
-        }
-        for step in OPT["loads"].split():
-            steps[step]()
+        for lo in (0, GROUPS // 2):
+            hi = lo + GROUPS // 2
+            nc.vector.tensor_copy(slot_sc[0][:, lo * P : hi * P], dy_sc[:].indirect(entries(DX, lo, hi)))
+        nc.sync.dma_start(out=gate_rows[0:GROUPS, :], in_=gate[0:1, :].rearrange("o (t c) -> (o t) c", c=P))
+        load_scale_rows(nc, w2_sc, w2t_scales.rearrange("e s b w -> (e s) b w"))
+        load_w2(0, 1)
+        load_a(1, 2)
+        nc.sync.dma_start(out=slot_sc[1][0:MOVED_ROWS, :].bitcast(I32), in_=slot_sc[0][4 : 4 + MOVED_ROWS, :].bitcast(I32))
+        load_scale_rows(nc, wp_sc, wpt_scales.rearrange("e s b w -> (e s) b w"))
+        wp_w = held([P, E, 4 * K], U8, "wp_w")
+        nc.sync.dma_start(out=wp_w[:].bitcast(I32), in_=wpt_words.rearrange("e s p k d -> p (e s) (k d)").bitcast(I32))
+        w1_w = held([P, E, 2 * K], U8, "w1_w")
+        nc.sync.dma_start(out=w1_w[:].bitcast(I32), in_=w1t_words.bitcast(I32).rearrange("e s p w -> p (e s) w"))
+        load_scale_rows(nc, w1_sc, w1t_scales.rearrange("e s b w -> (e s) b w"))
+        nc.sync.dma_start(partner_list[:], offs2)
+        load_w2(1, 2)
+        load_a(2, E)
+        load_w2(2, E)
 
-        g_w = {}
+        slot_w = {}
 
-        def gather_words(lo, hi, s, tag=None):
-            part = keep.tile([P, (hi - lo) * P], U32, name=f"g_w{lo}{s}", tag=tag or f"g_w{lo}{s}", align_bytes=64)
-            entries = token_list[:, lo * P // GROUP : hi * P // GROUP]
-            nc.vector.tensor_copy(part[:], dy_w[s][:].bitcast(U32).indirect(entries))
+        def gather_words(lo, hi, s, after=None):
+            part = held([P, (hi - lo) * P], U32, f"slot_w{lo}{s}", after)
+            nc.vector.tensor_copy(part[:], dy_w[s][:].bitcast(U32).indirect(entries(DX, lo, hi)))
             for t in range(lo, hi):
-                g_w[t, s] = part[:, (t - lo) * P : (t - lo + 1) * P]
-
-        sig, rest = {}, {}
+                slot_w[t, s] = part[:, (t - lo) * P : (t - lo + 1) * P]
 
         def turn_a(e, halves):
             banks = {}
             for u in halves:
-                a_ps = psum.tile([P, H], F32, name="a_ps", tag="a_ps", bufs=3)
+                banks[u] = psum.tile([P, H], F32, name="a_turned", bufs=A_BANKS)
                 for c in range(H // P):
-                    nc.tensor.transpose(a_ps[:, c * P : (c + 1) * P], a_sb[e][:, c, u * P : (u + 1) * P], ident[:])
-                banks[u] = a_ps
+                    nc.tensor.transpose(banks[u][:, c * P : (c + 1) * P], a_sb[e][:, c, u * P : (u + 1) * P], ident[:])
             return banks
 
-        def activate(e, banks, dest, func, scale, tag=None):
-            name = f"sig{e}" if dest is sig else f"rest{e}"
-            if e not in dest:
-                dest[e] = keep.tile([P, TPE * H], F32, name=name, tag=tag or name, align_bytes=64)
+        sig, silu_neg = {}, {}
+
+        def sigmoid(e, banks, after=None):
+            if e not in sig:
+                sig[e] = held([P, PER_EXPERT * H], F32, f"sig{e}", after)
             for u in banks:
-                nc.scalar.activation(dest[e][:, u * H : (u + 1) * H], banks[u][:], func, scale=scale)
+                nc.scalar.activation(sig[e][:, u * H : (u + 1) * H], banks[u][:], ACT.Sigmoid, scale=1.0)
 
-        if OPT["warm"]:
-            warm = psum.tile([P, H], F32, name="warm", tag="sums")
-            for c in range(OPT["warm"]):
-                nc.tensor.transpose(warm[:, (c % 4) * P : (c % 4 + 1) * P], ident[:], ident[:])
+        def silu(e, banks):
+            if e not in silu_neg:
+                silu_neg[e] = held([P, PER_EXPERT * H], F32, f"silu_neg{e}")
+            for u in banks:
+                nc.scalar.activation(silu_neg[e][:, u * H : (u + 1) * H], banks[u][:], ACT.Silu, scale=-1.0)
+
         banks = turn_a(0, (0, 1))
-        activate(0, banks, sig, ACT.Sigmoid, 1.0)
-        for lo, hi, s in OPT["g_early"]:
-            gather_words(lo, hi, s)
-        activate(0, banks, rest, ACT.Silu, -1.0)
-        gate_ps = psum.tile([P, P], F32, name="gate_ps", tag="turn", bufs=1)
-        nc.tensor.transpose(gate_ps[:], gate_rows[:], ident[:])
-        neg_gate = keep.tile([P, TILES], F32, name="neg_gate")
-        nc.vector.tensor_scalar(neg_gate[:], gate_ps[:, 0:TILES], -1.0, None, ALU.mult)
+        sigmoid(0, banks)
+        gather_words(0, GROUPS // 2, 0)
+        gather_words(0, GROUPS // 2, 1)
+        gather_words(GROUPS // 2, GROUPS, 0)
+        silu(0, banks)
+        gate_turned = psum.tile([P, P], F32, name="gate_turned", tag="back", bufs=1)
+        nc.tensor.transpose(gate_turned[:], gate_rows[:], ident[:])
+        neg_gate = keep.tile([P, GROUPS], F32, name="neg_gate")
+        nc.vector.tensor_scalar(neg_gate[:], gate_turned[:, 0:GROUPS], -1.0, None, ALU.mult)
 
-        stage = {}
-        window = [[keep.tile([P, T], F32, name=f"window{kt}{w}") for w in range(2)] for kt in range(KT)]
-        dh_rows, neg_ds, dq = {}, {}, {}
-
-        def make_factor(e, tag=None):
-            assert e in sig and e in rest
-            neg_ds[e] = keep.tile([P, TPE * H], F32, name=f"neg_d{e}", tag=tag or f"neg_d{e}", align_bytes=64)
-            if OPT["mode"][e] == "p":
-                nc.scalar.activation(neg_ds[e][:], rest[e][:], ACT.Copy, bias=-1.0)
-            elif e not in OPT["split"]:
-                nc.vector.scalar_tensor_tensor(neg_ds[e][:], rest[e][:], 1.0, sig[e][:], ALU.subtract, ALU.mult)
-
-        first_sums = {}
+        window = [[keep.tile([P, T], F32, name=f"window{kt}{which}") for which in (DX, DP)] for kt in range(K // P)]
+        factor, sums, gated, dh_rows, dq, products, staged = {}, {}, {}, {}, {}, {}, {}
 
         def first_product(t):
-            e = t // TPE
-            if True:
-                if t in OPT["sa"]:
-                    sums = psum.tile([P, H], F32, name="sums", tag="a_ps", bufs=3)
-                elif t in OPT["sb"]:
-                    sums = psum.tile([P, H], F32, name="sums", tag="both")
-                else:
-                    sums = psum.tile([P, H], F32, name="sums", tag="sums")
-                first_sums[t] = sums
-                for s in range(PASSES):
-                    m = e * PASSES + s
-                    nc.tensor.matmul_mx(
-                        out=sums[:],
-                        lhsT=g_w[t, s].bitcast(FP8X4),
-                        lhsT_scale=g_sc[s][:, t * P : (t + 1) * P],
-                        rhs=w2_w[e][:, s, :].bitcast(FP4X4),
-                        rhs_scale=w2_sc[:, m * H : (m + 1) * H],
-                        start=(s == 0),
-                        stop=(s == PASSES - 1),
-                    )
+            e = t // PER_EXPERT
+            sums[t] = psum.tile([P, H], F32, name="sums")
+            for s in range(PASSES):
+                m = e * PASSES + s
+                nc.tensor.matmul_mx(
+                    out=sums[t][:],
+                    lhsT=slot_w[t, s].bitcast(FP8X4),
+                    lhsT_scale=slot_sc[s][:, t * P : (t + 1) * P],
+                    rhs=w2_w[e][:, s, :].bitcast(FP4X4),
+                    rhs_scale=w2_sc[:, m * H : (m + 1) * H],
+                    start=(s == 0),
+                    stop=(s == PASSES - 1),
+                )
 
-        gateds = {}
+        def gate_sums(t):
+            first_product(t)
+            gated[t] = held([P, H], F32, f"gated{t}")
+            nc.scalar.activation(gated[t][:], sums[t][:], ACT.Copy, scale=neg_gate[:, t : t + 1])
 
-        def gate_sums(t, tag=None):
-            if t not in first_sums:
-                first_product(t)
-            gateds[t] = keep.tile([P, H], F32, name=f"gated{t}", tag=tag or f"gated{t}", align_bytes=64)
-            nc.scalar.activation(gateds[t][:], first_sums[t][:], ACT.Copy, scale=neg_gate[:, t : t + 1])
-
-        def make_dh(lo, hi, tag=None):
-            e = lo // TPE
-            neg_d = neg_ds[e]
-            turned = psum.tile([P, hi - lo, 2, P], F32, name="turned", tag="turn", bufs=1)
+        def make_dh(lo, hi):
+            e = lo // PER_EXPERT
+            back = psum.tile([P, hi - lo, 2, P], F32, name="back", tag="back", bufs=1)
             for t in range(lo, hi):
-                cols = slice((t % TPE) * H, (t % TPE + 1) * H)
-                if t not in first_sums:
-                    first_product(t)
-                sums = first_sums[t]
-                if e in OPT["split"]:
-                    nc.vector.scalar_tensor_tensor(neg_d[:, cols], rest[e][:, cols], 1.0, sig[e][:, cols], ALU.subtract, ALU.mult)
-                dh_t = keep.tile([P, H], BF16, name=f"dh_t{t}", tag=(tag if t == lo and tag and OPT["mode"][e] != "p" else OPT["zt"].get(t, f"dh_t{t}")), align_bytes=64)
-                if OPT["mode"][e] != "v":
-                    if t not in gateds:
-                        gate_sums(t)
-                    gated = gateds[t]
-                    if OPT["mode"][e] == "p":
-                        half = keep.tile([P, H], F32, name=f"half{t}", tag=(tag if t == lo and tag else f"half{t}"), align_bytes=64)
-                        nc.gpsimd.tensor_tensor(half[:], gated[:], sig[e][:, cols], ALU.mult)
-                        gated = half
-                    nc.gpsimd.tensor_tensor(dh_t[:], gated[:], neg_d[:, cols], ALU.mult)
+                cols = slice((t % PER_EXPERT) * H, (t % PER_EXPERT + 1) * H)
+                if e == 2:
+                    dh_t = held([P, H], BF16, f"dh_t{t}")
+                    partial = held([P, H], F32, f"partial{t}")
+                    nc.gpsimd.tensor_tensor(partial[:], gated[t][:], sig[e][:, cols], ALU.mult)
+                    nc.gpsimd.tensor_tensor(dh_t[:], partial[:], factor[e][:, cols], ALU.mult)
+                elif e == 3:
+                    dh_t = held([P, H], BF16, f"dh_t{t}")
+                    gate_sums(t)
+                    nc.gpsimd.tensor_tensor(dh_t[:], gated[t][:], factor[e][:, cols], ALU.mult)
                 else:
-                    nc.vector.scalar_tensor_tensor(dh_t[:], sums[:], neg_gate[:, t : t + 1], neg_d[:, cols], ALU.mult, ALU.mult)
+                    first_product(t)
+                    nc.vector.scalar_tensor_tensor(
+                        factor[e][:, cols], silu_neg[e][:, cols], 1.0, sig[e][:, cols], ALU.subtract, ALU.mult
+                    )
+                    dh_t = held([P, H], BF16, f"dh_t{t}")
+                    nc.vector.scalar_tensor_tensor(
+                        dh_t[:], sums[t][:], neg_gate[:, t : t + 1], factor[e][:, cols], ALU.mult, ALU.mult
+                    )
                 pairs = dh_t[:].bitcast(F32)
                 for v in range(2):
-                    nc.tensor.transpose(turned[:, t - lo, v, :], pairs[:, v : H // 2 : 2], ident[:])
-            dh_rows[lo] = keep.tile([P, (hi - lo) * H], BF16, name=f"dh_rows{lo}", tag=f"dh_rows{lo}", align_bytes=64)
+                    nc.tensor.transpose(back[:, t - lo, v, :], pairs[:, v : H // 2 : 2], ident[:])
+            dh_rows[lo] = held([P, (hi - lo) * H], BF16, f"dh_rows{lo}")
             nc.scalar.copy(
                 dh_rows[lo][:].bitcast(F32).rearrange("p (u j v) -> p u j v", u=hi - lo, v=2),
-                turned[:].rearrange("p u v j -> p u j v"),
+                back[:].rearrange("p u v j -> p u j v"),
             )
 
-        def quantise(lo, hi, tag=None):
-            codes = keep.tile([P, (hi - lo) * P], U32, name=f"dq_w{lo}", tag=tag or f"dq_w{lo}", align_bytes=64)
-            scales = keep.tile([P, (hi - lo) * P], U8, name=f"dq_sc{lo}", align_bytes=64)
+        def quantise(lo, hi):
+            codes = held([P, (hi - lo) * P], U32, f"dq_w{lo}")
+            scales = held([P, (hi - lo) * P], U8, f"dq_sc{lo}")
             nc.vector.quantize_mx(out=codes[:].bitcast(FP8X4), scales=scales[:], in_=dh_rows[lo][:])
             dq[lo] = (codes, scales)
 
-        banks2 = {}
-
-        def multiply(lo, hi, kt):
-            e = lo // TPE
+        def second_products(lo, hi, kt):
+            e = lo // PER_EXPERT
             codes, scales = dq[lo]
-            both = psum.tile([P, 2, (hi - lo) * P], F32, name="both", tag="both")
+            products[lo, kt] = psum.tile([P, 2, (hi - lo) * P], F32, name="products")
             cols = slice(e * K + kt * P, e * K + (kt + 1) * P)
             nc.tensor.matmul_mx(
-                out=both[:, 0, :],
-                lhsT=w1_w[e][:, 2 * kt * P : 2 * (kt + 1) * P].bitcast(FP4X4),
+                out=products[lo, kt][:, DX, :],
+                lhsT=w1_w[:, e, 2 * kt * P : 2 * (kt + 1) * P].bitcast(FP4X4),
                 lhsT_scale=w1_sc[:, cols],
                 rhs=codes[:].bitcast(FP8X4),
                 rhs_scale=scales[:],
@@ -278,66 +231,94 @@ def tile_moe_dub_silu_kernel(
                 stop=True,
             )
             nc.tensor.matmul_mx(
-                out=both[:, 1, :],
-                lhsT=wp_w[e][:, 4 * kt * P : 4 * (kt + 1) * P].bitcast(FP8X4),
+                out=products[lo, kt][:, DP, :],
+                lhsT=wp_w[:, e, 4 * kt * P : 4 * (kt + 1) * P].bitcast(FP8X4),
                 lhsT_scale=wp_sc[:, cols],
                 rhs=codes[:].bitcast(FP8X4),
                 rhs_scale=scales[:],
                 start=True,
                 stop=True,
             )
-            banks2[lo, kt] = both
 
-        def unload(lo, hi, kt, ws, tag=None):
-            part = keep.tile([P, len(ws), (hi - lo) * P], F32, name=f"stage{lo}{kt}{ws[0]}", tag=tag or f"stage{lo}{kt}{ws[0]}", align_bytes=64)
-            nc.scalar.copy(part[:], banks2[lo, kt][:, ws[0] : ws[-1] + 1, :])
-            for w in ws:
-                stage[lo, kt, w] = part[:, w - ws[0], :]
+        def stage(lo, hi, kt, results, after=None):
+            part = held([P, len(results), (hi - lo) * P], F32, f"staged{lo}{kt}{results[0]}", after)
+            nc.scalar.copy(part[:], products[lo, kt][:, results[0] : results[-1] + 1, :])
+            for which in results:
+                staged[lo, kt, which] = part[:, which - results[0], :]
 
-        def scatter(lo, hi, kt, w):
-            entries = (token_list, partner_list)[w][:, lo * P // GROUP : hi * P // GROUP]
-            nc.vector.tensor_copy(window[kt][w][:].indirect(entries), stage[lo, kt, w])
+        def scatter(lo, hi, kt, results):
+            for which in results:
+                nc.vector.tensor_copy(window[kt][which][:].indirect(entries(which, lo, hi)), staged[lo, kt, which])
 
-        def finish(kt, lo, hi):
-            total = keep.tile([P, hi - lo], F32, name=f"total{kt}_{lo}")
-            (nc.gpsimd if kt == 0 and OPT["padd"] else nc.vector).tensor_tensor(total[:], window[kt][0][:, lo:hi], window[kt][1][:, lo:hi], ALU.add)
-            (nc.scalar if kt == 0 else nc.sync).dma_start(out=out[kt * P : (kt + 1) * P, lo:hi], in_=total[:])
+        def add_and_store(adder, queue, kt, pieces):
+            width = T // pieces
+            for lo in range(0, T, width):
+                total = keep.tile([P, width], F32, name=f"total{kt}_{lo}")
+                adder.tensor_tensor(total[:], window[kt][DX][:, lo : lo + width], window[kt][DP][:, lo : lo + width], ALU.add)
+                queue.dma_start(out=out[kt * P : (kt + 1) * P, lo : lo + width], in_=total[:])
 
-        held = {}
-        FUNC = {"S": (sig, ACT.Sigmoid, 1.0), "L": (rest, ACT.Silu, -1.0)}
-        for step in OPT["prog"].split():
-            op, arg, tag = step[0], step[1:].split(":")[0], (step.split(":") + [None])[1]
-            if op in "SL":
-                e = int(arg[0])
-                if arg[1:] == "h":
-                    activate(e, held[e], *FUNC[op], tag)
-                elif arg[1:] == "b":
-                    activate(e, {1: held[e][1]}, *FUNC[op], tag)
-                    activate(e, turn_a(e, (0,)), *FUNC[op], tag)
-                else:
-                    held[e] = turn_a(e, (0, 1))
-                    activate(e, held[e], *FUNC[op], tag)
-            elif op == "G":
-                gather_words(int(arg[0]), int(arg[1]), int(arg[2]), tag)
-            elif op == "F":
-                make_factor(int(arg), tag)
-            elif op == "P":
-                assert int(arg) not in first_sums
-                first_product(int(arg))
-            elif op == "H":
-                assert int(arg) not in gateds and OPT["mode"][int(arg) // TPE] != "v"
-                gate_sums(int(arg), tag)
-            elif op == "D":
-                make_dh(int(arg[0]), int(arg[1]), tag)
-            elif op == "Q":
-                quantise(int(arg[0]), int(arg[1]), tag)
-            elif op == "M":
-                multiply(int(arg[0]), int(arg[1]), int(arg[2]))
-            elif op == "U":
-                unload(int(arg[0]), int(arg[1]), int(arg[2]), [int(w) for w in arg[3:]], tag)
-            elif op == "X":
-                for w in arg[3:]:
-                    scatter(int(arg[0]), int(arg[1]), int(arg[2]), int(w))
-            elif op == "E":
-                finish(int(arg), 0, T // 2)
-                finish(int(arg), T // 2, T)
+        both = (DX, DP)
+
+        factor[0] = held([P, PER_EXPERT * H], F32, "factor0")
+        make_dh(0, 1)
+        quantise(0, 1)
+        make_dh(1, 2)
+        banks = turn_a(1, (0, 1))
+        silu(1, banks)
+        quantise(1, 2)
+        second_products(0, 1, 0)
+        second_products(0, 1, 1)
+        gather_words(GROUPS // 2, GROUPS, 1, after="dh_rows0")
+        stage(0, 1, 0, both)
+        stage(0, 1, 1, both)
+        sigmoid(1, banks, after="dq_w0")
+        banks = turn_a(2, (0, 1))
+        sigmoid(2, banks)
+        second_products(1, 2, 0)
+        stage(1, 2, 0, both)
+
+        factor[1] = held([P, PER_EXPERT * H], F32, "factor1")
+        make_dh(2, 4)
+        second_products(1, 2, 1)
+        quantise(2, 4)
+        stage(1, 2, 1, both, after="dh_t3")
+        for kt in range(K // P):
+            second_products(2, 4, kt)
+            stage(2, 4, kt, both)
+
+        silu(2, {1: banks[1]})
+        silu(2, turn_a(2, (0,)))
+        gate_sums(4)
+        gate_sums(5)
+        factor[2] = held([P, PER_EXPERT * H], F32, "factor2", after="dq_w2")
+        nc.scalar.activation(factor[2][:], silu_neg[2][:], ACT.Copy, bias=-1.0)
+        make_dh(4, 6)
+        quantise(4, 6)
+        second_products(4, 6, 1)
+        stage(4, 6, 1, (DX,))
+        second_products(4, 6, 0)
+        stage(4, 6, 0, both)
+
+        banks = turn_a(3, (0, 1))
+        silu(3, banks)
+        sigmoid(3, {1: banks[1]})
+        sigmoid(3, turn_a(3, (0,)))
+        factor[3] = held([P, PER_EXPERT * H], F32, "factor3", after="dh_rows4")
+        nc.vector.scalar_tensor_tensor(factor[3][:], silu_neg[3][:], 1.0, sig[3][:], ALU.subtract, ALU.mult)
+        make_dh(6, 8)
+        quantise(6, 8)
+        stage(4, 6, 1, (DP,), after="dh_t7")
+        for kt in range(K // P):
+            second_products(6, 8, kt)
+            stage(6, 8, kt, both)
+
+        for lo, hi in ((0, 1), (1, 2), (2, 4)):
+            for kt in range(K // P):
+                scatter(lo, hi, kt, both)
+        scatter(4, 6, 1, (DX,))
+        scatter(4, 6, 0, both)
+        scatter(4, 6, 1, (DP,))
+        scatter(6, 8, 0, both)
+        add_and_store(nc.gpsimd, nc.scalar, 0, 2)
+        scatter(6, 8, 1, both)
+        add_and_store(nc.vector, nc.sync, 1, 4)

@@ -26,13 +26,13 @@ PER_COLUMN = 16
 QUADRANTS = 4
 MOVED_ROWS = 112
 DX, DP = 0, 1
-A_BANKS = 3
+RING = 4
 
 
-def load_scale_rows(nc, plane, rows):
+def load_scale_rows(queue, plane, rows):
     m = rows.shape[0]
     for q in range(QUADRANTS):
-        nc.sync.dma_start(
+        queue.dma_start(
             out=plane[32 * q : 32 * q + 4, :].bitcast(I32).rearrange("b (m w) -> b m w", m=m),
             in_=rows[:, 4 * q : 4 * q + 4, :].bitcast(I32).rearrange("m b w -> b m w"),
         )
@@ -93,25 +93,26 @@ def tile_moe_dub_silu_kernel(
                 in_=dy_scales[:, 4 * q : 4 * q + 4, :].bitcast(I32),
             )
         load_a(0, 1)
+        load_a(1, 2)
         for s in range(PASSES):
             nc.sync.dma_start(out=dy_w[s][:], in_=dy_words[s].rearrange("p n t -> p (n t)").bitcast(I32))
         for lo in (0, GROUPS // 2):
             hi = lo + GROUPS // 2
             nc.vector.tensor_copy(slot_sc[0][:, lo * P : hi * P], dy_sc[:].indirect(entries(DX, lo, hi)))
         nc.sync.dma_start(out=gate_rows[0:GROUPS, :], in_=gate[0:1, :].rearrange("o (t c) -> (o t) c", c=P))
-        load_scale_rows(nc, w2_sc, w2t_scales.rearrange("e s b w -> (e s) b w"))
         load_w2(0, 1)
-        load_a(1, 2)
+        load_scale_rows(nc.sync, w2_sc, w2t_scales.rearrange("e s b w -> (e s) b w"))
         nc.sync.dma_start(out=slot_sc[1][0:MOVED_ROWS, :].bitcast(I32), in_=slot_sc[0][4 : 4 + MOVED_ROWS, :].bitcast(I32))
-        load_scale_rows(nc, wp_sc, wpt_scales.rearrange("e s b w -> (e s) b w"))
+        load_a(2, 3)
+        load_a(3, 4)
+        load_w2(1, 2)
+        load_scale_rows(nc.sync, wp_sc, wpt_scales.rearrange("e s b w -> (e s) b w"))
         wp_w = held([P, E, 4 * K], U8, "wp_w")
         nc.sync.dma_start(out=wp_w[:].bitcast(I32), in_=wpt_words.rearrange("e s p k d -> p (e s) (k d)").bitcast(I32))
+        load_scale_rows(nc.sync, w1_sc, w1t_scales.rearrange("e s b w -> (e s) b w"))
         w1_w = held([P, E, 2 * K], U8, "w1_w")
         nc.sync.dma_start(out=w1_w[:].bitcast(I32), in_=w1t_words.bitcast(I32).rearrange("e s p w -> p (e s) w"))
-        load_scale_rows(nc, w1_sc, w1t_scales.rearrange("e s b w -> (e s) b w"))
         nc.sync.dma_start(partner_list[:], offs2)
-        load_w2(1, 2)
-        load_a(2, E)
         load_w2(2, E)
 
         slot_w = {}
@@ -122,45 +123,61 @@ def tile_moe_dub_silu_kernel(
             for t in range(lo, hi):
                 slot_w[t, s] = part[:, (t - lo) * P : (t - lo + 1) * P]
 
-        def turn_a(e, halves):
-            banks = {}
-            for u in halves:
-                banks[u] = psum.tile([P, H], F32, name="a_turned", bufs=A_BANKS)
+        sig, silu_neg, factor, a_turned = {}, {}, {}, {}
+
+        def ring(shape, name):
+            return psum.tile(shape, F32, name=name, tag="ring", bufs=RING)
+
+        def activate(t, func, scale, result):
+            if t not in a_turned:
+                e, u = divmod(t, PER_EXPERT)
+                a_turned[t] = psum.tile([P, H], F32, name="a_turned", bufs=4)
                 for c in range(H // P):
-                    nc.tensor.transpose(banks[u][:, c * P : (c + 1) * P], a_sb[e][:, c, u * P : (u + 1) * P], ident[:])
-            return banks
+                    nc.tensor.transpose(a_turned[t][:, c * P : (c + 1) * P], a_sb[e][:, c, u * P : (u + 1) * P], ident[:])
+            nc.scalar.activation(result, a_turned[t][:], func, scale=scale)
 
-        sig, silu_neg = {}, {}
+        def four_groups(table, lo, name, after=None):
+            part = held([P, 4 * H], F32, name, after)
+            for t in range(lo, lo + 4):
+                table[t] = part[:, (t - lo) * H : (t - lo + 1) * H]
+            for t in (lo, lo + 2):
+                table[t, t + 2] = part[:, (t - lo) * H : (t - lo + 2) * H]
+            table[lo, lo + 4] = part[:]
 
-        def sigmoid(e, banks, after=None):
-            if e not in sig:
-                sig[e] = held([P, PER_EXPERT * H], F32, f"sig{e}", after)
-            for u in banks:
-                nc.scalar.activation(sig[e][:, u * H : (u + 1) * H], banks[u][:], ACT.Sigmoid, scale=1.0)
+        def two_groups(table, lo, name, after=None):
+            part = held([P, 2 * H], F32, name, after)
+            table[lo], table[lo + 1], table[lo, lo + 2] = part[:, 0:H], part[:, H:], part[:]
 
-        def silu(e, banks):
-            if e not in silu_neg:
-                silu_neg[e] = held([P, PER_EXPERT * H], F32, f"silu_neg{e}")
-            for u in banks:
-                nc.scalar.activation(silu_neg[e][:, u * H : (u + 1) * H], banks[u][:], ACT.Silu, scale=-1.0)
+        four_groups(sig, 0, "sig_early")
+        four_groups(silu_neg, 0, "silu_early", after="a_sb1")
+        four_groups(silu_neg, 4, "silu_late")
 
-        banks = turn_a(0, (0, 1))
-        sigmoid(0, banks)
-        gather_words(0, GROUPS // 2, 0)
-        gather_words(0, GROUPS // 2, 1)
-        gather_words(GROUPS // 2, GROUPS, 0)
-        silu(0, banks)
-        gate_turned = psum.tile([P, P], F32, name="gate_turned", tag="back", bufs=1)
+        def sigmoid(t):
+            activate(t, ACT.Sigmoid, 1.0, sig[t])
+
+        def silu(t):
+            activate(t, ACT.Silu, -1.0, silu_neg[t])
+
+        for t in range(4):
+            sigmoid(t)
+        gather_words(0, 2, 0)
+        gather_words(0, 2, 1)
+        gather_words(2, 5, 0)
+        gather_words(2, 5, 1)
+        gather_words(5, 8, 0)
+        for t in range(4):
+            silu(t)
+        gate_turned = psum.tile([P, P], F32, name="gate_turned", tag="bank3", bufs=1)
         nc.tensor.transpose(gate_turned[:], gate_rows[:], ident[:])
         neg_gate = keep.tile([P, GROUPS], F32, name="neg_gate")
         nc.vector.tensor_scalar(neg_gate[:], gate_turned[:, 0:GROUPS], -1.0, None, ALU.mult)
 
         window = [[keep.tile([P, T], F32, name=f"window{kt}{which}") for which in (DX, DP)] for kt in range(K // P)]
-        factor, sums, gated, dh_rows, dq, products, staged = {}, {}, {}, {}, {}, {}, {}
+        sums, gated, dh_rows, dq, products, staged, dh_t = {}, {}, {}, {}, {}, {}, {}
 
-        def first_product(t):
+        def first_product(t, tag="sums"):
             e = t // PER_EXPERT
-            sums[t] = psum.tile([P, H], F32, name="sums")
+            sums[t] = psum.tile([P, H], F32, name="sums", tag=tag, bufs=1)
             for s in range(PASSES):
                 m = e * PASSES + s
                 nc.tensor.matmul_mx(
@@ -173,35 +190,50 @@ def tile_moe_dub_silu_kernel(
                     stop=(s == PASSES - 1),
                 )
 
-        def gate_sums(t):
-            first_product(t)
-            gated[t] = held([P, H], F32, f"gated{t}")
-            nc.scalar.activation(gated[t][:], sums[t][:], ACT.Copy, scale=neg_gate[:, t : t + 1])
+        def factor_on_vector(t, after=None):
+            factor[t] = held([P, H], F32, f"factor{t}", after)
+            nc.vector.scalar_tensor_tensor(factor[t][:], silu_neg[t], 1.0, sig[t], ALU.subtract, ALU.mult)
 
-        def make_dh(lo, hi):
-            e = lo // PER_EXPERT
-            back = psum.tile([P, hi - lo, 2, P], F32, name="back", tag="back", bufs=1)
+        def dh_on_vector(t):
+            dh_t[t] = held([P, H], BF16, f"dh_t{t}")[:]
+            nc.vector.scalar_tensor_tensor(dh_t[t], sums[t][:], neg_gate[:, t : t + 1], factor[t][:], ALU.mult, ALU.mult)
+
+        def less_one(engine, lo, hi, source, after=None):
+            part = held([P, (hi - lo) * H], F32, f"less_one{lo}", after)
+            if engine == "gpsimd":
+                nc.gpsimd.tensor_scalar(part[:], source, 1.0, -1.0, ALU.mult, ALU.add)
+            else:
+                nc.scalar.activation(part[:], source, ACT.Copy, bias=-1.0)
+            return part
+
+        def factor_on_gpsimd(lo, hi, less, sigm, after=None):
+            part = held([P, (hi - lo) * H], F32, f"factor{lo}", after)
+            nc.gpsimd.tensor_tensor(part[:], less, sigm, ALU.mult)
             for t in range(lo, hi):
-                cols = slice((t % PER_EXPERT) * H, (t % PER_EXPERT + 1) * H)
-                if e == 2:
-                    dh_t = held([P, H], BF16, f"dh_t{t}")
-                    partial = held([P, H], F32, f"partial{t}")
-                    nc.gpsimd.tensor_tensor(partial[:], gated[t][:], sig[e][:, cols], ALU.mult)
-                    nc.gpsimd.tensor_tensor(dh_t[:], partial[:], factor[e][:, cols], ALU.mult)
-                elif e == 3:
-                    dh_t = held([P, H], BF16, f"dh_t{t}")
-                    gate_sums(t)
-                    nc.gpsimd.tensor_tensor(dh_t[:], gated[t][:], factor[e][:, cols], ALU.mult)
-                else:
-                    first_product(t)
-                    nc.vector.scalar_tensor_tensor(
-                        factor[e][:, cols], silu_neg[e][:, cols], 1.0, sig[e][:, cols], ALU.subtract, ALU.mult
-                    )
-                    dh_t = held([P, H], BF16, f"dh_t{t}")
-                    nc.vector.scalar_tensor_tensor(
-                        dh_t[:], sums[t][:], neg_gate[:, t : t + 1], factor[e][:, cols], ALU.mult, ALU.mult
-                    )
-                pairs = dh_t[:].bitcast(F32)
+                factor[t] = part[:, (t - lo) * H : (t - lo + 1) * H]
+            factor[lo, hi] = part[:]
+
+        def gate_sums(t, tag="sums"):
+            first_product(t, tag)
+            e, u = divmod(t, PER_EXPERT)
+            if u == 0:
+                gated["expert", e] = held([P, PER_EXPERT * H], F32, f"gated{e}")
+            gated[t] = gated["expert", e][:, u * H : (u + 1) * H]
+            nc.scalar.activation(gated[t], sums[t][:], ACT.Copy, scale=neg_gate[:, t : t + 1])
+
+        def dh_on_gpsimd(lo, hi, wide, after=None):
+            both = held([P, (hi - lo) * H], BF16, f"dh_t{lo}", after)
+            for t in range(lo, hi):
+                dh_t[t] = both[:, (t - lo) * H : (t - lo + 1) * H]
+                if not wide:
+                    nc.gpsimd.tensor_tensor(dh_t[t], gated[t], factor[t], ALU.mult)
+            if wide:
+                nc.gpsimd.tensor_tensor(both[:], gated["expert", lo // PER_EXPERT][:], factor[lo, hi], ALU.mult)
+
+        def turn_back(lo, hi, tag="back"):
+            back = psum.tile([P, hi - lo, 2, P], F32, name="back", tag=tag, bufs=1)
+            for t in range(lo, hi):
+                pairs = dh_t[t].bitcast(F32)
                 for v in range(2):
                     nc.tensor.transpose(back[:, t - lo, v, :], pairs[:, v : H // 2 : 2], ident[:])
             dh_rows[lo] = held([P, (hi - lo) * H], BF16, f"dh_rows{lo}")
@@ -216,39 +248,30 @@ def tile_moe_dub_silu_kernel(
             nc.vector.quantize_mx(out=codes[:].bitcast(FP8X4), scales=scales[:], in_=dh_rows[lo][:])
             dq[lo] = (codes, scales)
 
-        def second_products(lo, hi, kt):
+        def second_products(lo, hi, parts, tag, after=None, part=None):
             e = lo // PER_EXPERT
             codes, scales = dq[lo]
-            products[lo, kt] = psum.tile([P, 2, (hi - lo) * P], F32, name="products")
-            cols = slice(e * K + kt * P, e * K + (kt + 1) * P)
-            nc.tensor.matmul_mx(
-                out=products[lo, kt][:, DX, :],
-                lhsT=w1_w[:, e, 2 * kt * P : 2 * (kt + 1) * P].bitcast(FP4X4),
-                lhsT_scale=w1_sc[:, cols],
-                rhs=codes[:].bitcast(FP8X4),
-                rhs_scale=scales[:],
-                start=True,
-                stop=True,
-            )
-            nc.tensor.matmul_mx(
-                out=products[lo, kt][:, DP, :],
-                lhsT=wp_w[:, e, 4 * kt * P : 4 * (kt + 1) * P].bitcast(FP8X4),
-                lhsT_scale=wp_sc[:, cols],
-                rhs=codes[:].bitcast(FP8X4),
-                rhs_scale=scales[:],
-                start=True,
-                stop=True,
-            )
-
-        def stage(lo, hi, kt, results, after=None):
-            part = held([P, len(results), (hi - lo) * P], F32, f"staged{lo}{kt}{results[0]}", after)
-            nc.scalar.copy(part[:], products[lo, kt][:, results[0] : results[-1] + 1, :])
-            for which in results:
-                staged[lo, kt, which] = part[:, which - results[0], :]
-
-        def scatter(lo, hi, kt, results):
-            for which in results:
-                nc.vector.tensor_copy(window[kt][which][:].indirect(entries(which, lo, hi)), staged[lo, kt, which])
+            bank = psum.tile([P, len(parts), (hi - lo) * P], F32, name="products", tag=tag, bufs=1)
+            for n, (kt, which) in enumerate(parts):
+                cols = slice(e * K + kt * P, e * K + (kt + 1) * P)
+                if which == DX:
+                    words, plane = w1_w[:, e, 2 * kt * P : 2 * (kt + 1) * P].bitcast(FP4X4), w1_sc
+                else:
+                    words, plane = wp_w[:, e, 4 * kt * P : 4 * (kt + 1) * P].bitcast(FP8X4), wp_sc
+                nc.tensor.matmul_mx(
+                    out=bank[:, n, :],
+                    lhsT=words,
+                    lhsT_scale=plane[:, cols],
+                    rhs=codes[:].bitcast(FP8X4),
+                    rhs_scale=scales[:],
+                    start=True,
+                    stop=True,
+                )
+            if part is None:
+                part = held([P, len(parts), (hi - lo) * P], F32, f"staged{lo}_{parts[0][0]}{parts[0][1]}", after)
+            nc.scalar.copy(part[:], bank[:])
+            for n, (kt, which) in enumerate(parts):
+                nc.vector.tensor_copy(window[kt][which][:].indirect(entries(which, lo, hi)), part[:, n, :])
 
         def add_and_store(adder, queue, kt, pieces):
             width = T // pieces
@@ -257,68 +280,56 @@ def tile_moe_dub_silu_kernel(
                 adder.tensor_tensor(total[:], window[kt][DX][:, lo : lo + width], window[kt][DP][:, lo : lo + width], ALU.add)
                 queue.dma_start(out=out[kt * P : (kt + 1) * P, lo : lo + width], in_=total[:])
 
-        both = (DX, DP)
-
-        factor[0] = held([P, PER_EXPERT * H], F32, "factor0")
-        make_dh(0, 1)
-        quantise(0, 1)
-        make_dh(1, 2)
-        banks = turn_a(1, (0, 1))
-        silu(1, banks)
-        quantise(1, 2)
-        second_products(0, 1, 0)
-        second_products(0, 1, 1)
-        gather_words(GROUPS // 2, GROUPS, 1, after="dh_rows0")
-        stage(0, 1, 0, both)
-        stage(0, 1, 1, both)
-        sigmoid(1, banks, after="dq_w0")
-        banks = turn_a(2, (0, 1))
-        sigmoid(2, banks)
-        second_products(1, 2, 0)
-        stage(1, 2, 0, both)
-
-        factor[1] = held([P, PER_EXPERT * H], F32, "factor1")
-        make_dh(2, 4)
-        second_products(1, 2, 1)
+        upper, lower = ((0, DX), (0, DP)), ((1, DX), (1, DP))
+        for t in range(4):
+            first_product(t, f"bank{t}")
+        factor_on_vector(0)
+        factor_on_vector(1)
+        dh_on_vector(0)
+        dh_on_vector(1)
+        for t in range(4, 6):
+            silu(t)
+        turn_back(0, 2, "bank0")
+        for t in range(6, 8):
+            silu(t)
+        factor_on_vector(2, after="factor0")
+        factor_on_vector(3, after="factor1")
+        gather_words(5, 8, 1, after="slot_w01")
+        quantise(0, 2)
+        dh_on_vector(2)
+        dh_on_vector(3)
+        less = less_one("gpsimd", 4, 8, silu_neg[4, 8], after="dh_rows0")
+        second_products(0, 2, upper, "bank1")
+        two_groups(sig, 4, "sig_of_2", after="dq_w0")
+        sigmoid(4)
+        turn_back(2, 4, "bank1")
         quantise(2, 4)
-        stage(1, 2, 1, both, after="dh_t3")
-        for kt in range(K // P):
-            second_products(2, 4, kt)
-            stage(2, 4, kt, both)
-
-        silu(2, {1: banks[1]})
-        silu(2, turn_a(2, (0,)))
-        gate_sums(4)
-        gate_sums(5)
-        factor[2] = held([P, PER_EXPERT * H], F32, "factor2", after="dq_w2")
-        nc.scalar.activation(factor[2][:], silu_neg[2][:], ACT.Copy, bias=-1.0)
-        make_dh(4, 6)
+        second_products(0, 2, lower, "bank2", after="dh_t3")
+        sigmoid(5)
+        second_products(2, 4, upper, "bank0")
+        factor_of_2 = held([P, 2 * H], F32, "factor_of_2", after="dh_rows2")
+        factor[4, 6] = factor_of_2[:]
+        for u in range(2):
+            nc.gpsimd.tensor_tensor(factor_of_2[:, u * H : (u + 1) * H], less[:, u * H : (u + 1) * H], sig[4 + u], ALU.mult)
+        gate_sums(4, "bank3")
+        gate_sums(5, "bank2")
+        second_products(2, 4, lower[:1], "bank1")
+        two_groups(sig, 6, "sig_of_3", after="dq_sc0")
+        sigmoid(6)
+        sigmoid(7)
+        dh_on_gpsimd(4, 6, True)
+        factor_on_gpsimd(6, 8, less[:, 2 * H :], sig[6, 8], after="gated2")
+        turn_back(4, 6, "bank1")
         quantise(4, 6)
-        second_products(4, 6, 1)
-        stage(4, 6, 1, (DX,))
-        second_products(4, 6, 0)
-        stage(4, 6, 0, both)
-
-        banks = turn_a(3, (0, 1))
-        silu(3, banks)
-        sigmoid(3, {1: banks[1]})
-        sigmoid(3, turn_a(3, (0,)))
-        factor[3] = held([P, PER_EXPERT * H], F32, "factor3", after="dh_rows4")
-        nc.vector.scalar_tensor_tensor(factor[3][:], silu_neg[3][:], 1.0, sig[3][:], ALU.subtract, ALU.mult)
-        make_dh(6, 8)
+        second_products(2, 4, lower[1:], "bank0", after="dh_t4")
+        second_products(4, 6, upper, "bank1")
+        gate_sums(6, "bank3")
+        gate_sums(7, "bank2")
+        dh_on_gpsimd(6, 8, True, after="dh_rows4")
+        turn_back(6, 8, "bank3")
         quantise(6, 8)
-        stage(4, 6, 1, (DP,), after="dh_t7")
-        for kt in range(K // P):
-            second_products(6, 8, kt)
-            stage(6, 8, kt, both)
-
-        for lo, hi in ((0, 1), (1, 2), (2, 4)):
-            for kt in range(K // P):
-                scatter(lo, hi, kt, both)
-        scatter(4, 6, 1, (DX,))
-        scatter(4, 6, 0, both)
-        scatter(4, 6, 1, (DP,))
-        scatter(6, 8, 0, both)
+        second_products(4, 6, lower, "bank0", after="dh_rows4")
+        second_products(6, 8, upper, "bank1")
         add_and_store(nc.gpsimd, nc.scalar, 0, 2)
-        scatter(6, 8, 1, both)
+        second_products(6, 8, lower, "bank2")
         add_and_store(nc.vector, nc.sync, 1, 4)

@@ -86,26 +86,26 @@ def tile_moe_dub_silu_kernel(
             for e in range(lo, hi):
                 w2_w[e] = part[:, (e - lo) * PASSES : (e - lo + 1) * PASSES, :]
 
+        load_a(0, 1)
         nc.sync.dma_start(token_list[:], offs)
         for q in range(QUADRANTS):
             nc.sync.dma_start(
                 out=dy_sc[32 * q : 32 * q + 4 * PASSES, :].bitcast(I32),
                 in_=dy_scales[:, 4 * q : 4 * q + 4, :].bitcast(I32),
             )
-        load_a(0, 1)
         load_a(1, 2)
-        for s in range(PASSES):
-            nc.sync.dma_start(out=dy_w[s][:], in_=dy_words[s].rearrange("p n t -> p (n t)").bitcast(I32))
+        nc.sync.dma_start(out=dy_w[0][:], in_=dy_words[0].rearrange("p n t -> p (n t)").bitcast(I32))
+        nc.sync.dma_start(out=gate_rows[0:GROUPS, :], in_=gate[0:1, :].rearrange("o (t c) -> (o t) c", c=P))
+        nc.sync.dma_start(out=dy_w[1][:], in_=dy_words[1].rearrange("p n t -> p (n t)").bitcast(I32))
         for lo in (0, GROUPS // 2):
             hi = lo + GROUPS // 2
             nc.vector.tensor_copy(slot_sc[0][:, lo * P : hi * P], dy_sc[:].indirect(entries(DX, lo, hi)))
-        nc.sync.dma_start(out=gate_rows[0:GROUPS, :], in_=gate[0:1, :].rearrange("o (t c) -> (o t) c", c=P))
         load_w2(0, 1)
         load_scale_rows(nc.sync, w2_sc, w2t_scales.rearrange("e s b w -> (e s) b w"))
         nc.sync.dma_start(out=slot_sc[1][0:MOVED_ROWS, :].bitcast(I32), in_=slot_sc[0][4 : 4 + MOVED_ROWS, :].bitcast(I32))
+        load_w2(1, 2)
         load_a(2, 3)
         load_a(3, 4)
-        load_w2(1, 2)
         load_scale_rows(nc.sync, wp_sc, wpt_scales.rearrange("e s b w -> (e s) b w"))
         wp_w = held([P, E, 4 * K], U8, "wp_w")
         nc.sync.dma_start(out=wp_w[:].bitcast(I32), in_=wpt_words.rearrange("e s p k d -> p (e s) (k d)").bitcast(I32))
@@ -160,11 +160,9 @@ def tile_moe_dub_silu_kernel(
 
         for t in range(4):
             sigmoid(t)
-        gather_words(0, 2, 0)
-        gather_words(0, 2, 1)
-        gather_words(2, 5, 0)
-        gather_words(2, 5, 1)
-        gather_words(5, 8, 0)
+        gather_words(0, 4, 0)
+        gather_words(0, 4, 1)
+        gather_words(4, 8, 0)
         for t in range(4):
             silu(t)
         gate_turned = psum.tile([P, P], F32, name="gate_turned", tag="bank3", bufs=1)
@@ -194,8 +192,8 @@ def tile_moe_dub_silu_kernel(
             factor[t] = held([P, H], F32, f"factor{t}", after)
             nc.vector.scalar_tensor_tensor(factor[t][:], silu_neg[t], 1.0, sig[t], ALU.subtract, ALU.mult)
 
-        def dh_on_vector(t):
-            dh_t[t] = held([P, H], BF16, f"dh_t{t}")[:]
+        def dh_on_vector(t, part=None):
+            dh_t[t] = held([P, H], BF16, f"dh_t{t}")[:] if part is None else part
             nc.vector.scalar_tensor_tensor(dh_t[t], sums[t][:], neg_gate[:, t : t + 1], factor[t][:], ALU.mult, ALU.mult)
 
         def less_one(engine, lo, hi, source, after=None):
@@ -251,7 +249,7 @@ def tile_moe_dub_silu_kernel(
         def second_products(lo, hi, parts, tag, after=None, part=None):
             e = lo // PER_EXPERT
             codes, scales = dq[lo]
-            bank = psum.tile([P, len(parts), (hi - lo) * P], F32, name="products", tag=tag, bufs=1)
+            bank = psum.tile([P, len(parts), (hi - lo) * P], F32, name="products", tag=tag, bufs=4 if tag == "a_turned" else 1)
             for n, (kt, which) in enumerate(parts):
                 cols = slice(e * K + kt * P, e * K + (kt + 1) * P)
                 if which == DX:
@@ -287,24 +285,25 @@ def tile_moe_dub_silu_kernel(
         factor_on_vector(1)
         dh_on_vector(0)
         dh_on_vector(1)
-        for t in range(4, 6):
-            silu(t)
-        turn_back(0, 2, "bank0")
-        for t in range(6, 8):
+        turn_back(0, 1, "bank0")
+        quantise(0, 1)
+        turn_back(1, 2, "bank1")
+        quantise(1, 2)
+        for t in range(4, 8):
             silu(t)
         factor_on_vector(2, after="factor0")
         factor_on_vector(3, after="factor1")
-        gather_words(5, 8, 1, after="slot_w01")
-        quantise(0, 2)
-        dh_on_vector(2)
-        dh_on_vector(3)
-        less = less_one("gpsimd", 4, 8, silu_neg[4, 8], after="dh_rows0")
-        second_products(0, 2, upper, "bank1")
+        gather_words(4, 8, 1, after="dh_rows0")
+        both = held([P, 2 * H], BF16, "dh_t2")
+        dh_on_vector(2, both[:, 0:H])
+        dh_on_vector(3, both[:, H:])
+        less = less_one("gpsimd", 4, 8, silu_neg[4, 8], after="dh_rows1")
+        second_products(0, 1, upper + lower, "bank0")
         two_groups(sig, 4, "sig_of_2", after="dq_w0")
         sigmoid(4)
-        turn_back(2, 4, "bank1")
+        turn_back(2, 4, "bank0")
         quantise(2, 4)
-        second_products(0, 2, lower, "bank2", after="dh_t3")
+        second_products(1, 2, upper + lower, "bank1", after="dh_t2")
         sigmoid(5)
         second_products(2, 4, upper, "bank0")
         factor_of_2 = held([P, 2 * H], F32, "factor_of_2", after="dh_rows2")
@@ -322,10 +321,11 @@ def tile_moe_dub_silu_kernel(
         turn_back(4, 6, "bank1")
         quantise(4, 6)
         second_products(2, 4, lower[1:], "bank0", after="dh_t4")
-        second_products(4, 6, upper, "bank1")
+        second_products(4, 6, upper[:1], "bank1")
+        second_products(4, 6, upper[1:], "a_turned")
         gate_sums(6, "bank3")
         gate_sums(7, "bank2")
-        dh_on_gpsimd(6, 8, True, after="dh_rows4")
+        dh_on_gpsimd(6, 8, False, after="dh_rows4")
         turn_back(6, 8, "bank3")
         quantise(6, 8)
         second_products(4, 6, lower, "bank0", after="dh_rows4")

@@ -86,6 +86,19 @@ def tile_moe_dub_silu_kernel(
             for e in range(lo, hi):
                 w2_w[e] = part[:, (e - lo) * PASSES : (e - lo + 1) * PASSES, :]
 
+        second_w = {}
+
+        def load_second(which, lo, hi):
+            if which == DX:
+                part = held([P, hi - lo, 2 * K], U8, f"w1_w{lo}")
+                source = w1t_words[lo:hi].bitcast(I32).rearrange("e s p w -> p (e s) w")
+            else:
+                part = held([P, hi - lo, 4 * K], U8, f"wp_w{lo}")
+                source = wpt_words[lo:hi].bitcast(I32).rearrange("e s p k d -> p (e s) (k d)")
+            nc.sync.dma_start(out=part[:].bitcast(I32), in_=source)
+            for e in range(lo, hi):
+                second_w[which, e] = part[:, e - lo, :]
+
         load_a(0, 1)
         nc.sync.dma_start(token_list[:], offs)
         for q in range(QUADRANTS):
@@ -103,17 +116,17 @@ def tile_moe_dub_silu_kernel(
         load_w2(0, 1)
         load_scale_rows(nc.sync, w2_sc, w2t_scales.rearrange("e s b w -> (e s) b w"))
         nc.sync.dma_start(out=slot_sc[1][0:MOVED_ROWS, :].bitcast(I32), in_=slot_sc[0][4 : 4 + MOVED_ROWS, :].bitcast(I32))
-        load_w2(1, 2)
         load_a(2, 3)
         load_a(3, 4)
+        load_w2(1, 2)
         load_scale_rows(nc.sync, wp_sc, wpt_scales.rearrange("e s b w -> (e s) b w"))
-        wp_w = held([P, E, 4 * K], U8, "wp_w")
-        nc.sync.dma_start(out=wp_w[:].bitcast(I32), in_=wpt_words.rearrange("e s p k d -> p (e s) (k d)").bitcast(I32))
+        load_second(DP, 0, 1)
         load_scale_rows(nc.sync, w1_sc, w1t_scales.rearrange("e s b w -> (e s) b w"))
-        w1_w = held([P, E, 2 * K], U8, "w1_w")
-        nc.sync.dma_start(out=w1_w[:].bitcast(I32), in_=w1t_words.bitcast(I32).rearrange("e s p w -> p (e s) w"))
+        load_second(DX, 0, 1)
         nc.sync.dma_start(partner_list[:], offs2)
         load_w2(2, E)
+        load_second(DP, 1, E)
+        load_second(DX, 1, E)
 
         slot_w = {}
 
@@ -189,12 +202,12 @@ def tile_moe_dub_silu_kernel(
                 )
 
         def factor_on_vector(t, after=None):
-            factor[t] = held([P, H], F32, f"factor{t}", after)
-            nc.vector.scalar_tensor_tensor(factor[t][:], silu_neg[t], 1.0, sig[t], ALU.subtract, ALU.mult)
+            factor[t] = held([P, H], F32, f"factor{t}", after)[:]
+            nc.vector.scalar_tensor_tensor(factor[t], silu_neg[t], 1.0, sig[t], ALU.subtract, ALU.mult)
 
         def dh_on_vector(t, part=None):
             dh_t[t] = held([P, H], BF16, f"dh_t{t}")[:] if part is None else part
-            nc.vector.scalar_tensor_tensor(dh_t[t], sums[t][:], neg_gate[:, t : t + 1], factor[t][:], ALU.mult, ALU.mult)
+            nc.vector.scalar_tensor_tensor(dh_t[t], sums[t][:], neg_gate[:, t : t + 1], factor[t], ALU.mult, ALU.mult)
 
         def less_one(engine, lo, hi, source, after=None):
             part = held([P, (hi - lo) * H], F32, f"less_one{lo}", after)
@@ -253,9 +266,9 @@ def tile_moe_dub_silu_kernel(
             for n, (kt, which) in enumerate(parts):
                 cols = slice(e * K + kt * P, e * K + (kt + 1) * P)
                 if which == DX:
-                    words, plane = w1_w[:, e, 2 * kt * P : 2 * (kt + 1) * P].bitcast(FP4X4), w1_sc
+                    words, plane = second_w[DX, e][:, 2 * kt * P : 2 * (kt + 1) * P].bitcast(FP4X4), w1_sc
                 else:
-                    words, plane = wp_w[:, e, 4 * kt * P : 4 * (kt + 1) * P].bitcast(FP8X4), wp_sc
+                    words, plane = second_w[DP, e][:, 4 * kt * P : 4 * (kt + 1) * P].bitcast(FP8X4), wp_sc
                 nc.tensor.matmul_mx(
                     out=bank[:, n, :],
                     lhsT=words,
@@ -279,21 +292,25 @@ def tile_moe_dub_silu_kernel(
                 queue.dma_start(out=out[kt * P : (kt + 1) * P, lo : lo + width], in_=total[:])
 
         upper, lower = ((0, DX), (0, DP)), ((1, DX), (1, DP))
-        for t in range(4):
-            first_product(t, f"bank{t}")
+        first_product(0, "bank0")
+        first_product(1, "bank1")
         factor_on_vector(0)
         factor_on_vector(1)
         dh_on_vector(0)
         dh_on_vector(1)
+        silu(4)
+        silu(5)
         turn_back(0, 1, "bank0")
         quantise(0, 1)
         turn_back(1, 2, "bank1")
         quantise(1, 2)
-        for t in range(4, 8):
-            silu(t)
-        factor_on_vector(2, after="factor0")
-        factor_on_vector(3, after="factor1")
-        gather_words(4, 8, 1, after="dh_rows0")
+        silu(6)
+        silu(7)
+        first_product(2, "bank2")
+        first_product(3, "bank3")
+        factor_on_gpsimd(2, 3, less_one("gpsimd", 2, 3, silu_neg[2])[:], sig[2])
+        gather_words(4, 8, 1, after="factor1")
+        factor_on_vector(3, after="dh_rows0")
         both = held([P, 2 * H], BF16, "dh_t2")
         dh_on_vector(2, both[:, 0:H])
         dh_on_vector(3, both[:, H:])
@@ -317,7 +334,7 @@ def tile_moe_dub_silu_kernel(
         sigmoid(6)
         sigmoid(7)
         dh_on_gpsimd(4, 6, True)
-        factor_on_gpsimd(6, 8, less[:, 2 * H :], sig[6, 8], after="gated2")
+        factor_on_gpsimd(6, 7, less[:, 2 * H : 3 * H], sig[6], after="gated2")
         turn_back(4, 6, "bank1")
         quantise(4, 6)
         second_products(2, 4, lower[1:], "bank0", after="dh_t4")
@@ -325,11 +342,17 @@ def tile_moe_dub_silu_kernel(
         second_products(4, 6, upper[1:], "a_turned")
         gate_sums(6, "bank3")
         gate_sums(7, "bank2")
-        dh_on_gpsimd(6, 8, False, after="dh_rows4")
+        second_products(4, 6, lower[:1], "a_turned")
+        last = held([P, 2 * H], F32, "last", after="dh_rows4")
+        dh_t[6], dh_t[7] = last[:, H : H + H // 2].bitcast(BF16), last[:, H + H // 2 :].bitcast(BF16)
+        nc.gpsimd.tensor_tensor(dh_t[6], gated[6], factor[6], ALU.mult)
+        nc.gpsimd.tensor_tensor(last[:, 0:H], less[:, 3 * H :], sig[7], ALU.mult)
+        nc.gpsimd.tensor_tensor(dh_t[7], gated[7], last[:, 0:H], ALU.mult)
         turn_back(6, 8, "bank3")
         quantise(6, 8)
-        second_products(4, 6, lower, "bank0", after="dh_rows4")
-        second_products(6, 8, upper, "bank1")
+        second_products(4, 6, lower[1:], "bank0", after="dh_rows4")
+        second_products(6, 8, upper[:1], "bank1")
+        second_products(6, 8, upper[1:], "a_turned")
         add_and_store(nc.gpsimd, nc.scalar, 0, 2)
         second_products(6, 8, lower, "bank2")
         add_and_store(nc.vector, nc.sync, 1, 4)

@@ -26,13 +26,15 @@ PER_COLUMN = 16
 QUADRANTS = 4
 MOVED_ROWS = 112
 DX, DP = 0, 1
-RING = 4
+HALF = GROUPS // 2
+A_BANKS = 4
+UPPER, LOWER = ((0, DX), (0, DP)), ((1, DX), (1, DP))
 
 
-def load_scale_rows(queue, plane, rows):
+def load_scale_rows(nc, plane, rows):
     m = rows.shape[0]
     for q in range(QUADRANTS):
-        queue.dma_start(
+        nc.sync.dma_start(
             out=plane[32 * q : 32 * q + 4, :].bitcast(I32).rearrange("b (m w) -> b m w", m=m),
             in_=rows[:, 4 * q : 4 * q + 4, :].bitcast(I32).rearrange("m b w -> b m w"),
         )
@@ -49,6 +51,9 @@ def tile_moe_dub_silu_kernel(
 
         def held(shape, dtype, name, after=None):
             return keep.tile(shape, dtype, name=name, tag=after or name, align_bytes=64)
+
+        def bank(shape, name, tag):
+            return psum.tile(shape, F32, name=name, tag=tag, bufs=A_BANKS if tag == "a_turned" else 1)
 
         token_list = lists.tile([P, SLOTS // PER_COLUMN], U16, name="token_list")
         partner_list = lists.tile([P, SLOTS // PER_COLUMN], U16, name="partner_list")
@@ -70,7 +75,7 @@ def tile_moe_dub_silu_kernel(
         make_identity(nc, ident[:])
 
         dy_w = [held([P, T], I32, f"dy_w{s}") for s in range(PASSES)]
-        a_sb, w2_w = {}, {}
+        a_sb, w2_w, second_w = {}, {}, {}
 
         def load_a(lo, hi):
             part = held([P, H // P, (hi - lo) * C], F32, f"a_sb{lo}")
@@ -85,8 +90,6 @@ def tile_moe_dub_silu_kernel(
             )
             for e in range(lo, hi):
                 w2_w[e] = part[:, (e - lo) * PASSES : (e - lo + 1) * PASSES, :]
-
-        second_w = {}
 
         def load_second(which, lo, hi):
             if which == DX:
@@ -110,60 +113,46 @@ def tile_moe_dub_silu_kernel(
         nc.sync.dma_start(out=dy_w[0][:], in_=dy_words[0].rearrange("p n t -> p (n t)").bitcast(I32))
         nc.sync.dma_start(out=gate_rows[0:GROUPS, :], in_=gate[0:1, :].rearrange("o (t c) -> (o t) c", c=P))
         nc.sync.dma_start(out=dy_w[1][:], in_=dy_words[1].rearrange("p n t -> p (n t)").bitcast(I32))
-        for lo in (0, GROUPS // 2):
-            hi = lo + GROUPS // 2
+        for lo in (0, HALF):
+            hi = lo + HALF
             nc.vector.tensor_copy(slot_sc[0][:, lo * P : hi * P], dy_sc[:].indirect(entries(DX, lo, hi)))
         load_w2(0, 1)
-        load_scale_rows(nc.sync, w2_sc, w2t_scales.rearrange("e s b w -> (e s) b w"))
+        load_scale_rows(nc, w2_sc, w2t_scales.rearrange("e s b w -> (e s) b w"))
         nc.sync.dma_start(out=slot_sc[1][0:MOVED_ROWS, :].bitcast(I32), in_=slot_sc[0][4 : 4 + MOVED_ROWS, :].bitcast(I32))
         load_a(2, 3)
         load_a(3, 4)
         load_w2(1, 2)
-        load_scale_rows(nc.sync, wp_sc, wpt_scales.rearrange("e s b w -> (e s) b w"))
+        load_scale_rows(nc, wp_sc, wpt_scales.rearrange("e s b w -> (e s) b w"))
         load_second(DP, 0, 1)
-        load_scale_rows(nc.sync, w1_sc, w1t_scales.rearrange("e s b w -> (e s) b w"))
+        load_scale_rows(nc, w1_sc, w1t_scales.rearrange("e s b w -> (e s) b w"))
         load_second(DX, 0, 1)
         nc.sync.dma_start(partner_list[:], offs2)
         load_w2(2, E)
         load_second(DP, 1, E)
         load_second(DX, 1, E)
 
-        slot_w = {}
+        slot_w, a_turned, sig, silu_neg, less_one, factor = {}, {}, {}, {}, {}, {}
+        sums, gated, dh_t, dh_rows, dq = {}, {}, {}, {}, {}
 
-        def gather_words(lo, hi, s, after=None):
-            part = held([P, (hi - lo) * P], U32, f"slot_w{lo}{s}", after)
-            nc.vector.tensor_copy(part[:], dy_w[s][:].bitcast(U32).indirect(entries(DX, lo, hi)))
+        def by_group(table, lo, hi, dtype, name, after=None):
+            part = held([P, (hi - lo) * H], dtype, name, after)
             for t in range(lo, hi):
+                table[t] = part[:, (t - lo) * H : (t - lo + 1) * H]
+            table[lo, hi] = part[:]
+
+        def gather_words(lo, s, after=None):
+            part = held([P, HALF * P], U32, f"slot_w{lo}{s}", after)
+            nc.vector.tensor_copy(part[:], dy_w[s][:].bitcast(U32).indirect(entries(DX, lo, lo + HALF)))
+            for t in range(lo, lo + HALF):
                 slot_w[t, s] = part[:, (t - lo) * P : (t - lo + 1) * P]
-
-        sig, silu_neg, factor, a_turned = {}, {}, {}, {}
-
-        def ring(shape, name):
-            return psum.tile(shape, F32, name=name, tag="ring", bufs=RING)
 
         def activate(t, func, scale, result):
             if t not in a_turned:
                 e, u = divmod(t, PER_EXPERT)
-                a_turned[t] = psum.tile([P, H], F32, name="a_turned", bufs=4)
+                a_turned[t] = bank([P, H], "a_turned", "a_turned")
                 for c in range(H // P):
                     nc.tensor.transpose(a_turned[t][:, c * P : (c + 1) * P], a_sb[e][:, c, u * P : (u + 1) * P], ident[:])
             nc.scalar.activation(result, a_turned[t][:], func, scale=scale)
-
-        def four_groups(table, lo, name, after=None):
-            part = held([P, 4 * H], F32, name, after)
-            for t in range(lo, lo + 4):
-                table[t] = part[:, (t - lo) * H : (t - lo + 1) * H]
-            for t in (lo, lo + 2):
-                table[t, t + 2] = part[:, (t - lo) * H : (t - lo + 2) * H]
-            table[lo, lo + 4] = part[:]
-
-        def two_groups(table, lo, name, after=None):
-            part = held([P, 2 * H], F32, name, after)
-            table[lo], table[lo + 1], table[lo, lo + 2] = part[:, 0:H], part[:, H:], part[:]
-
-        four_groups(sig, 0, "sig_early")
-        four_groups(silu_neg, 0, "silu_early", after="a_sb1")
-        four_groups(silu_neg, 4, "silu_late")
 
         def sigmoid(t):
             activate(t, ACT.Sigmoid, 1.0, sig[t])
@@ -171,24 +160,9 @@ def tile_moe_dub_silu_kernel(
         def silu(t):
             activate(t, ACT.Silu, -1.0, silu_neg[t])
 
-        for t in range(4):
-            sigmoid(t)
-        gather_words(0, 4, 0)
-        gather_words(0, 4, 1)
-        gather_words(4, 8, 0)
-        for t in range(4):
-            silu(t)
-        gate_turned = psum.tile([P, P], F32, name="gate_turned", tag="bank3", bufs=1)
-        nc.tensor.transpose(gate_turned[:], gate_rows[:], ident[:])
-        neg_gate = keep.tile([P, GROUPS], F32, name="neg_gate")
-        nc.vector.tensor_scalar(neg_gate[:], gate_turned[:, 0:GROUPS], -1.0, None, ALU.mult)
-
-        window = [[keep.tile([P, T], F32, name=f"window{kt}{which}") for which in (DX, DP)] for kt in range(K // P)]
-        sums, gated, dh_rows, dq, products, staged, dh_t = {}, {}, {}, {}, {}, {}, {}
-
-        def first_product(t, tag="sums"):
+        def first_product(t, tag):
             e = t // PER_EXPERT
-            sums[t] = psum.tile([P, H], F32, name="sums", tag=tag, bufs=1)
+            sums[t] = bank([P, H], "sums", tag)
             for s in range(PASSES):
                 m = e * PASSES + s
                 nc.tensor.matmul_mx(
@@ -202,47 +176,30 @@ def tile_moe_dub_silu_kernel(
                 )
 
         def factor_on_vector(t, after=None):
-            factor[t] = held([P, H], F32, f"factor{t}", after)[:]
+            by_group(factor, t, t + 1, F32, f"factor{t}", after)
             nc.vector.scalar_tensor_tensor(factor[t], silu_neg[t], 1.0, sig[t], ALU.subtract, ALU.mult)
 
-        def dh_on_vector(t, part=None):
-            dh_t[t] = held([P, H], BF16, f"dh_t{t}")[:] if part is None else part
+        def dh_on_vector(t):
             nc.vector.scalar_tensor_tensor(dh_t[t], sums[t][:], neg_gate[:, t : t + 1], factor[t], ALU.mult, ALU.mult)
 
-        def less_one(engine, lo, hi, source, after=None):
-            part = held([P, (hi - lo) * H], F32, f"less_one{lo}", after)
-            if engine == "gpsimd":
-                nc.gpsimd.tensor_scalar(part[:], source, 1.0, -1.0, ALU.mult, ALU.add)
-            else:
-                nc.scalar.activation(part[:], source, ACT.Copy, bias=-1.0)
-            return part
+        def less_one_on_gpsimd(lo, hi, source, after=None):
+            by_group(less_one, lo, hi, F32, f"less_one{lo}", after)
+            nc.gpsimd.tensor_scalar(less_one[lo, hi], source, 1.0, -1.0, ALU.mult, ALU.add)
 
-        def factor_on_gpsimd(lo, hi, less, sigm, after=None):
-            part = held([P, (hi - lo) * H], F32, f"factor{lo}", after)
-            nc.gpsimd.tensor_tensor(part[:], less, sigm, ALU.mult)
-            for t in range(lo, hi):
-                factor[t] = part[:, (t - lo) * H : (t - lo + 1) * H]
-            factor[lo, hi] = part[:]
+        def factor_on_gpsimd(t):
+            nc.gpsimd.tensor_tensor(factor[t], less_one[t], sig[t], ALU.mult)
 
-        def gate_sums(t, tag="sums"):
+        def dh_on_gpsimd(key):
+            nc.gpsimd.tensor_tensor(dh_t[key], gated[key], factor[key], ALU.mult)
+
+        def gate_sums(t, tag):
             first_product(t, tag)
-            e, u = divmod(t, PER_EXPERT)
-            if u == 0:
-                gated["expert", e] = held([P, PER_EXPERT * H], F32, f"gated{e}")
-            gated[t] = gated["expert", e][:, u * H : (u + 1) * H]
+            if t % PER_EXPERT == 0:
+                by_group(gated, t, t + PER_EXPERT, F32, f"gated{t}")
             nc.scalar.activation(gated[t], sums[t][:], ACT.Copy, scale=neg_gate[:, t : t + 1])
 
-        def dh_on_gpsimd(lo, hi, wide, after=None):
-            both = held([P, (hi - lo) * H], BF16, f"dh_t{lo}", after)
-            for t in range(lo, hi):
-                dh_t[t] = both[:, (t - lo) * H : (t - lo + 1) * H]
-                if not wide:
-                    nc.gpsimd.tensor_tensor(dh_t[t], gated[t], factor[t], ALU.mult)
-            if wide:
-                nc.gpsimd.tensor_tensor(both[:], gated["expert", lo // PER_EXPERT][:], factor[lo, hi], ALU.mult)
-
-        def turn_back(lo, hi, tag="back"):
-            back = psum.tile([P, hi - lo, 2, P], F32, name="back", tag=tag, bufs=1)
+        def turn_back_and_quantise(lo, hi, tag):
+            back = bank([P, hi - lo, 2, P], "back", tag)
             for t in range(lo, hi):
                 pairs = dh_t[t].bitcast(F32)
                 for v in range(2):
@@ -252,37 +209,33 @@ def tile_moe_dub_silu_kernel(
                 dh_rows[lo][:].bitcast(F32).rearrange("p (u j v) -> p u j v", u=hi - lo, v=2),
                 back[:].rearrange("p u v j -> p u j v"),
             )
-
-        def quantise(lo, hi):
             codes = held([P, (hi - lo) * P], U32, f"dq_w{lo}")
             scales = held([P, (hi - lo) * P], U8, f"dq_sc{lo}")
             nc.vector.quantize_mx(out=codes[:].bitcast(FP8X4), scales=scales[:], in_=dh_rows[lo][:])
             dq[lo] = (codes, scales)
 
-        def second_products(lo, hi, parts, tag, after=None, part=None):
+        def second_products(lo, hi, parts, tag, after=None):
             e = lo // PER_EXPERT
             codes, scales = dq[lo]
-            bank = psum.tile([P, len(parts), (hi - lo) * P], F32, name="products", tag=tag, bufs=4 if tag == "a_turned" else 1)
+            products = bank([P, len(parts), (hi - lo) * P], "products", tag)
             for n, (kt, which) in enumerate(parts):
-                cols = slice(e * K + kt * P, e * K + (kt + 1) * P)
                 if which == DX:
                     words, plane = second_w[DX, e][:, 2 * kt * P : 2 * (kt + 1) * P].bitcast(FP4X4), w1_sc
                 else:
                     words, plane = second_w[DP, e][:, 4 * kt * P : 4 * (kt + 1) * P].bitcast(FP8X4), wp_sc
                 nc.tensor.matmul_mx(
-                    out=bank[:, n, :],
+                    out=products[:, n, :],
                     lhsT=words,
-                    lhsT_scale=plane[:, cols],
+                    lhsT_scale=plane[:, e * K + kt * P : e * K + (kt + 1) * P],
                     rhs=codes[:].bitcast(FP8X4),
                     rhs_scale=scales[:],
                     start=True,
                     stop=True,
                 )
-            if part is None:
-                part = held([P, len(parts), (hi - lo) * P], F32, f"staged{lo}_{parts[0][0]}{parts[0][1]}", after)
-            nc.scalar.copy(part[:], bank[:])
+            staged = held([P, len(parts), (hi - lo) * P], F32, f"staged{lo}_{parts[0][0]}{parts[0][1]}", after)
+            nc.scalar.copy(staged[:], products[:])
             for n, (kt, which) in enumerate(parts):
-                nc.vector.tensor_copy(window[kt][which][:].indirect(entries(which, lo, hi)), part[:, n, :])
+                nc.vector.tensor_copy(window[kt][which][:].indirect(entries(which, lo, hi)), staged[:, n, :])
 
         def add_and_store(adder, queue, kt, pieces):
             width = T // pieces
@@ -291,68 +244,88 @@ def tile_moe_dub_silu_kernel(
                 adder.tensor_tensor(total[:], window[kt][DX][:, lo : lo + width], window[kt][DP][:, lo : lo + width], ALU.add)
                 queue.dma_start(out=out[kt * P : (kt + 1) * P, lo : lo + width], in_=total[:])
 
-        upper, lower = ((0, DX), (0, DP)), ((1, DX), (1, DP))
-        first_product(0, "bank0")
-        first_product(1, "bank1")
-        factor_on_vector(0)
-        factor_on_vector(1)
-        dh_on_vector(0)
-        dh_on_vector(1)
-        silu(4)
-        silu(5)
-        turn_back(0, 1, "bank0")
-        quantise(0, 1)
-        turn_back(1, 2, "bank1")
-        quantise(1, 2)
-        silu(6)
-        silu(7)
-        first_product(2, "bank2")
-        first_product(3, "bank3")
-        factor_on_gpsimd(2, 3, less_one("gpsimd", 2, 3, silu_neg[2])[:], sig[2])
-        gather_words(4, 8, 1, after="factor1")
+        by_group(sig, 0, HALF, F32, "sig_early")
+        by_group(silu_neg, 0, HALF, F32, "silu_early", after="a_sb1")
+        by_group(silu_neg, HALF, GROUPS, F32, "silu_late")
+        for t in range(HALF):
+            sigmoid(t)
+        gather_words(0, 0)
+        gather_words(0, 1)
+        gather_words(HALF, 0)
+        for t in range(HALF):
+            silu(t)
+        gate_turned = bank([P, P], "gate_turned", "bank3")
+        nc.tensor.transpose(gate_turned[:], gate_rows[:], ident[:])
+        neg_gate = keep.tile([P, GROUPS], F32, name="neg_gate")
+        nc.vector.tensor_scalar(neg_gate[:], gate_turned[:, 0:GROUPS], -1.0, None, ALU.mult)
+        window = [[keep.tile([P, T], F32, name=f"window{kt}{which}") for which in (DX, DP)] for kt in range(K // P)]
+
+        for t in (0, 1):
+            first_product(t, f"bank{t}")
+        for t in (0, 1):
+            factor_on_vector(t)
+        for t in (0, 1):
+            by_group(dh_t, t, t + 1, BF16, f"dh_t{t}")
+            dh_on_vector(t)
+        for t in (4, 5):
+            silu(t)
+        for t in (0, 1):
+            turn_back_and_quantise(t, t + 1, f"bank{t}")
+        for t in (6, 7):
+            silu(t)
+
+        for t in (2, 3):
+            first_product(t, f"bank{t}")
+        less_one_on_gpsimd(2, 3, silu_neg[2])
+        by_group(factor, 2, 3, F32, "factor2")
+        factor_on_gpsimd(2)
+        gather_words(HALF, 1, after="factor1")
         factor_on_vector(3, after="dh_rows0")
-        both = held([P, 2 * H], BF16, "dh_t2")
-        dh_on_vector(2, both[:, 0:H])
-        dh_on_vector(3, both[:, H:])
-        less = less_one("gpsimd", 4, 8, silu_neg[4, 8], after="dh_rows1")
-        second_products(0, 1, upper + lower, "bank0")
-        two_groups(sig, 4, "sig_of_2", after="dq_w0")
+        by_group(dh_t, 2, 4, BF16, "dh_t2")
+        for t in (2, 3):
+            dh_on_vector(t)
+        less_one_on_gpsimd(HALF, GROUPS, silu_neg[HALF, GROUPS], after="dh_rows1")
+
+        second_products(0, 1, UPPER + LOWER, "bank0")
+        by_group(sig, 4, 6, F32, "sig4", after="dq_w0")
         sigmoid(4)
-        turn_back(2, 4, "bank0")
-        quantise(2, 4)
-        second_products(1, 2, upper + lower, "bank1", after="dh_t2")
+        turn_back_and_quantise(2, 4, "bank0")
+        second_products(1, 2, UPPER + LOWER, "bank1", after="dh_t2")
         sigmoid(5)
-        second_products(2, 4, upper, "bank0")
-        factor_of_2 = held([P, 2 * H], F32, "factor_of_2", after="dh_rows2")
-        factor[4, 6] = factor_of_2[:]
-        for u in range(2):
-            nc.gpsimd.tensor_tensor(factor_of_2[:, u * H : (u + 1) * H], less[:, u * H : (u + 1) * H], sig[4 + u], ALU.mult)
+
+        second_products(2, 4, UPPER, "bank0")
+        by_group(factor, 4, 6, F32, "factor4", after="dh_rows2")
+        for t in (4, 5):
+            factor_on_gpsimd(t)
         gate_sums(4, "bank3")
         gate_sums(5, "bank2")
-        second_products(2, 4, lower[:1], "bank1")
-        two_groups(sig, 6, "sig_of_3", after="dq_sc0")
-        sigmoid(6)
-        sigmoid(7)
-        dh_on_gpsimd(4, 6, True)
-        factor_on_gpsimd(6, 7, less[:, 2 * H : 3 * H], sig[6], after="gated2")
-        turn_back(4, 6, "bank1")
-        quantise(4, 6)
-        second_products(2, 4, lower[1:], "bank0", after="dh_t4")
-        second_products(4, 6, upper[:1], "bank1")
-        second_products(4, 6, upper[1:], "a_turned")
+        second_products(2, 4, LOWER[:1], "bank1")
+        by_group(sig, 6, 8, F32, "sig6", after="dq_sc0")
+        for t in (6, 7):
+            sigmoid(t)
+        by_group(dh_t, 4, 6, BF16, "dh_t4")
+        dh_on_gpsimd((4, 6))
+        by_group(factor, 6, 7, F32, "factor6", after="gated4")
+        factor_on_gpsimd(6)
+        turn_back_and_quantise(4, 6, "bank1")
+        second_products(2, 4, LOWER[1:], "bank0", after="dh_t4")
+
+        second_products(4, 6, UPPER[:1], "bank1")
+        second_products(4, 6, UPPER[1:], "a_turned")
         gate_sums(6, "bank3")
         gate_sums(7, "bank2")
-        second_products(4, 6, lower[:1], "a_turned")
+        second_products(4, 6, LOWER[:1], "a_turned")
         last = held([P, 2 * H], F32, "last", after="dh_rows4")
+        factor[7] = last[:, 0:H]
         dh_t[6], dh_t[7] = last[:, H : H + H // 2].bitcast(BF16), last[:, H + H // 2 :].bitcast(BF16)
-        nc.gpsimd.tensor_tensor(dh_t[6], gated[6], factor[6], ALU.mult)
-        nc.gpsimd.tensor_tensor(last[:, 0:H], less[:, 3 * H :], sig[7], ALU.mult)
-        nc.gpsimd.tensor_tensor(dh_t[7], gated[7], last[:, 0:H], ALU.mult)
-        turn_back(6, 8, "bank3")
-        quantise(6, 8)
-        second_products(4, 6, lower[1:], "bank0", after="dh_rows4")
-        second_products(6, 8, upper[:1], "bank1")
-        second_products(6, 8, upper[1:], "a_turned")
+        dh_on_gpsimd(6)
+        factor_on_gpsimd(7)
+        dh_on_gpsimd(7)
+        turn_back_and_quantise(6, 8, "bank3")
+        second_products(4, 6, LOWER[1:], "bank0", after="dh_rows4")
+
+        second_products(6, 8, UPPER[:1], "bank1")
+        second_products(6, 8, UPPER[1:], "a_turned")
         add_and_store(nc.gpsimd, nc.scalar, 0, 2)
-        second_products(6, 8, lower, "bank2")
+        second_products(6, 8, LOWER, "bank2")
         add_and_store(nc.vector, nc.sync, 1, 4)

@@ -28,15 +28,16 @@ MOVED_ROWS = 112
 DX, DP = 0, 1
 HALF = GROUPS // 2
 A_BANKS = 4
+OWN, PARTNER = ((0, DX), (1, DX)), ((0, DP), (1, DP))
 UPPER, LOWER = ((0, DX), (0, DP)), ((1, DX), (1, DP))
 
 
 def load_scale_rows(nc, plane, rows):
     m = rows.shape[0]
-    for q in range(QUADRANTS):
+    for r in range(4):
         nc.sync.dma_start(
-            out=plane[32 * q : 32 * q + 4, :].bitcast(I32).rearrange("b (m w) -> b m w", m=m),
-            in_=rows[:, 4 * q : 4 * q + 4, :].bitcast(I32).rearrange("m b w -> b m w"),
+            out=plane[r:P:32, :].bitcast(I32).rearrange("q (m w) -> q m w", m=m),
+            in_=rows.bitcast(I32)[:, r:16:4, :].rearrange("m q w -> q m w"),
         )
 
 
@@ -49,11 +50,14 @@ def tile_moe_dub_silu_kernel(
         keep = ctx.enter_context(tc.tile_pool(name="keep", bufs=1))
         psum = ctx.enter_context(tc.psum_pool(name="psum", bufs=2))
 
+        tag_of = {}
+
         def held(shape, dtype, name, after=None):
-            return keep.tile(shape, dtype, name=name, tag=after or name, align_bytes=64)
+            tag_of[name] = tag_of[after] if after else name
+            return keep.tile(shape, dtype, name=name, tag=tag_of[name], align_bytes=64)
 
         def bank(shape, name, tag):
-            return psum.tile(shape, F32, name=name, tag=tag, bufs=A_BANKS if tag == "a_turned" else 1)
+            return psum.tile(shape, F32, name=name, tag=tag, bufs=1)
 
         token_list = lists.tile([P, SLOTS // PER_COLUMN], U16, name="token_list")
         partner_list = lists.tile([P, SLOTS // PER_COLUMN], U16, name="partner_list")
@@ -62,15 +66,15 @@ def tile_moe_dub_silu_kernel(
             return (token_list, partner_list)[which][:, lo * P // PER_COLUMN : hi * P // PER_COLUMN]
 
         dy_sc = held([P, T], U8, "dy_sc")
-        w2_sc = held([P, E * PASSES * H], U8, "w2_sc")
+        w2_sc = [held([P, 2 * PASSES * H], U8, f"w2_sc{h}") for h in range(2)]
         w1_sc = held([P, E * K], U8, "w1_sc")
         wp_sc = held([P, E * K], U8, "wp_sc")
-        slot_sc = [held([P, SLOTS], U8, f"slot_sc{s}") for s in range(PASSES)]
-        for plane in (dy_sc, w2_sc, slot_sc[1], w1_sc, wp_sc):
+        slot_sc = [[held([P, HALF * P], U8, f"slot_sc{h}{s}") for s in range(PASSES)] for h in range(2)]
+        for plane in (dy_sc, slot_sc[0][1], w2_sc[0], wp_sc, w1_sc, slot_sc[1][1], w2_sc[1]):
             nc.vector.memset(plane[:].bitcast(I32), 0)
 
         ident = keep.tile([P, P], F32, name="ident")
-        gate_rows = keep.tile([P, P], F32, name="gate_rows")
+        gate_rows = held([P, P], F32, "gate_rows")
         nc.gpsimd.memset(gate_rows[:], 0.0)
         make_identity(nc, ident[:])
 
@@ -78,8 +82,8 @@ def tile_moe_dub_silu_kernel(
         a_sb, w2_w, second_w = {}, {}, {}
 
         def load_a(lo, hi):
-            part = held([P, H // P, (hi - lo) * C], F32, f"a_sb{lo}")
-            nc.sync.dma_start(out=part[:], in_=a[:, lo * C : hi * C].rearrange("(c p) j -> p c j", p=P))
+            part = held([P, 4, (hi - lo) * C], F32, f"a_sb{lo}")
+            nc.sync.dma_start(out=part[:], in_=a[:, lo * C : hi * C].rearrange("(p r) j -> p r j", r=4))
             for e in range(lo, hi):
                 a_sb[e] = part[:, :, (e - lo) * C : (e - lo + 1) * C]
 
@@ -102,6 +106,12 @@ def tile_moe_dub_silu_kernel(
             for e in range(lo, hi):
                 second_w[which, e] = part[:, e - lo, :]
 
+        def move_scale_rows(h):
+            nc.sync.dma_start(
+                out=slot_sc[h][1][0:MOVED_ROWS, :].bitcast(I32), in_=slot_sc[h][0][4 : 4 + MOVED_ROWS, :].bitcast(I32)
+            )
+
+        w2_rows = w2t_scales.rearrange("e s b w -> (e s) b w")
         load_a(0, 1)
         nc.sync.dma_start(token_list[:], offs)
         for q in range(QUADRANTS):
@@ -113,26 +123,27 @@ def tile_moe_dub_silu_kernel(
         nc.sync.dma_start(out=dy_w[0][:], in_=dy_words[0].rearrange("p n t -> p (n t)").bitcast(I32))
         nc.sync.dma_start(out=gate_rows[0:GROUPS, :], in_=gate[0:1, :].rearrange("o (t c) -> (o t) c", c=P))
         nc.sync.dma_start(out=dy_w[1][:], in_=dy_words[1].rearrange("p n t -> p (n t)").bitcast(I32))
-        for lo in (0, HALF):
-            hi = lo + HALF
-            nc.vector.tensor_copy(slot_sc[0][:, lo * P : hi * P], dy_sc[:].indirect(entries(DX, lo, hi)))
+        for h in range(2):
+            nc.vector.tensor_copy(slot_sc[h][0][:], dy_sc[:].indirect(entries(DX, h * HALF, (h + 1) * HALF)))
+        move_scale_rows(0)
         load_w2(0, 1)
-        load_scale_rows(nc, w2_sc, w2t_scales.rearrange("e s b w -> (e s) b w"))
-        nc.sync.dma_start(out=slot_sc[1][0:MOVED_ROWS, :].bitcast(I32), in_=slot_sc[0][4 : 4 + MOVED_ROWS, :].bitcast(I32))
-        load_a(2, 3)
-        load_a(3, 4)
+        load_scale_rows(nc, w2_sc[0], w2_rows[0 : 2 * PASSES])
         load_w2(1, 2)
+        load_a(2, 3)
         load_scale_rows(nc, wp_sc, wpt_scales.rearrange("e s b w -> (e s) b w"))
         load_second(DP, 0, 1)
+        nc.sync.dma_start(partner_list[:], offs2)
+        load_a(3, 4)
         load_scale_rows(nc, w1_sc, w1t_scales.rearrange("e s b w -> (e s) b w"))
         load_second(DX, 0, 1)
-        nc.sync.dma_start(partner_list[:], offs2)
-        load_w2(2, E)
         load_second(DP, 1, E)
         load_second(DX, 1, E)
+        move_scale_rows(1)
+        load_scale_rows(nc, w2_sc[1], w2_rows[2 * PASSES :])
+        load_w2(2, E)
 
-        slot_w, a_turned, sig, silu_neg, less_one, factor = {}, {}, {}, {}, {}, {}
-        sums, gated, dh_t, dh_rows, dq = {}, {}, {}, {}, {}
+        slot_w, sig, silu_neg, less_one, factor = {}, {}, {}, {}, {}
+        sums, gated, turned, turned_sb, dh, dq, products, staged = {}, {}, {}, {}, {}, {}, {}, {}
 
         def by_group(table, lo, hi, dtype, name, after=None):
             part = held([P, (hi - lo) * H], dtype, name, after)
@@ -140,91 +151,96 @@ def tile_moe_dub_silu_kernel(
                 table[t] = part[:, (t - lo) * H : (t - lo + 1) * H]
             table[lo, hi] = part[:]
 
-        def gather_words(lo, s, after=None):
-            part = held([P, HALF * P], U32, f"slot_w{lo}{s}", after)
-            nc.vector.tensor_copy(part[:], dy_w[s][:].bitcast(U32).indirect(entries(DX, lo, lo + HALF)))
-            for t in range(lo, lo + HALF):
+        def gather_words(lo, hi, s, after=None):
+            part = held([P, (hi - lo) * P], U32, f"slot_w{lo}{s}", after)
+            nc.vector.tensor_copy(part[:], dy_w[s][:].bitcast(U32).indirect(entries(DX, lo, hi)))
+            for t in range(lo, hi):
                 slot_w[t, s] = part[:, (t - lo) * P : (t - lo + 1) * P]
 
-        def activate(t, func, scale, result):
-            if t not in a_turned:
-                e, u = divmod(t, PER_EXPERT)
-                a_turned[t] = bank([P, H], "a_turned", "a_turned")
-                for c in range(H // P):
-                    nc.tensor.transpose(a_turned[t][:, c * P : (c + 1) * P], a_sb[e][:, c, u * P : (u + 1) * P], ident[:])
-            nc.scalar.activation(result, a_turned[t][:], func, scale=scale)
+        def activate(lo, hi, func, scale, table):
+            e, u = divmod(lo, PER_EXPERT)
+            source = a_sb[e][:, :, u * P : (u + hi - lo) * P]
+            result = table[lo] if hi - lo == 1 else table[lo, hi]
+            nc.scalar.activation(
+                result.rearrange("p (c j r) -> p c r j", j=4, r=4),
+                source.rearrange("p r (c j) -> p c r j", j=4),
+                func,
+                scale=scale,
+            )
 
-        def sigmoid(t):
-            activate(t, ACT.Sigmoid, 1.0, sig[t])
+        def sigmoid(lo, hi):
+            activate(lo, hi, ACT.Sigmoid, 1.0, sig)
 
-        def silu(t):
-            activate(t, ACT.Silu, -1.0, silu_neg[t])
+        def silu(lo, hi):
+            activate(lo, hi, ACT.Silu, -1.0, silu_neg)
 
         def first_product(t, tag):
             e = t // PER_EXPERT
             sums[t] = bank([P, H], "sums", tag)
             for s in range(PASSES):
-                m = e * PASSES + s
+                m = e % 2 * PASSES + s
                 nc.tensor.matmul_mx(
                     out=sums[t][:],
                     lhsT=slot_w[t, s].bitcast(FP8X4),
-                    lhsT_scale=slot_sc[s][:, t * P : (t + 1) * P],
+                    lhsT_scale=slot_sc[t // HALF][s][:, t % HALF * P : (t % HALF + 1) * P],
                     rhs=w2_w[e][:, s, :].bitcast(FP4X4),
-                    rhs_scale=w2_sc[:, m * H : (m + 1) * H],
+                    rhs_scale=w2_sc[t // HALF][:, m * H : (m + 1) * H],
                     start=(s == 0),
                     stop=(s == PASSES - 1),
                 )
+
+        def gate_sums(t, after=None):
+            gated[t] = held([P, 4, P], F32, f"gated{t}", after)
+            nc.scalar.activation(gated[t][:], sums[t][:].rearrange("j (p r) -> j r p", r=4), ACT.Copy, scale=neg_gate[:, t : t + 1])
+
+        def turn(t, tag):
+            turned[t] = bank([P, 4, P], "turned", tag)
+            for r in range(4):
+                nc.tensor.transpose(turned[t][:, r, :], gated[t][:, r, :], ident[:])
 
         def factor_on_vector(t, after=None):
             by_group(factor, t, t + 1, F32, f"factor{t}", after)
             nc.vector.scalar_tensor_tensor(factor[t], silu_neg[t], 1.0, sig[t], ALU.subtract, ALU.mult)
 
         def dh_on_vector(t):
-            nc.vector.scalar_tensor_tensor(dh_t[t], sums[t][:], neg_gate[:, t : t + 1], factor[t], ALU.mult, ALU.mult)
+            nc.vector.tensor_tensor(
+                dh[t].rearrange("p (j r) -> p j r", r=4),
+                turned[t][:].rearrange("p r j -> p j r"),
+                factor[t].rearrange("p (j r) -> p j r", r=4),
+                ALU.mult,
+            )
 
-        def less_one_on_gpsimd(lo, hi, source, after=None):
+        def less_one_on_gpsimd(lo, hi, after=None):
             by_group(less_one, lo, hi, F32, f"less_one{lo}", after)
-            nc.gpsimd.tensor_scalar(less_one[lo, hi], source, 1.0, -1.0, ALU.mult, ALU.add)
+            nc.gpsimd.tensor_scalar(less_one[lo, hi], silu_neg[lo] if hi - lo == 1 else silu_neg[lo, hi], 1.0, -1.0, ALU.mult, ALU.add)
 
         def factor_on_gpsimd(t):
             nc.gpsimd.tensor_tensor(factor[t], less_one[t], sig[t], ALU.mult)
 
-        def dh_on_gpsimd(key):
-            nc.gpsimd.tensor_tensor(dh_t[key], gated[key], factor[key], ALU.mult)
+        def hand_over(t):
+            by_group(turned_sb, t, t + 1, F32, f"turned_sb{t}")
+            nc.scalar.copy(turned_sb[t].rearrange("p (j r) -> p j r", r=4), turned[t][:].rearrange("p r j -> p j r"))
 
-        def gate_sums(t, tag):
-            first_product(t, tag)
-            if t % PER_EXPERT == 0:
-                by_group(gated, t, t + PER_EXPERT, F32, f"gated{t}")
-            nc.scalar.activation(gated[t], sums[t][:], ACT.Copy, scale=neg_gate[:, t : t + 1])
+        def dh_on_gpsimd(t):
+            nc.gpsimd.tensor_tensor(dh[t], turned_sb[t], factor[t], ALU.mult)
 
-        def turn_back_and_quantise(lo, hi, tag):
-            back = bank([P, hi - lo, 2, P], "back", tag)
-            for t in range(lo, hi):
-                pairs = dh_t[t].bitcast(F32)
-                for v in range(2):
-                    nc.tensor.transpose(back[:, t - lo, v, :], pairs[:, v : H // 2 : 2], ident[:])
-            dh_rows[lo] = held([P, (hi - lo) * H], BF16, f"dh_rows{lo}")
-            nc.scalar.copy(
-                dh_rows[lo][:].bitcast(F32).rearrange("p (u j v) -> p u j v", u=hi - lo, v=2),
-                back[:].rearrange("p u v j -> p u j v"),
-            )
-            codes = held([P, (hi - lo) * P], U32, f"dq_w{lo}")
+        def quantise(lo, hi, after=None):
+            codes = held([P, (hi - lo) * P], U32, f"dq_w{lo}", after)
             scales = held([P, (hi - lo) * P], U8, f"dq_sc{lo}")
-            nc.vector.quantize_mx(out=codes[:].bitcast(FP8X4), scales=scales[:], in_=dh_rows[lo][:])
+            nc.vector.quantize_mx(out=codes[:].bitcast(FP8X4), scales=scales[:], in_=dh[lo, hi])
             dq[lo] = (codes, scales)
 
-        def second_products(lo, hi, parts, tag, after=None):
+        def second_products(lo, hi, parts, tag):
             e = lo // PER_EXPERT
             codes, scales = dq[lo]
-            products = bank([P, len(parts), (hi - lo) * P], "products", tag)
+            products[lo, parts] = bank([P, len(parts), (hi - lo) * P], "products", tag)
             for n, (kt, which) in enumerate(parts):
                 if which == DX:
                     words, plane = second_w[DX, e][:, 2 * kt * P : 2 * (kt + 1) * P].bitcast(FP4X4), w1_sc
                 else:
                     words, plane = second_w[DP, e][:, 4 * kt * P : 4 * (kt + 1) * P].bitcast(FP8X4), wp_sc
                 nc.tensor.matmul_mx(
-                    out=products[:, n, :],
+                    out=products[lo, parts][:, n, :],
                     lhsT=words,
                     lhsT_scale=plane[:, e * K + kt * P : e * K + (kt + 1) * P],
                     rhs=codes[:].bitcast(FP8X4),
@@ -232,10 +248,23 @@ def tile_moe_dub_silu_kernel(
                     start=True,
                     stop=True,
                 )
-            staged = held([P, len(parts), (hi - lo) * P], F32, f"staged{lo}_{parts[0][0]}{parts[0][1]}", after)
-            nc.scalar.copy(staged[:], products[:])
+
+        def stage(lo, hi, parts, after=None):
+            staged[lo, parts] = held([P, len(parts), (hi - lo) * P], F32, f"staged{lo}_{parts[0][0]}{parts[0][1]}", after)
+            nc.scalar.copy(staged[lo, parts][:], products[lo, parts][:])
+
+        def scatter(lo, hi, parts):
             for n, (kt, which) in enumerate(parts):
-                nc.vector.tensor_copy(window[kt][which][:].indirect(entries(which, lo, hi)), staged[:, n, :])
+                nc.vector.tensor_copy(window[kt][which][:].indirect(entries(which, lo, hi)), staged[lo, parts][:, n, :])
+
+        def send(lo, hi, parts, tag, after=None):
+            second_products(lo, hi, parts, tag)
+            stage(lo, hi, parts, after)
+            scatter(lo, hi, parts)
+
+        def send_on(lo, hi, parts, after=None):
+            stage(lo, hi, parts, after)
+            scatter(lo, hi, parts)
 
         def add_and_store(adder, queue, kt, pieces):
             width = T // pieces
@@ -244,88 +273,117 @@ def tile_moe_dub_silu_kernel(
                 adder.tensor_tensor(total[:], window[kt][DX][:, lo : lo + width], window[kt][DP][:, lo : lo + width], ALU.add)
                 queue.dma_start(out=out[kt * P : (kt + 1) * P, lo : lo + width], in_=total[:])
 
-        by_group(sig, 0, HALF, F32, "sig_early")
-        by_group(silu_neg, 0, HALF, F32, "silu_early", after="a_sb1")
-        by_group(silu_neg, HALF, GROUPS, F32, "silu_late")
-        for t in range(HALF):
-            sigmoid(t)
-        gather_words(0, 0)
-        gather_words(0, 1)
-        gather_words(HALF, 0)
-        for t in range(HALF):
-            silu(t)
-        gate_turned = bank([P, P], "gate_turned", "bank3")
+        by_group(sig, 0, 2, F32, "sig0")
+        by_group(sig, 2, 4, F32, "sig2")
+        sigmoid(0, 2)
+        sigmoid(2, 4)
+        gather_words(0, HALF, 0)
+        gather_words(0, 1, 1)
+        gather_words(1, HALF, 1)
+        gate_turned = bank([P, P], "gate_turned", "bank2")
         nc.tensor.transpose(gate_turned[:], gate_rows[:], ident[:])
         neg_gate = keep.tile([P, GROUPS], F32, name="neg_gate")
         nc.vector.tensor_scalar(neg_gate[:], gate_turned[:, 0:GROUPS], -1.0, None, ALU.mult)
+        gather_words(HALF, GROUPS, 0)
+        by_group(silu_neg, 0, 3, F32, "silu0", after="gate_rows")
+        for t in range(3):
+            silu(t, t + 1)
         window = [[keep.tile([P, T], F32, name=f"window{kt}{which}") for which in (DX, DP)] for kt in range(K // P)]
 
         for t in (0, 1):
-            first_product(t, f"bank{t}")
-        for t in (0, 1):
             factor_on_vector(t)
-        for t in (0, 1):
-            by_group(dh_t, t, t + 1, BF16, f"dh_t{t}")
-            dh_on_vector(t)
-        for t in (4, 5):
-            silu(t)
-        for t in (0, 1):
-            turn_back_and_quantise(t, t + 1, f"bank{t}")
-        for t in (6, 7):
-            silu(t)
-
-        for t in (2, 3):
-            first_product(t, f"bank{t}")
-        less_one_on_gpsimd(2, 3, silu_neg[2])
+        less_one_on_gpsimd(2, 3)
         by_group(factor, 2, 3, F32, "factor2")
         factor_on_gpsimd(2)
-        gather_words(HALF, 1, after="factor1")
-        factor_on_vector(3, after="dh_rows0")
-        by_group(dh_t, 2, 4, BF16, "dh_t2")
-        for t in (2, 3):
-            dh_on_vector(t)
-        less_one_on_gpsimd(HALF, GROUPS, silu_neg[HALF, GROUPS], after="dh_rows1")
+        first_product(0, "bank0")
+        first_product(1, "bank1")
+        gate_sums(0)
+        by_group(silu_neg, 3, 4, F32, "silu3", after="slot_w01")
+        silu(3, 4)
+        turn(0, "bank2")
+        first_product(2, "bank0")
+        gate_sums(1)
+        turn(1, "bank3")
+        first_product(3, "bank1")
+        gather_words(HALF, GROUPS, 1, after="a_sb0")
+        by_group(dh, 0, 1, BF16, "dh0")
+        dh_on_vector(0)
+        quantise(0, 1)
+        by_group(dh, 1, 2, BF16, "dh1")
+        dh_on_vector(1)
+        quantise(1, 2)
+        by_group(silu_neg, 4, 6, F32, "silu4")
+        silu(4, 6)
+        gate_sums(2)
+        send(0, 1, PARTNER[:1], "bank4")
+        send(0, 1, PARTNER[1:], "bank5")
+        second_products(1, 2, PARTNER, "bank6")
+        turn(2, "bank4")
+        by_group(dh, 2, 4, BF16, "dh2")
+        dh_on_vector(2)
+        send_on(1, 2, PARTNER)
+        less_one_on_gpsimd(3, 4, after="dh1")
+        by_group(factor, 3, 4, F32, "factor3")
+        factor_on_gpsimd(3)
+        less_one_on_gpsimd(4, 6, after="less_one3")
+        gate_sums(3, after="staged0_01")
+        turn(3, "bank5")
+        by_group(silu_neg, 6, 8, F32, "silu6")
+        silu(6, 8)
+        less_one_on_gpsimd(6, 8)
+        dh_on_vector(3)
+        quantise(2, 4)
+        send(0, 1, OWN, "bank7")
+        send(1, 2, OWN, "bank2")
+        by_group(sig, 4, 6, F32, "sig4", after="dq_w1")
+        sigmoid(4, 5)
+        sigmoid(5, 6)
 
-        second_products(0, 1, UPPER + LOWER, "bank0")
-        by_group(sig, 4, 6, F32, "sig4", after="dq_w0")
-        sigmoid(4)
-        turn_back_and_quantise(2, 4, "bank0")
-        second_products(1, 2, UPPER + LOWER, "bank1", after="dh_t2")
-        sigmoid(5)
-
-        second_products(2, 4, UPPER, "bank0")
-        by_group(factor, 4, 6, F32, "factor4", after="dh_rows2")
+        for t in (4, 5):
+            first_product(t, f"bank{t - 4}")
+        by_group(factor, 4, 6, F32, "factor4", after="dh2")
         for t in (4, 5):
             factor_on_gpsimd(t)
-        gate_sums(4, "bank3")
-        gate_sums(5, "bank2")
-        second_products(2, 4, LOWER[:1], "bank1")
-        by_group(sig, 6, 8, F32, "sig6", after="dq_sc0")
+        gate_sums(4)
+        send(2, 4, PARTNER[:1], "bank6")
+        turn(4, "bank2")
+        gate_sums(5)
+        send(2, 4, PARTNER[1:], "bank7")
+        turn(5, "bank3")
+        hand_over(4)
+        hand_over(5)
+        send(2, 4, OWN[:1], "bank4")
+        by_group(sig, 6, 8, F32, "sig6", after="gated5")
+        sigmoid(6, 8)
+        by_group(dh, 4, 6, BF16, "dh4")
+        for t in (4, 5):
+            dh_on_gpsimd(t)
         for t in (6, 7):
-            sigmoid(t)
-        by_group(dh_t, 4, 6, BF16, "dh_t4")
-        dh_on_gpsimd((4, 6))
-        by_group(factor, 6, 7, F32, "factor6", after="gated4")
-        factor_on_gpsimd(6)
-        turn_back_and_quantise(4, 6, "bank1")
-        second_products(2, 4, LOWER[1:], "bank0", after="dh_t4")
+            first_product(t, f"bank{t - 6}")
+        for t in (6, 7):
+            gate_sums(t)
+            turn(t, f"bank{t - 4}")
+        for t in (6, 7):
+            hand_over(t)
+        quantise(4, 6)
+        send(2, 4, OWN[1:], "bank5", after="turned_sb5")
 
-        second_products(4, 6, UPPER[:1], "bank1")
-        second_products(4, 6, UPPER[1:], "a_turned")
-        gate_sums(6, "bank3")
-        gate_sums(7, "bank2")
-        second_products(4, 6, LOWER[:1], "a_turned")
-        last = held([P, 2 * H], F32, "last", after="dh_rows4")
-        factor[7] = last[:, 0:H]
-        dh_t[6], dh_t[7] = last[:, H : H + H // 2].bitcast(BF16), last[:, H + H // 2 :].bitcast(BF16)
-        dh_on_gpsimd(6)
-        factor_on_gpsimd(7)
-        dh_on_gpsimd(7)
-        turn_back_and_quantise(6, 8, "bank3")
-        second_products(4, 6, LOWER[1:], "bank0", after="dh_rows4")
+        send(4, 6, UPPER[:1], "bank6")
+        send(4, 6, UPPER[1:], "bank7")
+        send(4, 6, LOWER[:1], "bank4")
+        by_group(factor, 6, 8, F32, "factor6", after="dh4")
+        for t in (6, 7):
+            factor_on_gpsimd(t)
+        by_group(dh, 6, 8, BF16, "dh6")
+        for t in (6, 7):
+            dh_on_gpsimd(t)
+        quantise(6, 8)
+        send(4, 6, LOWER[1:], "bank5", after="turned_sb7")
 
-        second_products(6, 8, UPPER[:1], "bank1")
-        second_products(6, 8, UPPER[1:], "a_turned")
+        send(6, 8, UPPER[:1], "bank6")
+        send(6, 8, UPPER[1:], "bank7")
+        second_products(6, 8, LOWER, "bank4")
+        stage(6, 8, LOWER)
         add_and_store(nc.gpsimd, nc.scalar, 0, 2)
-        second_products(6, 8, LOWER, "bank2")
+        scatter(6, 8, LOWER)
         add_and_store(nc.vector, nc.sync, 1, 4)

@@ -25,6 +25,7 @@ PER_EXPERT = C // P
 PER_COLUMN = 16
 QUADRANTS = 4
 MOVED_ROWS = 112
+EARLY = 2
 DX, DP = 0, 1
 HALF = GROUPS // 2
 A_BANKS = 4
@@ -83,7 +84,8 @@ def tile_moe_dub_silu_kernel(
 
         def load_a(lo, hi):
             part = held([P, 4, (hi - lo) * C], F32, f"a_sb{lo}")
-            nc.sync.dma_start(out=part[:], in_=a[:, lo * C : hi * C].rearrange("(p r) j -> p r j", r=4))
+            pattern = "(c p) j -> p c j" if lo < EARLY else "(p c) j -> p c j"
+            nc.sync.dma_start(out=part[:], in_=a[:, lo * C : hi * C].rearrange(pattern, c=4))
             for e in range(lo, hi):
                 a_sb[e] = part[:, :, (e - lo) * C : (e - lo + 1) * C]
 
@@ -128,21 +130,21 @@ def tile_moe_dub_silu_kernel(
         move_scale_rows(0)
         load_w2(0, 1)
         load_scale_rows(nc, w2_sc[0], w2_rows[0 : 2 * PASSES])
-        load_w2(1, 2)
         load_a(2, 3)
+        load_w2(1, 2)
         load_scale_rows(nc, wp_sc, wpt_scales.rearrange("e s b w -> (e s) b w"))
-        load_second(DP, 0, 1)
         nc.sync.dma_start(partner_list[:], offs2)
+        load_second(DP, 0, 1)
         load_a(3, 4)
         load_scale_rows(nc, w1_sc, w1t_scales.rearrange("e s b w -> (e s) b w"))
         load_second(DX, 0, 1)
-        load_second(DP, 1, E)
-        load_second(DX, 1, E)
         move_scale_rows(1)
         load_scale_rows(nc, w2_sc[1], w2_rows[2 * PASSES :])
         load_w2(2, E)
+        load_second(DP, 1, E)
+        load_second(DX, 1, E)
 
-        slot_w, sig, silu_neg, less_one, factor = {}, {}, {}, {}, {}
+        slot_w, sig, silu_neg, less_one, factor, a_turned, dh_t, back = {}, {}, {}, {}, {}, {}, {}, {}
         sums, gated, turned, turned_sb, dh, dq, products, staged = {}, {}, {}, {}, {}, {}, {}, {}
 
         def by_group(table, lo, hi, dtype, name, after=None):
@@ -157,16 +159,24 @@ def tile_moe_dub_silu_kernel(
             for t in range(lo, hi):
                 slot_w[t, s] = part[:, (t - lo) * P : (t - lo + 1) * P]
 
+        def turn_a(t):
+            e, u = divmod(t, PER_EXPERT)
+            a_turned[t] = bank([P, H], "a_turned", f"bank{4 + t}")
+            for c in range(H // P):
+                nc.tensor.transpose(a_turned[t][:, c * P : (c + 1) * P], a_sb[e][:, c, u * P : (u + 1) * P], ident[:])
+
         def activate(lo, hi, func, scale, table):
             e, u = divmod(lo, PER_EXPERT)
-            source = a_sb[e][:, :, u * P : (u + hi - lo) * P]
-            result = table[lo] if hi - lo == 1 else table[lo, hi]
-            nc.scalar.activation(
-                result.rearrange("p (c j r) -> p c r j", j=4, r=4),
-                source.rearrange("p r (c j) -> p c r j", j=4),
-                func,
-                scale=scale,
-            )
+            if e < EARLY:
+                nc.scalar.activation(table[lo], a_turned[lo][:], func, scale=scale)
+            else:
+                result = table[lo] if hi - lo == 1 else table[lo, hi]
+                nc.scalar.activation(
+                    result.rearrange("p (u r j) -> p u r j", r=4, j=P),
+                    a_sb[e][:, :, u * P : (u + hi - lo) * P].rearrange("p r (u j) -> p u r j", j=P),
+                    func,
+                    scale=scale,
+                )
 
         def sigmoid(lo, hi):
             activate(lo, hi, ACT.Sigmoid, 1.0, sig)
@@ -203,16 +213,29 @@ def tile_moe_dub_silu_kernel(
             nc.vector.scalar_tensor_tensor(factor[t], silu_neg[t], 1.0, sig[t], ALU.subtract, ALU.mult)
 
         def dh_on_vector(t):
-            nc.vector.tensor_tensor(
-                dh[t].rearrange("p (j r) -> p j r", r=4),
-                turned[t][:].rearrange("p r j -> p j r"),
-                factor[t].rearrange("p (j r) -> p j r", r=4),
-                ALU.mult,
+            nc.vector.scalar_tensor_tensor(dh_t[t], sums[t][:], neg_gate[:, t : t + 1], factor[t], ALU.mult, ALU.mult)
+
+        def turn_back(lo, hi, tag):
+            back[lo] = bank([P, hi - lo, 2, P], "back", tag)
+            for t in range(lo, hi):
+                pairs = dh_t[t].bitcast(F32)
+                for v in range(2):
+                    nc.tensor.transpose(back[lo][:, t - lo, v, :], pairs[:, v : H // 2 : 2], ident[:])
+
+        def copy_back(lo, hi, after=None):
+            by_group(dh, lo, hi, BF16, f"dh{lo}", after)
+            nc.scalar.copy(
+                dh[lo, hi].bitcast(F32).rearrange("p (u j v) -> p u j v", u=hi - lo, v=2),
+                back[lo][:].rearrange("p u v j -> p u j v"),
             )
 
         def less_one_on_gpsimd(lo, hi, after=None):
             by_group(less_one, lo, hi, F32, f"less_one{lo}", after)
             nc.gpsimd.tensor_scalar(less_one[lo, hi], silu_neg[lo] if hi - lo == 1 else silu_neg[lo, hi], 1.0, -1.0, ALU.mult, ALU.add)
+
+        def less_one_on_scalar(t, after=None):
+            by_group(less_one, t, t + 1, F32, f"less_one{t}", after)
+            nc.scalar.activation(less_one[t], silu_neg[t], ACT.Copy, bias=-1.0)
 
         def factor_on_gpsimd(t):
             nc.gpsimd.tensor_tensor(factor[t], less_one[t], sig[t], ALU.mult)
@@ -222,7 +245,12 @@ def tile_moe_dub_silu_kernel(
             nc.scalar.copy(turned_sb[t].rearrange("p (j r) -> p j r", r=4), turned[t][:].rearrange("p r j -> p j r"))
 
         def dh_on_gpsimd(t):
-            nc.gpsimd.tensor_tensor(dh[t], turned_sb[t], factor[t], ALU.mult)
+            nc.gpsimd.tensor_tensor(
+                dh[t].rearrange("p (j r) -> p j r", r=4),
+                turned_sb[t].rearrange("p (j r) -> p j r", r=4),
+                factor[t].rearrange("p (r j) -> p j r", r=4),
+                ALU.mult,
+            )
 
         def quantise(lo, hi, after=None):
             codes = held([P, (hi - lo) * P], U32, f"dq_w{lo}", after)
@@ -273,10 +301,11 @@ def tile_moe_dub_silu_kernel(
                 adder.tensor_tensor(total[:], window[kt][DX][:, lo : lo + width], window[kt][DP][:, lo : lo + width], ALU.add)
                 queue.dma_start(out=out[kt * P : (kt + 1) * P, lo : lo + width], in_=total[:])
 
-        by_group(sig, 0, 2, F32, "sig0")
-        by_group(sig, 2, 4, F32, "sig2")
-        sigmoid(0, 2)
-        sigmoid(2, 4)
+        by_group(sig, 0, 1, F32, "sig0")
+        by_group(sig, 1, 4, F32, "sig1")
+        for t in range(HALF):
+            turn_a(t)
+            sigmoid(t, t + 1)
         gather_words(0, HALF, 0)
         gather_words(0, 1, 1)
         gather_words(1, HALF, 1)
@@ -285,58 +314,55 @@ def tile_moe_dub_silu_kernel(
         neg_gate = keep.tile([P, GROUPS], F32, name="neg_gate")
         nc.vector.tensor_scalar(neg_gate[:], gate_turned[:, 0:GROUPS], -1.0, None, ALU.mult)
         gather_words(HALF, GROUPS, 0)
-        by_group(silu_neg, 0, 3, F32, "silu0", after="gate_rows")
-        for t in range(3):
+        by_group(silu_neg, 0, 3, F32, "silu0", after="a_sb1")
+        by_group(silu_neg, 3, 4, F32, "silu3")
+        for t in range(HALF):
             silu(t, t + 1)
         window = [[keep.tile([P, T], F32, name=f"window{kt}{which}") for which in (DX, DP)] for kt in range(K // P)]
 
-        for t in (0, 1):
-            factor_on_vector(t)
-        less_one_on_gpsimd(2, 3)
-        by_group(factor, 2, 3, F32, "factor2")
-        factor_on_gpsimd(2)
         first_product(0, "bank0")
         first_product(1, "bank1")
-        gate_sums(0)
-        by_group(silu_neg, 3, 4, F32, "silu3", after="slot_w01")
-        silu(3, 4)
-        turn(0, "bank2")
-        first_product(2, "bank0")
-        gate_sums(1)
-        turn(1, "bank3")
-        first_product(3, "bank1")
-        gather_words(HALF, GROUPS, 1, after="a_sb0")
-        by_group(dh, 0, 1, BF16, "dh0")
-        dh_on_vector(0)
-        quantise(0, 1)
-        by_group(dh, 1, 2, BF16, "dh1")
-        dh_on_vector(1)
-        quantise(1, 2)
+        for t in (0, 1):
+            factor_on_vector(t)
+        for t in (0, 1):
+            by_group(dh_t, t, t + 1, BF16, f"dh_t{t}")
+            dh_on_vector(t)
+        gather_words(HALF, GROUPS, 1, after="factor0")
+        less_one_on_gpsimd(2, 3, after="sig0")
+        by_group(factor, 2, 3, F32, "factor2")
+        factor_on_gpsimd(2)
         by_group(silu_neg, 4, 6, F32, "silu4")
         silu(4, 6)
-        gate_sums(2)
+        turn_back(0, 1, "bank2")
+        first_product(2, "bank0")
+        turn_back(1, 2, "bank3")
+        copy_back(0, 1)
+        quantise(0, 1)
+        less_one_on_scalar(3, after="dh_t0")
+        by_group(dh_t, 2, 4, BF16, "dh_t2", after="silu3")
+        dh_on_vector(2)
+        copy_back(1, 2)
+        quantise(1, 2)
         send(0, 1, PARTNER[:1], "bank4")
         send(0, 1, PARTNER[1:], "bank5")
         second_products(1, 2, PARTNER, "bank6")
-        turn(2, "bank4")
-        by_group(dh, 2, 4, BF16, "dh2")
-        dh_on_vector(2)
-        send_on(1, 2, PARTNER)
-        less_one_on_gpsimd(3, 4, after="dh1")
-        by_group(factor, 3, 4, F32, "factor3")
+        first_product(3, "bank4")
+        by_group(factor, 3, 4, F32, "factor3", after="dh1")
         factor_on_gpsimd(3)
         less_one_on_gpsimd(4, 6, after="less_one3")
-        gate_sums(3, after="staged0_01")
-        turn(3, "bank5")
+        dh_on_vector(3)
         by_group(silu_neg, 6, 8, F32, "silu6")
         silu(6, 8)
+        send_on(1, 2, PARTNER, after="slot_w11")
         less_one_on_gpsimd(6, 8)
-        dh_on_vector(3)
-        quantise(2, 4)
         send(0, 1, OWN, "bank7")
-        send(1, 2, OWN, "bank2")
-        by_group(sig, 4, 6, F32, "sig4", after="dq_w1")
+        second_products(1, 2, OWN, "bank5")
+        by_group(sig, 4, 6, F32, "sig4", after="dq_w0")
         sigmoid(4, 5)
+        turn_back(2, 4, "bank7")
+        copy_back(2, 4)
+        quantise(2, 4)
+        send_on(1, 2, OWN, after="dh_t2")
         sigmoid(5, 6)
 
         for t in (4, 5):

@@ -28,7 +28,6 @@ MOVED_ROWS = 112
 EARLY = 2
 DX, DP = 0, 1
 HALF = GROUPS // 2
-A_BANKS = 4
 OWN, PARTNER = ((0, DX), (1, DX)), ((0, DP), (1, DP))
 UPPER, LOWER = ((0, DX), (0, DP)), ((1, DX), (1, DP))
 
@@ -181,6 +180,12 @@ def tile_moe_dub_silu_kernel(
         def sigmoid(lo, hi):
             activate(lo, hi, ACT.Sigmoid, 1.0, sig)
 
+        def sigmoid_rows(t, lo, hi):
+            e, u = divmod(t, PER_EXPERT)
+            nc.scalar.activation(
+                sig[t].rearrange("p (r j) -> p r j", r=4)[:, lo:hi, :], a_sb[e][:, lo:hi, u * P : (u + 1) * P], ACT.Sigmoid
+            )
+
         def silu(lo, hi):
             activate(lo, hi, ACT.Silu, -1.0, silu_neg)
 
@@ -199,8 +204,8 @@ def tile_moe_dub_silu_kernel(
                     stop=(s == PASSES - 1),
                 )
 
-        def gate_sums(t, after=None):
-            gated[t] = held([P, 4, P], F32, f"gated{t}", after)
+        def gate_sums(t):
+            gated[t] = held([P, 4, P], F32, f"gated{t}")
             nc.scalar.activation(gated[t][:], sums[t][:].rearrange("j (p r) -> j r p", r=4), ACT.Copy, scale=neg_gate[:, t : t + 1])
 
         def turn(t, tag):
@@ -208,8 +213,8 @@ def tile_moe_dub_silu_kernel(
             for r in range(4):
                 nc.tensor.transpose(turned[t][:, r, :], gated[t][:, r, :], ident[:])
 
-        def factor_on_vector(t, after=None):
-            by_group(factor, t, t + 1, F32, f"factor{t}", after)
+        def factor_on_vector(t):
+            by_group(factor, t, t + 1, F32, f"factor{t}")
             nc.vector.scalar_tensor_tensor(factor[t], silu_neg[t], 1.0, sig[t], ALU.subtract, ALU.mult)
 
         def dh_on_vector(t):
@@ -222,8 +227,8 @@ def tile_moe_dub_silu_kernel(
                 for v in range(2):
                     nc.tensor.transpose(back[lo][:, t - lo, v, :], pairs[:, v : H // 2 : 2], ident[:])
 
-        def copy_back(lo, hi, after=None):
-            by_group(dh, lo, hi, BF16, f"dh{lo}", after)
+        def copy_back(lo, hi):
+            by_group(dh, lo, hi, BF16, f"dh{lo}")
             nc.scalar.copy(
                 dh[lo, hi].bitcast(F32).rearrange("p (u j v) -> p u j v", u=hi - lo, v=2),
                 back[lo][:].rearrange("p u v j -> p u j v"),
@@ -252,8 +257,8 @@ def tile_moe_dub_silu_kernel(
                 ALU.mult,
             )
 
-        def quantise(lo, hi, after=None):
-            codes = held([P, (hi - lo) * P], U32, f"dq_w{lo}", after)
+        def quantise(lo, hi):
+            codes = held([P, (hi - lo) * P], U32, f"dq_w{lo}")
             scales = held([P, (hi - lo) * P], U8, f"dq_sc{lo}")
             nc.vector.quantize_mx(out=codes[:].bitcast(FP8X4), scales=scales[:], in_=dh[lo, hi])
             dq[lo] = (codes, scales)
@@ -271,6 +276,21 @@ def tile_moe_dub_silu_kernel(
                     out=products[lo, parts][:, n, :],
                     lhsT=words,
                     lhsT_scale=plane[:, e * K + kt * P : e * K + (kt + 1) * P],
+                    rhs=codes[:].bitcast(FP8X4),
+                    rhs_scale=scales[:],
+                    start=True,
+                    stop=True,
+                )
+
+        def joined_products(parts, tag):
+            kt = parts[0][0]
+            products[0, parts] = bank([P, 1, C], "products", tag)
+            for t in range(PER_EXPERT):
+                codes, scales = dq[t]
+                nc.tensor.matmul_mx(
+                    out=products[0, parts][:, 0, t * P : (t + 1) * P],
+                    lhsT=second_w[DX, 0][:, 2 * kt * P : 2 * (kt + 1) * P].bitcast(FP4X4),
+                    lhsT_scale=w1_sc[:, kt * P : (kt + 1) * P],
                     rhs=codes[:].bitcast(FP8X4),
                     rhs_scale=scales[:],
                     start=True,
@@ -345,7 +365,8 @@ def tile_moe_dub_silu_kernel(
         quantise(1, 2)
         send(0, 1, PARTNER[:1], "bank4")
         send(0, 1, PARTNER[1:], "bank5")
-        second_products(1, 2, PARTNER, "bank6")
+        send(1, 2, PARTNER[:1], "bank6")
+        second_products(1, 2, PARTNER[1:], "bank1")
         first_product(3, "bank4")
         by_group(factor, 3, 4, F32, "factor3", after="dh1")
         factor_on_gpsimd(3)
@@ -353,16 +374,18 @@ def tile_moe_dub_silu_kernel(
         dh_on_vector(3)
         by_group(silu_neg, 6, 8, F32, "silu6")
         silu(6, 8)
-        send_on(1, 2, PARTNER, after="slot_w11")
+        send_on(1, 2, PARTNER[1:], after="slot_w11")
         less_one_on_gpsimd(6, 8)
-        send(0, 1, OWN, "bank7")
-        second_products(1, 2, OWN, "bank5")
+        for part, tag in ((OWN[:1], "bank7"), (OWN[1:], "bank5")):
+            joined_products(part, tag)
+        send_on(0, 2, OWN[:1])
         by_group(sig, 4, 6, F32, "sig4", after="dq_w0")
-        sigmoid(4, 5)
+        sigmoid_rows(4, 0, 1)
         turn_back(2, 4, "bank7")
         copy_back(2, 4)
         quantise(2, 4)
-        send_on(1, 2, OWN, after="dh_t2")
+        send_on(0, 2, OWN[1:], after="dh_t2")
+        sigmoid_rows(4, 1, 4)
         sigmoid(5, 6)
 
         for t in (4, 5):

@@ -16,6 +16,7 @@ FP8X4 = mybir.dt.float8_e4m3fn_x4
 FP4X4 = mybir.dt.float4_e2m1fn_x4
 ACT = mybir.ActivationFunctionType
 ALU = mybir.AluOpType
+WIDTH = {F32: 4, I32: 4, U32: 4, BF16: 2, U8: 1}
 
 P = 128
 PASSES = N // 512
@@ -25,11 +26,10 @@ PER_EXPERT = C // P
 PER_COLUMN = 16
 QUADRANTS = 4
 MOVED_ROWS = 112
-EARLY = 2
 DX, DP = 0, 1
 HALF = GROUPS // 2
-OWN, PARTNER = ((0, DX), (1, DX)), ((0, DP), (1, DP))
-UPPER, LOWER = ((0, DX), (0, DP)), ((1, DX), (1, DP))
+ROW_TILES = K // P
+ALIGN = 64
 
 
 def load_scale_rows(nc, plane, rows):
@@ -48,16 +48,26 @@ def tile_moe_dub_silu_kernel(
     with ExitStack() as ctx:
         lists = ctx.enter_context(tc.tile_pool(name="lists", bufs=1))
         keep = ctx.enter_context(tc.tile_pool(name="keep", bufs=1))
-        psum = ctx.enter_context(tc.psum_pool(name="psum", bufs=2))
+        psum = ctx.enter_context(tc.psum_pool(name="psum", bufs=1))
 
-        tag_of = {}
+        place = {"free": 0}
 
-        def held(shape, dtype, name, after=None):
-            tag_of[name] = tag_of[after] if after else name
-            return keep.tile(shape, dtype, name=name, tag=tag_of[name], align_bytes=64)
+        def held(shape, dtype, name, over=None, at=0, room=0, lead=0):
+            size = WIDTH[dtype]
+            for n in shape[1:]:
+                size = size * n
+            if over is None:
+                start = place["free"] + lead
+                place["free"] = start + (size + room + ALIGN - 1) // ALIGN * ALIGN
+                place[name] = (start, size + room, lead)
+            else:
+                start = place[over][0] + at
+                assert at + size <= place[over][1] and -at <= place[over][2]
+                place[name] = (start, place[over][1] - at, 0)
+            return keep.tile(shape, dtype, name=name, align_bytes=ALIGN, offset=start)
 
-        def bank(shape, name, tag):
-            return psum.tile(shape, F32, name=name, tag=tag, bufs=1)
+        def bank(shape, name, number):
+            return psum.tile(shape, F32, name=name, tag=f"bank{number}")
 
         token_list = lists.tile([P, SLOTS // PER_COLUMN], U16, name="token_list")
         partner_list = lists.tile([P, SLOTS // PER_COLUMN], U16, name="partner_list")
@@ -73,7 +83,7 @@ def tile_moe_dub_silu_kernel(
         for plane in (dy_sc, slot_sc[0][1], w2_sc[0], wp_sc, w1_sc, slot_sc[1][1], w2_sc[1]):
             nc.vector.memset(plane[:].bitcast(I32), 0)
 
-        ident = keep.tile([P, P], F32, name="ident")
+        ident = held([P, P], F32, "ident")
         gate_rows = held([P, P], F32, "gate_rows")
         nc.gpsimd.memset(gate_rows[:], 0.0)
         make_identity(nc, ident[:])
@@ -81,12 +91,9 @@ def tile_moe_dub_silu_kernel(
         dy_w = [held([P, T], I32, f"dy_w{s}") for s in range(PASSES)]
         a_sb, w2_w, second_w = {}, {}, {}
 
-        def load_a(lo, hi):
-            part = held([P, 4, (hi - lo) * C], F32, f"a_sb{lo}")
-            pattern = "(c p) j -> p c j" if lo < EARLY else "(p c) j -> p c j"
-            nc.sync.dma_start(out=part[:], in_=a[:, lo * C : hi * C].rearrange(pattern, c=4))
-            for e in range(lo, hi):
-                a_sb[e] = part[:, :, (e - lo) * C : (e - lo + 1) * C]
+        def load_a(e):
+            a_sb[e] = held([P, 4, C], F32, f"a_sb{e}")
+            nc.sync.dma_start(out=a_sb[e][:], in_=a[:, e * C : (e + 1) * C].rearrange("(c p) j -> p c j", c=4))
 
         def load_w2(lo, hi):
             part = held([P, (hi - lo) * PASSES, 2 * H], U8, f"w2_w{lo}")
@@ -113,85 +120,65 @@ def tile_moe_dub_silu_kernel(
             )
 
         w2_rows = w2t_scales.rearrange("e s b w -> (e s) b w")
-        load_a(0, 1)
         nc.sync.dma_start(token_list[:], offs)
         for q in range(QUADRANTS):
             nc.sync.dma_start(
                 out=dy_sc[32 * q : 32 * q + 4 * PASSES, :].bitcast(I32),
                 in_=dy_scales[:, 4 * q : 4 * q + 4, :].bitcast(I32),
             )
-        load_a(1, 2)
-        nc.sync.dma_start(out=dy_w[0][:], in_=dy_words[0].rearrange("p n t -> p (n t)").bitcast(I32))
+        load_a(0)
         nc.sync.dma_start(out=gate_rows[0:GROUPS, :], in_=gate[0:1, :].rearrange("o (t c) -> (o t) c", c=P))
+        nc.sync.dma_start(out=dy_w[0][:], in_=dy_words[0].rearrange("p n t -> p (n t)").bitcast(I32))
+        load_a(1)
         nc.sync.dma_start(out=dy_w[1][:], in_=dy_words[1].rearrange("p n t -> p (n t)").bitcast(I32))
         for h in range(2):
             nc.vector.tensor_copy(slot_sc[h][0][:], dy_sc[:].indirect(entries(DX, h * HALF, (h + 1) * HALF)))
-        move_scale_rows(0)
         load_w2(0, 1)
         load_scale_rows(nc, w2_sc[0], w2_rows[0 : 2 * PASSES])
-        load_a(2, 3)
+        move_scale_rows(0)
+        load_a(2)
         load_w2(1, 2)
-        load_scale_rows(nc, wp_sc, wpt_scales.rearrange("e s b w -> (e s) b w"))
-        nc.sync.dma_start(partner_list[:], offs2)
-        load_second(DP, 0, 1)
-        load_a(3, 4)
+        load_a(3)
         load_scale_rows(nc, w1_sc, w1t_scales.rearrange("e s b w -> (e s) b w"))
-        load_second(DX, 0, 1)
+        load_second(DX, 0, E)
+        load_scale_rows(nc, wp_sc, wpt_scales.rearrange("e s b w -> (e s) b w"))
+        load_second(DP, 0, E)
+        nc.sync.dma_start(partner_list[:], offs2)
         move_scale_rows(1)
         load_scale_rows(nc, w2_sc[1], w2_rows[2 * PASSES :])
-        load_w2(2, E)
-        load_second(DP, 1, E)
-        load_second(DX, 1, E)
+        load_w2(2, 3)
+        load_w2(3, 4)
 
-        slot_w, sig, silu_neg, less_one, factor, a_turned, dh_t, back = {}, {}, {}, {}, {}, {}, {}, {}
-        sums, gated, turned, turned_sb, dh, dq, products, staged = {}, {}, {}, {}, {}, {}, {}, {}
+        slot_w, tanh_half, silu_neg, gated, part_dh, dh_t, sums, dh, dq, products, staged, a_turned, back = ({} for n in range(13))
+        window = [[held([P, T], F32, f"window{kt}{which}") for which in (DX, DP)] for kt in range(ROW_TILES)]
 
-        def by_group(table, lo, hi, dtype, name, after=None):
-            part = held([P, (hi - lo) * H], dtype, name, after)
-            for t in range(lo, hi):
-                table[t] = part[:, (t - lo) * H : (t - lo + 1) * H]
-            table[lo, hi] = part[:]
-
-        def gather_words(lo, hi, s, after=None):
-            part = held([P, (hi - lo) * P], U32, f"slot_w{lo}{s}", after)
+        def gather_words(lo, hi, s, over=None):
+            part = held([P, (hi - lo) * P], U32, f"slot_w{lo}{s}", over)
             nc.vector.tensor_copy(part[:], dy_w[s][:].bitcast(U32).indirect(entries(DX, lo, hi)))
             for t in range(lo, hi):
                 slot_w[t, s] = part[:, (t - lo) * P : (t - lo + 1) * P]
 
-        def turn_a(t):
+        def turn_a(t, number):
             e, u = divmod(t, PER_EXPERT)
-            a_turned[t] = bank([P, H], "a_turned", f"bank{4 + t}")
+            turned = bank([P, H], "a_turned", number)
             for c in range(H // P):
-                nc.tensor.transpose(a_turned[t][:, c * P : (c + 1) * P], a_sb[e][:, c, u * P : (u + 1) * P], ident[:])
+                nc.tensor.transpose(turned[:, c * P : (c + 1) * P], a_sb[e][:, c, u * P : (u + 1) * P], ident[:])
+            a_turned[t] = turned
 
-        def activate(lo, hi, func, scale, table):
-            e, u = divmod(lo, PER_EXPERT)
-            if e < EARLY:
-                nc.scalar.activation(table[lo], a_turned[lo][:], func, scale=scale)
-            else:
-                result = table[lo] if hi - lo == 1 else table[lo, hi]
-                nc.scalar.activation(
-                    result.rearrange("p (u r j) -> p u r j", r=4, j=P),
-                    a_sb[e][:, :, u * P : (u + hi - lo) * P].rearrange("p r (u j) -> p u r j", j=P),
-                    func,
-                    scale=scale,
-                )
+        def activations(t):
+            turned = a_turned[t]
+            silu_neg[t] = held([P, H], F32, f"silu{t}")
+            nc.scalar.activation(silu_neg[t][:], turned[:], ACT.Silu, scale=-1.0)
+            tanh_half[t] = held([P, H], F32, f"tanh{t}")
+            nc.scalar.activation(tanh_half[t][:], turned[:], ACT.Tanh, scale=0.5)
 
-        def sigmoid(lo, hi):
-            activate(lo, hi, ACT.Sigmoid, 1.0, sig)
+        def gate_factor(t, over=None):
+            gated[t] = held([P, H], F32, f"gated{t}", over)
+            nc.gpsimd.tensor_scalar(gated[t][:], silu_neg[t][:], neg_gate[:, t : t + 1], pos_gate[:, t : t + 1], ALU.mult, ALU.add)
 
-        def sigmoid_rows(t, lo, hi):
-            e, u = divmod(t, PER_EXPERT)
-            nc.scalar.activation(
-                sig[t].rearrange("p (r j) -> p r j", r=4)[:, lo:hi, :], a_sb[e][:, lo:hi, u * P : (u + 1) * P], ACT.Sigmoid
-            )
-
-        def silu(lo, hi):
-            activate(lo, hi, ACT.Silu, -1.0, silu_neg)
-
-        def first_product(t, tag):
+        def first_product(t, number):
             e = t // PER_EXPERT
-            sums[t] = bank([P, H], "sums", tag)
+            sums[t] = bank([P, H], "sums", number)
             for s in range(PASSES):
                 m = e % 2 * PASSES + s
                 nc.tensor.matmul_mx(
@@ -204,76 +191,46 @@ def tile_moe_dub_silu_kernel(
                     stop=(s == PASSES - 1),
                 )
 
-        def gate_sums(t):
-            gated[t] = held([P, 4, P], F32, f"gated{t}")
-            nc.scalar.activation(gated[t][:], sums[t][:].rearrange("j (p r) -> j r p", r=4), ACT.Copy, scale=neg_gate[:, t : t + 1])
+        def begin_dh(t, over=None, at=0):
+            part_dh[t] = held([P, H], F32, f"part{t}", over, at)
+            nc.vector.scalar_tensor_tensor(part_dh[t][:], tanh_half[t][:], 1.0, sums[t][:], ALU.add, ALU.mult)
 
-        def turn(t, tag):
-            turned[t] = bank([P, 4, P], "turned", tag)
-            for r in range(4):
-                nc.tensor.transpose(turned[t][:, r, :], gated[t][:, r, :], ident[:])
+        def finish_dh(engine, t, over=None, at=0):
+            dh_t[t] = held([P, H], BF16, f"dh_t{t}", over, at)
+            engine.tensor_tensor(dh_t[t][:], part_dh[t][:], gated[t][:], ALU.mult)
 
-        def factor_on_vector(t):
-            by_group(factor, t, t + 1, F32, f"factor{t}")
-            nc.vector.scalar_tensor_tensor(factor[t], silu_neg[t], 1.0, sig[t], ALU.subtract, ALU.mult)
-
-        def dh_on_vector(t):
-            nc.vector.scalar_tensor_tensor(dh_t[t], sums[t][:], neg_gate[:, t : t + 1], factor[t], ALU.mult, ALU.mult)
-
-        def turn_back(lo, hi, tag):
-            back[lo] = bank([P, hi - lo, 2, P], "back", tag)
+        def turn_back(lo, hi, number):
+            back[lo] = bank([P, hi - lo, 2, P], "back", number)
             for t in range(lo, hi):
-                pairs = dh_t[t].bitcast(F32)
+                pairs = dh_t[t][:].bitcast(F32)
                 for v in range(2):
                     nc.tensor.transpose(back[lo][:, t - lo, v, :], pairs[:, v : H // 2 : 2], ident[:])
 
-        def copy_back(lo, hi):
-            by_group(dh, lo, hi, BF16, f"dh{lo}")
-            nc.scalar.copy(
-                dh[lo, hi].bitcast(F32).rearrange("p (u j v) -> p u j v", u=hi - lo, v=2),
-                back[lo][:].rearrange("p u v j -> p u j v"),
-            )
-
-        def less_one_on_gpsimd(lo, hi, after=None):
-            by_group(less_one, lo, hi, F32, f"less_one{lo}", after)
-            nc.gpsimd.tensor_scalar(less_one[lo, hi], silu_neg[lo] if hi - lo == 1 else silu_neg[lo, hi], 1.0, -1.0, ALU.mult, ALU.add)
-
-        def less_one_on_scalar(t, after=None):
-            by_group(less_one, t, t + 1, F32, f"less_one{t}", after)
-            nc.scalar.activation(less_one[t], silu_neg[t], ACT.Copy, bias=-1.0)
-
-        def factor_on_gpsimd(t):
-            nc.gpsimd.tensor_tensor(factor[t], less_one[t], sig[t], ALU.mult)
-
-        def hand_over(t):
-            by_group(turned_sb, t, t + 1, F32, f"turned_sb{t}")
-            nc.scalar.copy(turned_sb[t].rearrange("p (j r) -> p j r", r=4), turned[t][:].rearrange("p r j -> p j r"))
-
-        def dh_on_gpsimd(t):
-            nc.gpsimd.tensor_tensor(
-                dh[t].rearrange("p (j r) -> p j r", r=4),
-                turned_sb[t].rearrange("p (j r) -> p j r", r=4),
-                factor[t].rearrange("p (r j) -> p j r", r=4),
-                ALU.mult,
-            )
+        def copy_back(lo, hi, on_vector, over=None, at=0):
+            dh[lo] = held([P, (hi - lo) * H], BF16, f"dh{lo}", over, at)
+            target = dh[lo][:].bitcast(F32).rearrange("p (u j v) -> p u j v", u=hi - lo, v=2)
+            if on_vector:
+                nc.vector.tensor_copy(target, back[lo][:].rearrange("p u v j -> p u j v"))
+            else:
+                nc.scalar.copy(target, back[lo][:].rearrange("p u v j -> p u j v"))
 
         def quantise(lo, hi):
             codes = held([P, (hi - lo) * P], U32, f"dq_w{lo}")
             scales = held([P, (hi - lo) * P], U8, f"dq_sc{lo}")
-            nc.vector.quantize_mx(out=codes[:].bitcast(FP8X4), scales=scales[:], in_=dh[lo, hi])
+            nc.vector.quantize_mx(out=codes[:].bitcast(FP8X4), scales=scales[:], in_=dh[lo][:])
             dq[lo] = (codes, scales)
 
-        def second_products(lo, hi, parts, tag):
+        def second_products(lo, hi, which, number):
             e = lo // PER_EXPERT
             codes, scales = dq[lo]
-            products[lo, parts] = bank([P, len(parts), (hi - lo) * P], "products", tag)
-            for n, (kt, which) in enumerate(parts):
+            products[lo, which] = bank([P, ROW_TILES, (hi - lo) * P], "products", number)
+            for kt in range(ROW_TILES):
                 if which == DX:
                     words, plane = second_w[DX, e][:, 2 * kt * P : 2 * (kt + 1) * P].bitcast(FP4X4), w1_sc
                 else:
                     words, plane = second_w[DP, e][:, 4 * kt * P : 4 * (kt + 1) * P].bitcast(FP8X4), wp_sc
                 nc.tensor.matmul_mx(
-                    out=products[lo, parts][:, n, :],
+                    out=products[lo, which][:, kt, :],
                     lhsT=words,
                     lhsT_scale=plane[:, e * K + kt * P : e * K + (kt + 1) * P],
                     rhs=codes[:].bitcast(FP8X4),
@@ -282,157 +239,123 @@ def tile_moe_dub_silu_kernel(
                     stop=True,
                 )
 
-        def joined_products(parts, tag):
-            kt = parts[0][0]
-            products[0, parts] = bank([P, 1, C], "products", tag)
-            for t in range(PER_EXPERT):
-                codes, scales = dq[t]
-                nc.tensor.matmul_mx(
-                    out=products[0, parts][:, 0, t * P : (t + 1) * P],
-                    lhsT=second_w[DX, 0][:, 2 * kt * P : 2 * (kt + 1) * P].bitcast(FP4X4),
-                    lhsT_scale=w1_sc[:, kt * P : (kt + 1) * P],
-                    rhs=codes[:].bitcast(FP8X4),
-                    rhs_scale=scales[:],
-                    start=True,
-                    stop=True,
-                )
+        def stage(e, which, kt, on_vector, over=None, room=0, lead=0):
+            staged[e, which, kt] = held([P, C], F32, f"staged{e}{which}{kt}", over, 0, room, lead)
+            if on_vector:
+                nc.vector.tensor_copy(staged[e, which, kt][:], products[PER_EXPERT * e, which][:, kt, :])
+            else:
+                nc.scalar.copy(staged[e, which, kt][:], products[PER_EXPERT * e, which][:, kt, :])
 
-        def stage(lo, hi, parts, after=None):
-            staged[lo, parts] = held([P, len(parts), (hi - lo) * P], F32, f"staged{lo}_{parts[0][0]}{parts[0][1]}", after)
-            nc.scalar.copy(staged[lo, parts][:], products[lo, parts][:])
+        def scatter(e, which, kt, on_vector):
+            target = window[kt][which][:].indirect(entries(which, PER_EXPERT * e, PER_EXPERT * (e + 1)))
+            if on_vector:
+                nc.vector.tensor_copy(target, staged[e, which, kt][:])
+            else:
+                nc.scalar.activation(target, staged[e, which, kt][:], ACT.Copy)
 
-        def scatter(lo, hi, parts):
-            for n, (kt, which) in enumerate(parts):
-                nc.vector.tensor_copy(window[kt][which][:].indirect(entries(which, lo, hi)), staged[lo, parts][:, n, :])
+        def add_and_store(adder, kt, lo, hi):
+            total = held([P, hi - lo], F32, f"total{kt}_{lo}")
+            adder.tensor_tensor(total[:], window[kt][DX][:, lo:hi], window[kt][DP][:, lo:hi], ALU.add)
+            nc.sync.dma_start(out=out[kt * P : (kt + 1) * P, lo:hi], in_=total[:])
 
-        def send(lo, hi, parts, tag, after=None):
-            second_products(lo, hi, parts, tag)
-            stage(lo, hi, parts, after)
-            scatter(lo, hi, parts)
-
-        def send_on(lo, hi, parts, after=None):
-            stage(lo, hi, parts, after)
-            scatter(lo, hi, parts)
-
-        def add_and_store(adder, queue, kt, pieces):
-            width = T // pieces
-            for lo in range(0, T, width):
-                total = keep.tile([P, width], F32, name=f"total{kt}_{lo}")
-                adder.tensor_tensor(total[:], window[kt][DX][:, lo : lo + width], window[kt][DP][:, lo : lo + width], ALU.add)
-                queue.dma_start(out=out[kt * P : (kt + 1) * P, lo : lo + width], in_=total[:])
-
-        by_group(sig, 0, 1, F32, "sig0")
-        by_group(sig, 1, 4, F32, "sig1")
-        for t in range(HALF):
-            turn_a(t)
-            sigmoid(t, t + 1)
-        gather_words(0, HALF, 0)
-        gather_words(0, 1, 1)
-        gather_words(1, HALF, 1)
-        gate_turned = bank([P, P], "gate_turned", "bank2")
+        turn_a(0, 0)
+        gate_turned = bank([P, P], "gate_turned", 4)
         nc.tensor.transpose(gate_turned[:], gate_rows[:], ident[:])
-        neg_gate = keep.tile([P, GROUPS], F32, name="neg_gate")
-        nc.vector.tensor_scalar(neg_gate[:], gate_turned[:, 0:GROUPS], -1.0, None, ALU.mult)
+        turn_a(1, 1)
+        activations(0)
+        neg_gate = held([P, GROUPS], F32, "neg_gate")
+        pos_gate = held([P, GROUPS], F32, "pos_gate")
+        nc.vector.tensor_scalar(neg_gate[:], gate_turned[:, 0:GROUPS], -0.5, None, ALU.mult)
+        nc.gpsimd.tensor_scalar(pos_gate[:], neg_gate[:], -1.0, 0.0, ALU.mult, ALU.add)
+        activations(1)
+        turn_a(2, 7)
+        turn_a(3, 0)
+        activations(2)
+        activations(3)
+        gather_words(0, HALF, 0)
         gather_words(HALF, GROUPS, 0)
-        by_group(silu_neg, 0, 3, F32, "silu0", after="a_sb1")
-        by_group(silu_neg, 3, 4, F32, "silu3")
+        gather_words(0, 2, 1)
+        gather_words(2, HALF, 1)
+        gather_words(HALF, GROUPS, 1)
         for t in range(HALF):
-            silu(t, t + 1)
-        window = [[keep.tile([P, T], F32, name=f"window{kt}{which}") for which in (DX, DP)] for kt in range(K // P)]
-
-        first_product(0, "bank0")
-        first_product(1, "bank1")
-        for t in (0, 1):
-            factor_on_vector(t)
-        for t in (0, 1):
-            by_group(dh_t, t, t + 1, BF16, f"dh_t{t}")
-            dh_on_vector(t)
-        gather_words(HALF, GROUPS, 1, after="factor0")
-        less_one_on_gpsimd(2, 3, after="sig0")
-        by_group(factor, 2, 3, F32, "factor2")
-        factor_on_gpsimd(2)
-        by_group(silu_neg, 4, 6, F32, "silu4")
-        silu(4, 6)
-        turn_back(0, 1, "bank2")
-        first_product(2, "bank0")
-        turn_back(1, 2, "bank3")
-        copy_back(0, 1)
-        quantise(0, 1)
-        less_one_on_scalar(3, after="dh_t0")
-        by_group(dh_t, 2, 4, BF16, "dh_t2", after="silu3")
-        dh_on_vector(2)
-        copy_back(1, 2)
-        quantise(1, 2)
-        send(0, 1, PARTNER[:1], "bank4")
-        send(0, 1, PARTNER[1:], "bank5")
-        send(1, 2, PARTNER[:1], "bank6")
-        second_products(1, 2, PARTNER[1:], "bank1")
-        first_product(3, "bank4")
-        by_group(factor, 3, 4, F32, "factor3", after="dh1")
-        factor_on_gpsimd(3)
-        less_one_on_gpsimd(4, 6, after="less_one3")
-        dh_on_vector(3)
-        by_group(silu_neg, 6, 8, F32, "silu6")
-        silu(6, 8)
-        send_on(1, 2, PARTNER[1:], after="slot_w11")
-        less_one_on_gpsimd(6, 8)
-        for part, tag in ((OWN[:1], "bank7"), (OWN[1:], "bank5")):
-            joined_products(part, tag)
-        send_on(0, 2, OWN[:1])
-        by_group(sig, 4, 6, F32, "sig4", after="dq_w0")
-        sigmoid_rows(4, 0, 1)
-        turn_back(2, 4, "bank7")
-        copy_back(2, 4)
+            gate_factor(t)
+        first_product(0, 2)
+        first_product(1, 3)
+        turn_a(4, 1)
+        first_product(2, 5)
+        turn_a(5, 7)
+        first_product(3, 6)
+        begin_dh(0)
+        begin_dh(1)
+        finish_dh(nc.vector, 0)
+        finish_dh(nc.vector, 1)
+        activations(4)
+        activations(5)
+        turn_a(6, 0)
+        turn_back(0, 2, 4)
+        turn_a(7, 1)
+        copy_back(0, 2, False)
+        begin_dh(2)
+        gate_factor(4, over="gated1")
+        begin_dh(3)
+        finish_dh(nc.vector, 2)
+        quantise(0, 2)
+        finish_dh(nc.vector, 3)
+        activations(6)
+        activations(7)
+        second_products(0, 2, DX, 3)
+        second_products(0, 2, DP, 4)
+        turn_back(2, 4, 2)
+        first_product(4, 5)
+        first_product(5, 6)
+        first_product(6, 7)
+        first_product(7, 0)
+        gate_factor(5, over="gated3")
+        gate_factor(6, over="silu5")
+        gate_factor(7, over="silu6")
+        stage(0, DX, 1, True, room=1536, lead=1536)
+        scatter(0, DX, 1, True)
+        stage(0, DX, 0, False)
+        scatter(0, DX, 0, False)
+        stage(0, DP, 0, False)
+        stage(0, DP, 1, False)
+        scatter(0, DP, 0, False)
+        scatter(0, DP, 1, False)
+        copy_back(2, 4, True, over="staged001", at=512)
+        begin_dh(4, over="staged001", at=-1536)
         quantise(2, 4)
-        send_on(0, 2, OWN[1:], after="dh_t2")
-        sigmoid_rows(4, 1, 4)
-        sigmoid(5, 6)
-
-        for t in (4, 5):
-            first_product(t, f"bank{t - 4}")
-        by_group(factor, 4, 6, F32, "factor4", after="dh2")
-        for t in (4, 5):
-            factor_on_gpsimd(t)
-        gate_sums(4)
-        send(2, 4, PARTNER[:1], "bank6")
-        turn(4, "bank2")
-        gate_sums(5)
-        send(2, 4, PARTNER[1:], "bank7")
-        turn(5, "bank3")
-        hand_over(4)
-        hand_over(5)
-        send(2, 4, OWN[:1], "bank4")
-        by_group(sig, 6, 8, F32, "sig6", after="gated5")
-        sigmoid(6, 8)
-        by_group(dh, 4, 6, BF16, "dh4")
-        for t in (4, 5):
-            dh_on_gpsimd(t)
-        for t in (6, 7):
-            first_product(t, f"bank{t - 6}")
-        for t in (6, 7):
-            gate_sums(t)
-            turn(t, f"bank{t - 4}")
-        for t in (6, 7):
-            hand_over(t)
-        quantise(4, 6)
-        send(2, 4, OWN[1:], "bank5", after="turned_sb5")
-
-        send(4, 6, UPPER[:1], "bank6")
-        send(4, 6, UPPER[1:], "bank7")
-        send(4, 6, LOWER[:1], "bank4")
-        by_group(factor, 6, 8, F32, "factor6", after="dh4")
-        for t in (6, 7):
-            factor_on_gpsimd(t)
-        by_group(dh, 6, 8, BF16, "dh6")
-        for t in (6, 7):
-            dh_on_gpsimd(t)
-        quantise(6, 8)
-        send(4, 6, LOWER[1:], "bank5", after="turned_sb7")
-
-        send(6, 8, UPPER[:1], "bank6")
-        send(6, 8, UPPER[1:], "bank7")
-        second_products(6, 8, LOWER, "bank4")
-        stage(6, 8, LOWER)
-        add_and_store(nc.gpsimd, nc.scalar, 0, 2)
-        scatter(6, 8, LOWER)
-        add_and_store(nc.vector, nc.sync, 1, 4)
+        begin_dh(5)
+        begin_dh(6)
+        second_products(2, 4, DX, 6)
+        second_products(2, 4, DP, 5)
+        finish_dh(nc.gpsimd, 4, over="dh2")
+        finish_dh(nc.gpsimd, 5, over="dh2", at=1024)
+        finish_dh(nc.gpsimd, 6)
+        stage(1, DX, 0, True)
+        begin_dh(7)
+        for e in (1, 2):
+            scatter(e, DX, 0, True)
+            for kt in range(2):
+                stage(e, DP, kt, False)
+            for kt in range(2):
+                scatter(e, DP, kt, False)
+            turn_back(2 * e + 2, 2 * e + 4, 7)
+            copy_back(2 * e + 2, 2 * e + 4, True)
+            stage(e, DX, 1, True, over=f"dh_t{2 * e + 3}")
+            quantise(2 * e + 2, 2 * e + 4)
+            if e == 1:
+                finish_dh(nc.gpsimd, 7, over="dh4")
+            second_products(2 * e + 2, 2 * e + 4, DX, 2 * e - 1)
+            second_products(2 * e + 2, 2 * e + 4, DP, 2 * e)
+            scatter(e, DX, 1, True)
+            stage(e + 1, DX, 0, True)
+        stage(3, DX, 1, True)
+        for kt in range(2):
+            stage(3, DP, kt, False)
+        for kt in range(2):
+            scatter(3, DX, kt, True)
+            scatter(3, DP, kt, False)
+        add_and_store(nc.gpsimd, 0, 0, 640)
+        add_and_store(nc.vector, 0, 640, 1024)
+        for lo in range(0, T, 256):
+            add_and_store(nc.vector, 1, lo, lo + 256)

@@ -149,7 +149,7 @@ def tile_moe_dub_silu_kernel(
         load_w2(2, 3)
         load_w2(3, 4)
 
-        slot_w, tanh_half, silu_neg, gated, part_dh, dh_t, sums, dh, dq, products, staged, a_turned, back = ({} for n in range(13))
+        slot_w, tanh_half, silu_neg, gated, part_dh, dh_t, sums, dh, dq, products, staged, a_turned, back, sig = ({} for n in range(14))
         window = [[held([P, T], F32, f"window{kt}{which}") for which in (DX, DP)] for kt in range(ROW_TILES)]
 
         def gather_words(lo, hi, s, over=None):
@@ -166,15 +166,25 @@ def tile_moe_dub_silu_kernel(
             a_turned[t] = turned
 
         def activations(t):
-            turned = a_turned[t]
-            silu_neg[t] = held([P, H], F32, f"silu{t}")
-            nc.scalar.activation(silu_neg[t][:], turned[:], ACT.Silu, scale=-1.0)
-            tanh_half[t] = held([P, H], F32, f"tanh{t}")
-            nc.scalar.activation(tanh_half[t][:], turned[:], ACT.Tanh, scale=0.5)
+            e, u = divmod(t, PER_EXPERT)
+            if u == 0:
+                silu_neg[e] = held([P, PER_EXPERT * H], F32, f"silu{e}")
+                tanh_half[e] = held([P, PER_EXPERT * H], F32, f"tanh{e}")
+            nc.scalar.activation(silu_neg[e][:, u * H : (u + 1) * H], a_turned[t][:], ACT.Silu, scale=-1.0)
+            nc.scalar.activation(tanh_half[e][:, u * H : (u + 1) * H], a_turned[t][:], ACT.Tanh, scale=0.5)
 
-        def gate_factor(t, over=None):
-            gated[t] = held([P, H], F32, f"gated{t}", over)
-            nc.gpsimd.tensor_scalar(gated[t][:], silu_neg[t][:], neg_gate[:, t : t + 1], pos_gate[:, t : t + 1], ALU.mult, ALU.add)
+        def affine(table, name, source, lo, hi, times, plus, over, at):
+            e, u = divmod(lo, PER_EXPERT)
+            part = held([P, (hi - lo) * H], F32, f"{name}{lo}", over, at)
+            nc.gpsimd.tensor_scalar(part[:], source[e][:, u * H : (u + hi - lo) * H], times, plus, ALU.mult, ALU.add)
+            for t in range(lo, hi):
+                table[t] = part[:, (t - lo) * H : (t - lo + 1) * H]
+
+        def sigmoid(lo, hi, over=None, at=0):
+            affine(sig, "sig", tanh_half, lo, hi, 0.5, 0.5, over, at)
+
+        def less_one(lo, hi, over=None, at=0):
+            affine(gated, "less", silu_neg, lo, hi, 1.0, -1.0, over, at)
 
         def first_product(t, number):
             e = t // PER_EXPERT
@@ -193,11 +203,17 @@ def tile_moe_dub_silu_kernel(
 
         def begin_dh(t, over=None, at=0):
             part_dh[t] = held([P, H], F32, f"part{t}", over, at)
-            nc.vector.scalar_tensor_tensor(part_dh[t][:], tanh_half[t][:], 1.0, sums[t][:], ALU.add, ALU.mult)
+            nc.vector.scalar_tensor_tensor(part_dh[t][:], sums[t][:], neg_gate[:, t : t + 1], sig[t], ALU.mult, ALU.mult)
 
-        def finish_dh(engine, t, over=None, at=0):
+        def finish_dh(on_vector, t, over=None, at=0):
+            e, u = divmod(t, PER_EXPERT)
             dh_t[t] = held([P, H], BF16, f"dh_t{t}", over, at)
-            engine.tensor_tensor(dh_t[t][:], part_dh[t][:], gated[t][:], ALU.mult)
+            if on_vector:
+                nc.vector.scalar_tensor_tensor(
+                    dh_t[t][:], silu_neg[e][:, u * H : (u + 1) * H], 1.0, part_dh[t][:], ALU.subtract, ALU.mult
+                )
+            else:
+                nc.gpsimd.tensor_tensor(dh_t[t][:], part_dh[t][:], gated[t], ALU.mult)
 
         def turn_back(lo, hi, number):
             back[lo] = bank([P, hi - lo, 2, P], "back", number)
@@ -264,9 +280,7 @@ def tile_moe_dub_silu_kernel(
         turn_a(1, 1)
         activations(0)
         neg_gate = held([P, GROUPS], F32, "neg_gate")
-        pos_gate = held([P, GROUPS], F32, "pos_gate")
-        nc.vector.tensor_scalar(neg_gate[:], gate_turned[:, 0:GROUPS], -0.5, None, ALU.mult)
-        nc.gpsimd.tensor_scalar(pos_gate[:], neg_gate[:], -1.0, 0.0, ALU.mult, ALU.add)
+        nc.vector.tensor_scalar(neg_gate[:], gate_turned[:, 0:GROUPS], -1.0, None, ALU.mult)
         activations(1)
         turn_a(2, 7)
         turn_a(3, 0)
@@ -278,7 +292,7 @@ def tile_moe_dub_silu_kernel(
         gather_words(2, HALF, 1)
         gather_words(HALF, GROUPS, 1)
         for t in range(HALF):
-            gate_factor(t)
+            sigmoid(t, t + 1)
         first_product(0, 2)
         first_product(1, 3)
         turn_a(4, 1)
@@ -287,8 +301,8 @@ def tile_moe_dub_silu_kernel(
         first_product(3, 6)
         begin_dh(0)
         begin_dh(1)
-        finish_dh(nc.vector, 0)
-        finish_dh(nc.vector, 1)
+        finish_dh(True, 0)
+        finish_dh(True, 1)
         activations(4)
         activations(5)
         turn_a(6, 0)
@@ -296,11 +310,11 @@ def tile_moe_dub_silu_kernel(
         turn_a(7, 1)
         copy_back(0, 2, False)
         begin_dh(2)
-        gate_factor(4, over="gated1")
+        sigmoid(4, 5, over="part1")
         begin_dh(3)
-        finish_dh(nc.vector, 2)
+        finish_dh(True, 2)
         quantise(0, 2)
-        finish_dh(nc.vector, 3)
+        finish_dh(True, 3, over="dh0")
         activations(6)
         activations(7)
         second_products(0, 2, DX, 3)
@@ -310,9 +324,9 @@ def tile_moe_dub_silu_kernel(
         first_product(5, 6)
         first_product(6, 7)
         first_product(7, 0)
-        gate_factor(5, over="gated3")
-        gate_factor(6, over="silu5")
-        gate_factor(7, over="silu6")
+        sigmoid(5, 6, over="part3")
+        less_one(4, 6, over="silu1")
+        sigmoid(6, 8)
         stage(0, DX, 1, True, room=1536, lead=1536)
         scatter(0, DX, 1, True)
         stage(0, DX, 0, False)
@@ -328,11 +342,11 @@ def tile_moe_dub_silu_kernel(
         begin_dh(6)
         second_products(2, 4, DX, 6)
         second_products(2, 4, DP, 5)
-        finish_dh(nc.gpsimd, 4, over="dh2")
-        finish_dh(nc.gpsimd, 5, over="dh2", at=1024)
-        finish_dh(nc.gpsimd, 6)
+        finish_dh(False, 4, over="dh2")
+        finish_dh(False, 5, over="dh2", at=1024)
         stage(1, DX, 0, True)
         begin_dh(7)
+        less_one(6, 8, over="sig6")
         for e in (1, 2):
             scatter(e, DX, 0, True)
             for kt in range(2):
@@ -344,7 +358,8 @@ def tile_moe_dub_silu_kernel(
             stage(e, DX, 1, True, over=f"dh_t{2 * e + 3}")
             quantise(2 * e + 2, 2 * e + 4)
             if e == 1:
-                finish_dh(nc.gpsimd, 7, over="dh4")
+                finish_dh(False, 6, over="dh4")
+                finish_dh(False, 7, over="dh4", at=1024)
             second_products(2 * e + 2, 2 * e + 4, DX, 2 * e - 1)
             second_products(2 * e + 2, 2 * e + 4, DP, 2 * e)
             scatter(e, DX, 1, True)

@@ -30,6 +30,7 @@ DX, DP = 0, 1
 HALF = GROUPS // 2
 ROW_TILES = K // P
 ALIGN = 64
+FAR = 208 * 1024
 
 
 def load_scale_rows(nc, plane, rows):
@@ -150,7 +151,11 @@ def tile_moe_dub_silu_kernel(
         load_w2(3, 4)
 
         slot_w, tanh_half, silu_neg, gated, part_dh, dh_t, sums, dh, dq, products, staged, a_turned, back, sig = ({} for n in range(14))
-        window = [[held([P, T], F32, f"window{kt}{which}") for which in (DX, DP)] for kt in range(ROW_TILES)]
+        place["far"] = (FAR, ROW_TILES * T * 4, 0)
+        window = [
+            [held([P, T], F32, f"window{kt}{DX}"), held([P, T], F32, f"window{kt}{DP}", "far", kt * T * 4)]
+            for kt in range(ROW_TILES)
+        ]
 
         def gather_words(lo, hi, s, over=None):
             part = held([P, (hi - lo) * P], U32, f"slot_w{lo}{s}", over)

@@ -29,6 +29,8 @@ MOVED_ROWS = 112
 DX, DP = 0, 1
 HALF = GROUPS // 2
 ROW_TILES = K // P
+OWN, PARTNER = ((DX, 0), (DX, 1)), ((DP, 0), (DP, 1))
+UPPER, LOWER = ((DX, 0), (DP, 0)), ((DX, 1), (DP, 1))
 ALIGN = 64
 FAR = 208 * 1024
 
@@ -236,22 +238,21 @@ def tile_moe_dub_silu_kernel(
                 nc.scalar.copy(target, back[lo][:].rearrange("p u v j -> p u j v"))
 
         def quantise(lo, hi):
-            codes = held([P, (hi - lo) * P], U32, f"dq_w{lo}")
+            codes = held([P, (hi - lo) * P], U32, f"dq_w{lo}", room=1024)
             scales = held([P, (hi - lo) * P], U8, f"dq_sc{lo}")
             nc.vector.quantize_mx(out=codes[:].bitcast(FP8X4), scales=scales[:], in_=dh[lo][:])
             dq[lo] = (codes, scales)
 
-        def second_products(lo, hi, which, number):
-            e = lo // PER_EXPERT
-            codes, scales = dq[lo]
-            products[lo, which] = bank([P, ROW_TILES, (hi - lo) * P], "products", number)
-            for kt in range(ROW_TILES):
+        def second_products(e, parts, number):
+            codes, scales = dq[PER_EXPERT * e]
+            products[e, parts] = bank([P, 2, C], "products", number)
+            for n, (which, kt) in enumerate(parts):
                 if which == DX:
                     words, plane = second_w[DX, e][:, 2 * kt * P : 2 * (kt + 1) * P].bitcast(FP4X4), w1_sc
                 else:
                     words, plane = second_w[DP, e][:, 4 * kt * P : 4 * (kt + 1) * P].bitcast(FP8X4), wp_sc
                 nc.tensor.matmul_mx(
-                    out=products[lo, which][:, kt, :],
+                    out=products[e, parts][:, n, :],
                     lhsT=words,
                     lhsT_scale=plane[:, e * K + kt * P : e * K + (kt + 1) * P],
                     rhs=codes[:].bitcast(FP8X4),
@@ -260,19 +261,21 @@ def tile_moe_dub_silu_kernel(
                     stop=True,
                 )
 
-        def stage(e, which, kt, on_vector, over=None, room=0, lead=0):
-            staged[e, which, kt] = held([P, C], F32, f"staged{e}{which}{kt}", over, 0, room, lead)
+        def stage(e, parts, lo, hi, on_vector, over=None, room=0, lead=0):
+            part = held([P, hi - lo, C], F32, f"staged{e}{parts[lo][0]}{parts[lo][1]}", over, 0, room, lead)
             if on_vector:
-                nc.vector.tensor_copy(staged[e, which, kt][:], products[PER_EXPERT * e, which][:, kt, :])
+                nc.vector.tensor_copy(part[:], products[e, parts][:, lo:hi, :])
             else:
-                nc.scalar.copy(staged[e, which, kt][:], products[PER_EXPERT * e, which][:, kt, :])
+                nc.scalar.copy(part[:], products[e, parts][:, lo:hi, :])
+            for n in range(lo, hi):
+                staged[e, parts[n]] = part[:, n - lo, :]
 
-        def scatter(e, which, kt, on_vector):
+        def scatter(e, which, kt):
             target = window[kt][which][:].indirect(entries(which, PER_EXPERT * e, PER_EXPERT * (e + 1)))
-            if on_vector:
-                nc.vector.tensor_copy(target, staged[e, which, kt][:])
+            if which == DX:
+                nc.vector.tensor_copy(target, staged[e, (which, kt)])
             else:
-                nc.scalar.activation(target, staged[e, which, kt][:], ACT.Copy)
+                nc.scalar.activation(target, staged[e, (which, kt)], ACT.Copy)
 
         def add_and_store(adder, kt, lo, hi):
             total = held([P, hi - lo], F32, f"total{kt}_{lo}")
@@ -322,8 +325,8 @@ def tile_moe_dub_silu_kernel(
         finish_dh(True, 3, over="dh0")
         activations(6)
         activations(7)
-        second_products(0, 2, DX, 3)
-        second_products(0, 2, DP, 4)
+        second_products(0, OWN, 3)
+        second_products(0, PARTNER, 4)
         turn_back(2, 4, 2)
         first_product(4, 5)
         first_product(5, 6)
@@ -332,50 +335,56 @@ def tile_moe_dub_silu_kernel(
         sigmoid(5, 6, over="part3")
         less_one(4, 6, over="silu1")
         sigmoid(6, 8)
-        stage(0, DX, 1, True, room=1536, lead=1536)
-        scatter(0, DX, 1, True)
-        stage(0, DX, 0, False)
-        scatter(0, DX, 0, False)
-        stage(0, DP, 0, False)
-        stage(0, DP, 1, False)
-        scatter(0, DP, 0, False)
-        scatter(0, DP, 1, False)
-        copy_back(2, 4, True, over="staged001", at=512)
-        begin_dh(4, over="staged001", at=-1536)
+        stage(0, OWN, 0, 1, True, room=1536, lead=1536)
+        scatter(0, DX, 0)
+        stage(0, PARTNER, 0, 1, False)
+        stage(0, PARTNER, 1, 2, False)
+        scatter(0, DP, 0)
+        scatter(0, DP, 1)
+        copy_back(2, 4, True, over="staged000", at=512)
+        begin_dh(4, over="staged000", at=-1536)
         quantise(2, 4)
         begin_dh(5)
         begin_dh(6)
-        second_products(2, 4, DX, 6)
-        second_products(2, 4, DP, 5)
+        stage(0, OWN, 1, 2, True, over="sig5")
+        begin_dh(7)
+        scatter(0, DX, 1)
+        second_products(1, OWN, 6)
+        second_products(1, PARTNER, 5)
         finish_dh(False, 4, over="dh2")
         finish_dh(False, 5, over="dh2", at=1024)
-        stage(1, DX, 0, True)
-        begin_dh(7)
-        less_one(6, 8, over="sig6")
-        for e in (1, 2):
-            scatter(e, DX, 0, True)
-            for kt in range(2):
-                stage(e, DP, kt, False)
-            for kt in range(2):
-                scatter(e, DP, kt, False)
-            turn_back(2 * e + 2, 2 * e + 4, 7)
-            copy_back(2 * e + 2, 2 * e + 4, True)
-            stage(e, DX, 1, True, over=f"dh_t{2 * e + 3}")
-            quantise(2 * e + 2, 2 * e + 4)
-            if e == 1:
-                finish_dh(False, 6, over="dh4")
-                finish_dh(False, 7, over="dh4", at=1024)
-            second_products(2 * e + 2, 2 * e + 4, DX, 2 * e - 1)
-            second_products(2 * e + 2, 2 * e + 4, DP, 2 * e)
-            scatter(e, DX, 1, True)
-            stage(e + 1, DX, 0, True)
-        stage(3, DX, 1, True)
-        for kt in range(2):
-            stage(3, DP, kt, False)
-        for kt in range(2):
-            scatter(3, DX, kt, True)
-            scatter(3, DP, kt, False)
-        add_and_store(nc.gpsimd, 0, 0, 640)
-        add_and_store(nc.vector, 0, 640, 1024)
+        stage(1, PARTNER, 0, 1, False)
+        stage(1, PARTNER, 1, 2, False)
+        scatter(1, DP, 0)
+        scatter(1, DP, 1)
+        finish_dh(True, 6, over="part5")
+        finish_dh(True, 7, over="part5", at=1024)
+        turn_back(4, 6, 7)
+        turn_back(6, 8, 0)
+        copy_back(4, 6, True)
+        stage(1, OWN, 0, 1, True, over="dh_t5")
+        quantise(4, 6)
+        copy_back(6, 8, True)
+        stage(1, OWN, 1, 2, True, over="dh_t7")
+        quantise(6, 8)
+        second_products(2, UPPER, 1)
+        second_products(2, LOWER, 2)
+        second_products(3, UPPER, 3)
+        second_products(3, LOWER, 4)
+        scatter(1, DX, 0)
+        scatter(1, DX, 1)
+        stage(2, UPPER, 0, 2, False)
+        scatter(2, DP, 0)
+        scatter(2, DX, 0)
+        stage(3, UPPER, 0, 2, False)
+        stage(2, LOWER, 0, 2, False, over="dq_w6")
+        stage(3, LOWER, 0, 2, True, over="tanh3")
+        scatter(3, DP, 0)
+        scatter(3, DX, 0)
+        for e in (2, 3):
+            scatter(e, DP, 1)
+            scatter(e, DX, 1)
+        for lo in range(0, T, 512):
+            add_and_store(nc.gpsimd, 0, lo, lo + 512)
         for lo in range(0, T, 256):
             add_and_store(nc.vector, 1, lo, lo + 256)

@@ -66,7 +66,7 @@ def tile_moe_dub_silu_kernel(
             else:
                 start = place[over][0] + at
                 assert at + size <= place[over][1] and -at <= place[over][2]
-                place[name] = (start, place[over][1] - at, 0)
+                place[name] = (start, place[over][1] - at, place[over][2] + at)
             return keep.tile(shape, dtype, name=name, align_bytes=ALIGN, offset=start)
 
         def bank(shape, name, number):
@@ -83,12 +83,15 @@ def tile_moe_dub_silu_kernel(
         w1_sc = held([P, E * K], U8, "w1_sc")
         wp_sc = held([P, E * K], U8, "wp_sc")
         slot_sc = [[held([P, HALF * P], U8, f"slot_sc{h}{s}") for s in range(PASSES)] for h in range(2)]
-        for plane in (dy_sc, slot_sc[0][1], w2_sc[0], wp_sc, w1_sc, slot_sc[1][1], w2_sc[1]):
+        nc.gpsimd.memset(dy_sc[:].bitcast(I32), 0)
+        gate_rows = held([P, P], F32, "gate_rows")
+        nc.vector.memset(gate_rows[:], 0.0)
+        for plane in (slot_sc[0][1], w2_sc[0], wp_sc, w1_sc, slot_sc[1][1], w2_sc[1]):
             nc.vector.memset(plane[:].bitcast(I32), 0)
 
+        one = held([P, 1], F32, "one")
+        nc.gpsimd.memset(one[:], 1.0)
         ident = held([P, P], F32, "ident")
-        gate_rows = held([P, P], F32, "gate_rows")
-        nc.gpsimd.memset(gate_rows[:], 0.0)
         make_identity(nc, ident[:])
 
         dy_w = [held([P, T], I32, f"dy_w{s}") for s in range(PASSES)]
@@ -123,13 +126,13 @@ def tile_moe_dub_silu_kernel(
             )
 
         w2_rows = w2t_scales.rearrange("e s b w -> (e s) b w")
+        load_a(0)
         nc.sync.dma_start(token_list[:], offs)
         for q in range(QUADRANTS):
             nc.sync.dma_start(
                 out=dy_sc[32 * q : 32 * q + 4 * PASSES, :].bitcast(I32),
                 in_=dy_scales[:, 4 * q : 4 * q + 4, :].bitcast(I32),
             )
-        load_a(0)
         nc.sync.dma_start(out=gate_rows[0:GROUPS, :], in_=gate[0:1, :].rearrange("o (t c) -> (o t) c", c=P))
         nc.sync.dma_start(out=dy_w[0][:], in_=dy_words[0].rearrange("p n t -> p (n t)").bitcast(I32))
         load_a(1)
@@ -143,9 +146,9 @@ def tile_moe_dub_silu_kernel(
         load_w2(1, 2)
         load_a(3)
         load_scale_rows(nc, w1_sc, w1t_scales.rearrange("e s b w -> (e s) b w"))
-        load_second(DX, 0, E)
+        load_second(DX, 0, 4)
         load_scale_rows(nc, wp_sc, wpt_scales.rearrange("e s b w -> (e s) b w"))
-        load_second(DP, 0, E)
+        load_second(DP, 0, 4)
         nc.sync.dma_start(partner_list[:], offs2)
         move_scale_rows(1)
         load_scale_rows(nc, w2_sc[1], w2_rows[2 * PASSES :])
@@ -159,8 +162,8 @@ def tile_moe_dub_silu_kernel(
             for kt in range(ROW_TILES)
         ]
 
-        def gather_words(lo, hi, s, over=None):
-            part = held([P, (hi - lo) * P], U32, f"slot_w{lo}{s}", over)
+        def gather_words(lo, hi, s, over=None, at=0):
+            part = held([P, (hi - lo) * P], U32, f"slot_w{lo}{s}", over, at)
             nc.vector.tensor_copy(part[:], dy_w[s][:].bitcast(U32).indirect(entries(DX, lo, hi)))
             for t in range(lo, hi):
                 slot_w[t, s] = part[:, (t - lo) * P : (t - lo + 1) * P]
@@ -173,25 +176,27 @@ def tile_moe_dub_silu_kernel(
             a_turned[t] = turned
 
         def activations(t):
-            e, u = divmod(t, PER_EXPERT)
-            if u == 0:
-                silu_neg[e] = held([P, PER_EXPERT * H], F32, f"silu{e}")
-                tanh_half[e] = held([P, PER_EXPERT * H], F32, f"tanh{e}")
-            nc.scalar.activation(silu_neg[e][:, u * H : (u + 1) * H], a_turned[t][:], ACT.Silu, scale=-1.0)
-            nc.scalar.activation(tanh_half[e][:, u * H : (u + 1) * H], a_turned[t][:], ACT.Tanh, scale=0.5)
+            turned = a_turned[t]
+            silu_neg[t] = held([P, H], F32, f"silu{t}")
+            nc.scalar.activation(silu_neg[t][:], turned[:], ACT.Silu, scale=-1.0)
+            tanh_half[t] = held([P, H], F32, f"tanh{t}")
+            nc.scalar.activation(tanh_half[t][:], turned[:], ACT.Tanh, scale=0.5)
 
-        def affine(table, name, source, lo, hi, times, plus, over, at):
-            e, u = divmod(lo, PER_EXPERT)
-            part = held([P, (hi - lo) * H], F32, f"{name}{lo}", over, at)
-            nc.gpsimd.tensor_scalar(part[:], source[e][:, u * H : (u + hi - lo) * H], times, plus, ALU.mult, ALU.add)
-            for t in range(lo, hi):
-                table[t] = part[:, (t - lo) * H : (t - lo + 1) * H]
+        def gate_factor(t, over=None):
+            gated[t] = held([P, H], F32, f"gated{t}", over)
+            nc.gpsimd.tensor_scalar(gated[t][:], silu_neg[t][:], neg_gate[:, t : t + 1], pos_gate[:, t : t + 1], ALU.mult, ALU.add)
 
-        def sigmoid(lo, hi, over=None, at=0):
-            affine(sig, "sig", tanh_half, lo, hi, 0.5, 0.5, over, at)
+        def whole_factor(t):
+            less = held([P, H], F32, f"less{t}")
+            nc.scalar.activation(less[:], silu_neg[t][:], ACT.Copy, bias=-1.0)
+            more = held([P, H], F32, f"more{t}")
+            nc.scalar.activation(more[:], tanh_half[t][:], ACT.Copy, bias=1.0)
+            gated[t] = held([P, H], F32, f"factor{t}")
+            nc.gpsimd.tensor_tensor(gated[t][:], less[:], more[:], ALU.mult)
 
-        def less_one(lo, hi, over=None, at=0):
-            affine(gated, "less", silu_neg, lo, hi, 1.0, -1.0, over, at)
+        def whole_dh(t, over=None):
+            dh_t[t] = held([P, H], BF16, f"dh_t{t}", over)
+            nc.vector.scalar_tensor_tensor(dh_t[t][:], sums[t][:], neg_gate[:, t : t + 1], gated[t][:], ALU.mult, ALU.mult)
 
         def first_product(t, number):
             e = t // PER_EXPERT
@@ -209,18 +214,12 @@ def tile_moe_dub_silu_kernel(
                 )
 
         def begin_dh(t, over=None, at=0):
-            part_dh[t] = held([P, H], F32, f"part{t}", over, at)
-            nc.vector.scalar_tensor_tensor(part_dh[t][:], sums[t][:], neg_gate[:, t : t + 1], sig[t], ALU.mult, ALU.mult)
+            part_dh[t] = held([P, H], F32, f"part{t}", over, at, room=1024, lead=1024)
+            nc.vector.scalar_tensor_tensor(part_dh[t][:], tanh_half[t][:], 1.0, sums[t][:], ALU.add, ALU.mult)
 
-        def finish_dh(on_vector, t, over=None, at=0):
-            e, u = divmod(t, PER_EXPERT)
-            dh_t[t] = held([P, H], BF16, f"dh_t{t}", over, at)
-            if on_vector:
-                nc.vector.scalar_tensor_tensor(
-                    dh_t[t][:], silu_neg[e][:, u * H : (u + 1) * H], 1.0, part_dh[t][:], ALU.subtract, ALU.mult
-                )
-            else:
-                nc.gpsimd.tensor_tensor(dh_t[t][:], part_dh[t][:], gated[t], ALU.mult)
+        def finish_dh(engine, t, over=None, at=0):
+            dh_t[t] = held([P, H], BF16, f"dh_t{t}", over, at, room=1024)
+            engine.tensor_tensor(dh_t[t][:], part_dh[t][:], gated[t][:], ALU.mult)
 
         def turn_back(lo, hi, number):
             back[lo] = bank([P, hi - lo, 2, P], "back", number)
@@ -230,39 +229,42 @@ def tile_moe_dub_silu_kernel(
                     nc.tensor.transpose(back[lo][:, t - lo, v, :], pairs[:, v : H // 2 : 2], ident[:])
 
         def copy_back(lo, hi, on_vector, over=None, at=0):
-            dh[lo] = held([P, (hi - lo) * H], BF16, f"dh{lo}", over, at)
+            dh[lo] = held([P, (hi - lo) * H], BF16, f"dh{lo}", over, at, room=1024)
             target = dh[lo][:].bitcast(F32).rearrange("p (u j v) -> p u j v", u=hi - lo, v=2)
             if on_vector:
                 nc.vector.tensor_copy(target, back[lo][:].rearrange("p u v j -> p u j v"))
             else:
                 nc.scalar.copy(target, back[lo][:].rearrange("p u v j -> p u j v"))
 
-        def quantise(lo, hi):
-            codes = held([P, (hi - lo) * P], U32, f"dq_w{lo}", room=1024)
-            scales = held([P, (hi - lo) * P], U8, f"dq_sc{lo}")
+        def quantise(lo, hi, over=None, also=None):
+            codes = held([P, (hi - lo) * P], U32, f"dq_w{lo}", over, room=1024)
+            scales = held([P, (hi - lo) * P], U8, f"dq_sc{lo}", also)
             nc.vector.quantize_mx(out=codes[:].bitcast(FP8X4), scales=scales[:], in_=dh[lo][:])
             dq[lo] = (codes, scales)
 
-        def second_products(e, parts, number):
+        def second_product(target, e, which, kt):
             codes, scales = dq[PER_EXPERT * e]
-            products[e, parts] = bank([P, 2, C], "products", number)
-            for n, (which, kt) in enumerate(parts):
-                if which == DX:
-                    words, plane = second_w[DX, e][:, 2 * kt * P : 2 * (kt + 1) * P].bitcast(FP4X4), w1_sc
-                else:
-                    words, plane = second_w[DP, e][:, 4 * kt * P : 4 * (kt + 1) * P].bitcast(FP8X4), wp_sc
-                nc.tensor.matmul_mx(
-                    out=products[e, parts][:, n, :],
-                    lhsT=words,
-                    lhsT_scale=plane[:, e * K + kt * P : e * K + (kt + 1) * P],
-                    rhs=codes[:].bitcast(FP8X4),
-                    rhs_scale=scales[:],
-                    start=True,
-                    stop=True,
-                )
+            if which == DX:
+                words, plane = second_w[DX, e][:, 2 * kt * P : 2 * (kt + 1) * P].bitcast(FP4X4), w1_sc
+            else:
+                words, plane = second_w[DP, e][:, 4 * kt * P : 4 * (kt + 1) * P].bitcast(FP8X4), wp_sc
+            nc.tensor.matmul_mx(
+                out=target,
+                lhsT=words,
+                lhsT_scale=plane[:, e * K + kt * P : e * K + (kt + 1) * P],
+                rhs=codes[:].bitcast(FP8X4),
+                rhs_scale=scales[:],
+                start=True,
+                stop=True,
+            )
 
-        def stage(e, parts, lo, hi, on_vector, over=None, room=0, lead=0):
-            part = held([P, hi - lo, C], F32, f"staged{e}{parts[lo][0]}{parts[lo][1]}", over, 0, room, lead)
+        def second_products(e, parts, number):
+            products[e, parts] = bank([P, len(parts), C], "products", number)
+            for n, (which, kt) in enumerate(parts):
+                second_product(products[e, parts][:, n, :], e, which, kt)
+
+        def stage(e, parts, lo, hi, on_vector, over=None, at=0):
+            part = held([P, hi - lo, C], F32, f"staged{e}{parts[lo][0]}{parts[lo][1]}", over, at)
             if on_vector:
                 nc.vector.tensor_copy(part[:], products[e, parts][:, lo:hi, :])
             else:
@@ -270,26 +272,29 @@ def tile_moe_dub_silu_kernel(
             for n in range(lo, hi):
                 staged[e, parts[n]] = part[:, n - lo, :]
 
-        def scatter(e, which, kt):
+        def scatter(e, which, kt, on_vector):
             target = window[kt][which][:].indirect(entries(which, PER_EXPERT * e, PER_EXPERT * (e + 1)))
-            if which == DX:
+            if on_vector:
                 nc.vector.tensor_copy(target, staged[e, (which, kt)])
             else:
                 nc.scalar.activation(target, staged[e, (which, kt)], ACT.Copy)
 
-        def add_and_store(adder, kt, lo, hi):
-            total = held([P, hi - lo], F32, f"total{kt}_{lo}")
+        def add_and_store(adder, kt, lo, hi, over=None, at=0):
+            total = held([P, hi - lo], F32, f"total{kt}_{lo}", over, at)
             adder.tensor_tensor(total[:], window[kt][DX][:, lo:hi], window[kt][DP][:, lo:hi], ALU.add)
             nc.sync.dma_start(out=out[kt * P : (kt + 1) * P, lo:hi], in_=total[:])
 
         turn_a(0, 0)
+        turn_a(1, 1)
         gate_turned = bank([P, P], "gate_turned", 4)
         nc.tensor.transpose(gate_turned[:], gate_rows[:], ident[:])
-        turn_a(1, 1)
-        activations(0)
+        for t in range(2):
+            activations(t)
+            whole_factor(t)
         neg_gate = held([P, GROUPS], F32, "neg_gate")
-        nc.vector.tensor_scalar(neg_gate[:], gate_turned[:, 0:GROUPS], -1.0, None, ALU.mult)
-        activations(1)
+        pos_gate = held([P, GROUPS], F32, "pos_gate")
+        nc.vector.tensor_scalar(neg_gate[:], gate_turned[:, 0:GROUPS], -0.5, None, ALU.mult)
+        nc.gpsimd.tensor_scalar(pos_gate[:], neg_gate[:], -1.0, 0.0, ALU.mult, ALU.add)
         turn_a(2, 7)
         turn_a(3, 0)
         activations(2)
@@ -298,31 +303,29 @@ def tile_moe_dub_silu_kernel(
         gather_words(HALF, GROUPS, 0)
         gather_words(0, 2, 1)
         gather_words(2, HALF, 1)
-        gather_words(HALF, GROUPS, 1)
-        for t in range(HALF):
-            sigmoid(t, t + 1)
+        gate_factor(2)
+        gate_factor(3)
         first_product(0, 2)
         first_product(1, 3)
         turn_a(4, 1)
-        first_product(2, 5)
         turn_a(5, 7)
+        first_product(2, 5)
         first_product(3, 6)
-        begin_dh(0)
-        begin_dh(1)
-        finish_dh(True, 0)
-        finish_dh(True, 1)
+        whole_dh(0)
+        whole_dh(1)
+        gather_words(4, 6, 1, over="factor0")
+        begin_dh(2)
         activations(4)
         activations(5)
         turn_a(6, 0)
-        turn_back(0, 2, 4)
+        turn_back(0, 2, 5)
         turn_a(7, 1)
         copy_back(0, 2, False)
-        begin_dh(2)
-        sigmoid(4, 5, over="part1")
         begin_dh(3)
-        finish_dh(True, 2)
+        gather_words(6, 8, 1, over="factor1")
+        finish_dh(nc.vector, 2)
         quantise(0, 2)
-        finish_dh(True, 3, over="dh0")
+        finish_dh(nc.vector, 3, over="dh0")
         activations(6)
         activations(7)
         second_products(0, OWN, 3)
@@ -332,33 +335,36 @@ def tile_moe_dub_silu_kernel(
         first_product(5, 6)
         first_product(6, 7)
         first_product(7, 0)
-        sigmoid(5, 6, over="part3")
-        less_one(4, 6, over="silu1")
-        sigmoid(6, 8)
-        stage(0, OWN, 0, 1, True, room=1536, lead=1536)
-        scatter(0, DX, 0)
+        gate_factor(4, over="gated3")
+        gate_factor(5, over="part3")
+        gate_factor(6, over="silu4")
+        gate_factor(7, over="silu5")
+        place["pad"] = (place["free"], 4096 + 1024, 0)
+        place["free"] = place["free"] + 4096 + 1024
+        stage(0, OWN, 0, 1, True, over="pad", at=1536)
+        scatter(0, DX, 0, True)
         stage(0, PARTNER, 0, 1, False)
         stage(0, PARTNER, 1, 2, False)
-        scatter(0, DP, 0)
-        scatter(0, DP, 1)
+        scatter(0, DP, 0, False)
+        scatter(0, DP, 1, False)
         copy_back(2, 4, True, over="staged000", at=512)
         begin_dh(4, over="staged000", at=-1536)
         quantise(2, 4)
         begin_dh(5)
         begin_dh(6)
-        stage(0, OWN, 1, 2, True, over="sig5")
+        stage(0, OWN, 1, 2, True, over="tanh5")
         begin_dh(7)
-        scatter(0, DX, 1)
+        scatter(0, DX, 1, True)
         second_products(1, OWN, 6)
         second_products(1, PARTNER, 5)
-        finish_dh(False, 4, over="dh2")
-        finish_dh(False, 5, over="dh2", at=1024)
+        finish_dh(nc.gpsimd, 4, over="dh2")
+        finish_dh(nc.gpsimd, 5, over="dh2", at=1024)
         stage(1, PARTNER, 0, 1, False)
         stage(1, PARTNER, 1, 2, False)
-        scatter(1, DP, 0)
-        scatter(1, DP, 1)
-        finish_dh(True, 6, over="part5")
-        finish_dh(True, 7, over="part5", at=1024)
+        scatter(1, DP, 0, False)
+        scatter(1, DP, 1, False)
+        finish_dh(nc.vector, 6, over="part5")
+        finish_dh(nc.vector, 7, over="part5", at=1024)
         turn_back(4, 6, 7)
         turn_back(6, 8, 0)
         copy_back(4, 6, True)
@@ -368,23 +374,29 @@ def tile_moe_dub_silu_kernel(
         stage(1, OWN, 1, 2, True, over="dh_t7")
         quantise(6, 8)
         second_products(2, UPPER, 1)
-        second_products(2, LOWER, 2)
         second_products(3, UPPER, 3)
-        second_products(3, LOWER, 4)
-        scatter(1, DX, 0)
-        scatter(1, DX, 1)
-        stage(2, UPPER, 0, 2, False)
-        scatter(2, DP, 0)
-        scatter(2, DX, 0)
-        stage(3, UPPER, 0, 2, False)
-        stage(2, LOWER, 0, 2, False, over="dq_w6")
-        stage(3, LOWER, 0, 2, True, over="tanh3")
-        scatter(3, DP, 0)
-        scatter(3, DX, 0)
+        lower = [bank([P, 2, C], "lower", number) for number in (2, 4)]
+        for which in (DP, DX):
+            for e in (2, 3):
+                second_product(lower[which][:, e - 2, :], e, which, 1)
+        scatter(1, DX, 0, True)
+        scatter(1, DX, 1, True)
+        upper = held([P, 2, 2, C], F32, "upper")
         for e in (2, 3):
-            scatter(e, DP, 1)
-            scatter(e, DX, 1)
+            nc.scalar.copy(upper[:, :, e - 2, :], products[e, UPPER][:])
+            if e == 3:
+                lower_dp = held([P, 2 * C], F32, "lower_dp")
+                nc.scalar.copy(lower_dp[:], lower[DP][:].rearrange("p e c -> p (e c)"))
+            target = window[0][DP][:].indirect(entries(DP, PER_EXPERT * e, PER_EXPERT * (e + 1)))
+            nc.scalar.activation(target, upper[:, DP, e - 2, :], ACT.Copy)
+        lower_dx = held([P, 2 * C], F32, "lower_dx")
+        nc.vector.tensor_copy(lower_dx[:], lower[DX][:].rearrange("p e c -> p (e c)"))
+        nc.vector.tensor_copy(
+            window[0][DX][:].indirect(entries(DX, HALF, GROUPS)), upper[:, DX, :, :].rearrange("p e c -> p (e c)")
+        )
+        nc.scalar.activation(window[1][DP][:].indirect(entries(DP, HALF, GROUPS)), lower_dp[:], ACT.Copy, scale=one[:])
+        nc.vector.tensor_copy(window[1][DX][:].indirect(entries(DX, HALF, GROUPS)), lower_dx[:])
         for lo in range(0, T, 512):
             add_and_store(nc.gpsimd, 0, lo, lo + 512)
         for lo in range(0, T, 256):
-            add_and_store(nc.vector, 1, lo, lo + 256)
+            add_and_store(nc.vector, 1, lo, lo + 256, "window00", 4 * lo)

@@ -146,21 +146,21 @@ def tile_moe_dub_silu_kernel(
         load_w2(1, 2)
         load_a(3)
         load_scale_rows(nc, w1_sc, w1t_scales.rearrange("e s b w -> (e s) b w"))
-        load_second(DX, 0, 4)
+        load_second(DX, 0, 1)
         load_scale_rows(nc, wp_sc, wpt_scales.rearrange("e s b w -> (e s) b w"))
-        load_second(DP, 0, 4)
+        load_second(DP, 0, 1)
         nc.sync.dma_start(partner_list[:], offs2)
         move_scale_rows(1)
         load_scale_rows(nc, w2_sc[1], w2_rows[2 * PASSES :])
         load_w2(2, 3)
         load_w2(3, 4)
+        load_second(DX, 1, 4)
+        load_second(DP, 1, 4)
 
         slot_w, tanh_half, silu_neg, gated, part_dh, dh_t, sums, dh, dq, products, staged, a_turned, back, sig = ({} for n in range(14))
         place["far"] = (FAR, ROW_TILES * T * 4, 0)
-        window = [
-            [held([P, T], F32, f"window{kt}{DX}"), held([P, T], F32, f"window{kt}{DP}", "far", kt * T * 4)]
-            for kt in range(ROW_TILES)
-        ]
+        window = [[None, held([P, T], F32, f"window{kt}{DP}", "far", kt * T * 4)] for kt in range(ROW_TILES)]
+        window[0][DX] = held([P, T], F32, "window00")
 
         def gather_words(lo, hi, s, over=None, at=0):
             part = held([P, (hi - lo) * P], U32, f"slot_w{lo}{s}", over, at)
@@ -179,7 +179,7 @@ def tile_moe_dub_silu_kernel(
             turned = a_turned[t]
             silu_neg[t] = held([P, H], F32, f"silu{t}")
             nc.scalar.activation(silu_neg[t][:], turned[:], ACT.Silu, scale=-1.0)
-            tanh_half[t] = held([P, H], F32, f"tanh{t}")
+            tanh_half[t] = held([P, H], F32, f"tanh{t}", room=2048 if t == 6 else 0)
             nc.scalar.activation(tanh_half[t][:], turned[:], ACT.Tanh, scale=0.5)
 
         def gate_factor(t, over=None):
@@ -264,7 +264,7 @@ def tile_moe_dub_silu_kernel(
                 second_product(products[e, parts][:, n, :], e, which, kt)
 
         def stage(e, parts, lo, hi, on_vector, over=None, at=0):
-            part = held([P, hi - lo, C], F32, f"staged{e}{parts[lo][0]}{parts[lo][1]}", over, at)
+            part = held([P, hi - lo, C], F32, f"staged{e}{parts[lo][0]}{parts[lo][1]}", over, at, room=1024)
             if on_vector:
                 nc.vector.tensor_copy(part[:], products[e, parts][:, lo:hi, :])
             else:
@@ -328,8 +328,11 @@ def tile_moe_dub_silu_kernel(
         finish_dh(nc.vector, 3, over="dh0")
         activations(6)
         activations(7)
-        second_products(0, OWN, 3)
+        second_products(0, OWN[:1], 2)
+        second_products(0, OWN[1:], 3)
         second_products(0, PARTNER, 4)
+        stage(0, OWN[:1], 0, 1, True)
+        stage(0, OWN[1:], 0, 1, True)
         turn_back(2, 4, 2)
         first_product(4, 5)
         first_product(5, 6)
@@ -339,21 +342,18 @@ def tile_moe_dub_silu_kernel(
         gate_factor(5, over="part3")
         gate_factor(6, over="silu4")
         gate_factor(7, over="silu5")
-        place["pad"] = (place["free"], 4096 + 1024, 0)
-        place["free"] = place["free"] + 4096 + 1024
-        stage(0, OWN, 0, 1, True, over="pad", at=1536)
         scatter(0, DX, 0, True)
         stage(0, PARTNER, 0, 1, False)
         stage(0, PARTNER, 1, 2, False)
         scatter(0, DP, 0, False)
         scatter(0, DP, 1, False)
-        copy_back(2, 4, True, over="staged000", at=512)
-        begin_dh(4, over="staged000", at=-1536)
+        copy_back(2, 4, True)
+        begin_dh(4, over="staged000")
         quantise(2, 4)
         begin_dh(5)
         begin_dh(6)
-        stage(0, OWN, 1, 2, True, over="tanh5")
         begin_dh(7)
+        window[1][DX] = held([P, T], F32, "window10", "tanh6")
         scatter(0, DX, 1, True)
         second_products(1, OWN, 6)
         second_products(1, PARTNER, 5)
@@ -365,37 +365,34 @@ def tile_moe_dub_silu_kernel(
         scatter(1, DP, 1, False)
         finish_dh(nc.vector, 6, over="part5")
         finish_dh(nc.vector, 7, over="part5", at=1024)
-        turn_back(4, 6, 7)
+        turn_back(4, 6, 5)
         turn_back(6, 8, 0)
         copy_back(4, 6, True)
         stage(1, OWN, 0, 1, True, over="dh_t5")
         quantise(4, 6)
+        pair = {(which, kt): bank([P, 2, C], "pair", 1 + 2 * kt + which) for kt in range(ROW_TILES) for which in (DP, DX)}
+        for which, kt in pair:
+            second_product(pair[which, kt][:, 0, :], 2, which, kt)
         copy_back(6, 8, True)
         stage(1, OWN, 1, 2, True, over="dh_t7")
+        both = {key: held([P, 2 * C], F32, f"both{key[0]}{key[1]}") for key in pair}
+        nc.scalar.copy(both[DP, 0][:, 0:C], pair[DP, 0][:, 0, :])
         quantise(6, 8)
-        second_products(2, UPPER, 1)
-        second_products(3, UPPER, 3)
-        lower = [bank([P, 2, C], "lower", number) for number in (2, 4)]
-        for which in (DP, DX):
-            for e in (2, 3):
-                second_product(lower[which][:, e - 2, :], e, which, 1)
+        last = bank([P, C], "last", 7)
+        second_product(last[:], 3, DP, 0)
+        for which, kt in ((DX, 0), (DX, 1), (DP, 1)):
+            second_product(pair[which, kt][:, 1, :], 3, which, kt)
         scatter(1, DX, 0, True)
         scatter(1, DX, 1, True)
-        upper = held([P, 2, 2, C], F32, "upper")
-        for e in (2, 3):
-            nc.scalar.copy(upper[:, :, e - 2, :], products[e, UPPER][:])
-            if e == 3:
-                lower_dp = held([P, 2 * C], F32, "lower_dp")
-                nc.scalar.copy(lower_dp[:], lower[DP][:].rearrange("p e c -> p (e c)"))
-            target = window[0][DP][:].indirect(entries(DP, PER_EXPERT * e, PER_EXPERT * (e + 1)))
-            nc.scalar.activation(target, upper[:, DP, e - 2, :], ACT.Copy)
-        lower_dx = held([P, 2 * C], F32, "lower_dx")
-        nc.vector.tensor_copy(lower_dx[:], lower[DX][:].rearrange("p e c -> p (e c)"))
-        nc.vector.tensor_copy(
-            window[0][DX][:].indirect(entries(DX, HALF, GROUPS)), upper[:, DX, :, :].rearrange("p e c -> p (e c)")
-        )
-        nc.scalar.activation(window[1][DP][:].indirect(entries(DP, HALF, GROUPS)), lower_dp[:], ACT.Copy, scale=one[:])
-        nc.vector.tensor_copy(window[1][DX][:].indirect(entries(DX, HALF, GROUPS)), lower_dx[:])
+        nc.scalar.activation(window[0][DP][:].indirect(entries(DP, 4, 6)), both[DP, 0][:, 0:C], ACT.Copy)
+        nc.scalar.copy(both[DP, 0][:, C:], last[:])
+        nc.scalar.copy(both[DP, 1][:], pair[DP, 1][:].rearrange("p e c -> p (e c)"))
+        nc.scalar.copy(both[DX, 1][:], pair[DX, 1][:].rearrange("p e c -> p (e c)"))
+        nc.scalar.activation(window[0][DP][:].indirect(entries(DP, 6, 8)), both[DP, 0][:, C:], ACT.Copy)
+        nc.scalar.activation(window[1][DP][:].indirect(entries(DP, HALF, GROUPS)), both[DP, 1][:], ACT.Copy, scale=one[:])
+        nc.vector.tensor_copy(both[DX, 0][:], pair[DX, 0][:].rearrange("p e c -> p (e c)"))
+        for kt in range(ROW_TILES):
+            nc.vector.tensor_copy(window[kt][DX][:].indirect(entries(DX, HALF, GROUPS)), both[DX, kt][:])
         for lo in range(0, T, 512):
             add_and_store(nc.gpsimd, 0, lo, lo + 512)
         for lo in range(0, T, 256):

@@ -154,8 +154,8 @@ def tile_moe_dub_silu_kernel(
         load_scale_rows(nc, w2_sc[1], w2_rows[2 * PASSES :])
         load_w2(2, 3)
         load_w2(3, 4)
-        load_second(DX, 1, 4)
         load_second(DP, 1, 4)
+        load_second(DX, 1, 4)
 
         slot_w, tanh_half, silu_neg, gated, part_dh, dh_t, sums, dh, dq, products, staged, a_turned, back, sig = ({} for n in range(14))
         place["far"] = (FAR, ROW_TILES * T * 4, 0)
@@ -316,10 +316,11 @@ def tile_moe_dub_silu_kernel(
         gather_words(4, 6, 1, over="factor0")
         begin_dh(2)
         activations(4)
+        gate_factor(4)
         activations(5)
         turn_a(6, 0)
-        turn_back(0, 2, 5)
-        turn_a(7, 1)
+        turn_back(0, 2, 1)
+        turn_a(7, 5)
         copy_back(0, 2, False)
         begin_dh(3)
         gather_words(6, 8, 1, over="factor1")
@@ -338,9 +339,8 @@ def tile_moe_dub_silu_kernel(
         first_product(5, 6)
         first_product(6, 7)
         first_product(7, 0)
-        gate_factor(4, over="gated3")
-        gate_factor(5, over="part3")
-        gate_factor(6, over="silu4")
+        gate_factor(5, over="gated3")
+        gate_factor(6, over="part3")
         gate_factor(7, over="silu5")
         scatter(0, DX, 0, True)
         stage(0, PARTNER, 0, 1, False)
@@ -355,8 +355,8 @@ def tile_moe_dub_silu_kernel(
         begin_dh(7)
         window[1][DX] = held([P, T], F32, "window10", "tanh6")
         scatter(0, DX, 1, True)
-        second_products(1, OWN, 6)
         second_products(1, PARTNER, 5)
+        second_products(1, OWN, 6)
         finish_dh(nc.gpsimd, 4, over="dh2")
         finish_dh(nc.gpsimd, 5, over="dh2", at=1024)
         stage(1, PARTNER, 0, 1, False)
@@ -386,14 +386,14 @@ def tile_moe_dub_silu_kernel(
         scatter(1, DX, 1, True)
         nc.scalar.activation(window[0][DP][:].indirect(entries(DP, 4, 6)), both[DP, 0][:, 0:C], ACT.Copy)
         nc.scalar.copy(both[DP, 0][:, C:], last[:])
+        nc.scalar.copy(both[DX, 0][:], pair[DX, 0][:].rearrange("p e c -> p (e c)"))
         nc.scalar.copy(both[DP, 1][:], pair[DP, 1][:].rearrange("p e c -> p (e c)"))
         nc.scalar.copy(both[DX, 1][:], pair[DX, 1][:].rearrange("p e c -> p (e c)"))
         nc.scalar.activation(window[0][DP][:].indirect(entries(DP, 6, 8)), both[DP, 0][:, C:], ACT.Copy)
         nc.scalar.activation(window[1][DP][:].indirect(entries(DP, HALF, GROUPS)), both[DP, 1][:], ACT.Copy, scale=one[:])
-        nc.vector.tensor_copy(both[DX, 0][:], pair[DX, 0][:].rearrange("p e c -> p (e c)"))
         for kt in range(ROW_TILES):
             nc.vector.tensor_copy(window[kt][DX][:].indirect(entries(DX, HALF, GROUPS)), both[DX, kt][:])
         for lo in range(0, T, 512):
             add_and_store(nc.gpsimd, 0, lo, lo + 512)
-        for lo in range(0, T, 256):
-            add_and_store(nc.vector, 1, lo, lo + 256, "window00", 4 * lo)
+        for lo, hi in ((0, 128), (128, 384), (384, 704), (704, T)):
+            add_and_store(nc.vector, 1, lo, hi, "window00", 4 * lo)

@@ -144,11 +144,11 @@ def tile_moe_dub_silu_kernel(
         move_scale_rows(0)
         load_a(2)
         load_w2(1, 2)
+        load_scale_rows(nc, wp_sc, wpt_scales.rearrange("e s b w -> (e s) b w"))
+        load_second(DP, 0, 1)
         load_a(3)
         load_scale_rows(nc, w1_sc, w1t_scales.rearrange("e s b w -> (e s) b w"))
         load_second(DX, 0, 1)
-        load_scale_rows(nc, wp_sc, wpt_scales.rearrange("e s b w -> (e s) b w"))
-        load_second(DP, 0, 1)
         nc.sync.dma_start(partner_list[:], offs2)
         move_scale_rows(1)
         load_scale_rows(nc, w2_sc[1], w2_rows[2 * PASSES :])
@@ -318,14 +318,14 @@ def tile_moe_dub_silu_kernel(
         activations(4)
         gate_factor(4)
         activations(5)
-        turn_a(6, 0)
         turn_back(0, 2, 1)
+        turn_a(6, 0)
         turn_a(7, 5)
         copy_back(0, 2, False)
         begin_dh(3)
         gather_words(6, 8, 1, over="factor1")
         finish_dh(nc.vector, 2)
-        quantise(0, 2)
+        quantise(0, 2, also="a_sb3")
         finish_dh(nc.vector, 3, over="dh0")
         activations(6)
         activations(7)
@@ -369,6 +369,7 @@ def tile_moe_dub_silu_kernel(
         turn_back(6, 8, 0)
         copy_back(4, 6, True)
         stage(1, OWN, 0, 1, True, over="dh_t5")
+        nc.scalar.activation(window[0][DX][:].indirect(entries(DX, 2, 3)), staged[1, (DX, 0)][:, 0:P], ACT.Copy)
         quantise(4, 6)
         pair = {(which, kt): bank([P, 2, C], "pair", 1 + 2 * kt + which) for kt in range(ROW_TILES) for which in (DP, DX)}
         for which, kt in pair:
@@ -379,18 +380,19 @@ def tile_moe_dub_silu_kernel(
         nc.scalar.copy(both[DP, 0][:, 0:C], pair[DP, 0][:, 0, :])
         quantise(6, 8)
         last = bank([P, C], "last", 7)
+        second_product(pair[DX, 0][:, 1, :], 3, DX, 0)
         second_product(last[:], 3, DP, 0)
-        for which, kt in ((DX, 0), (DX, 1), (DP, 1)):
-            second_product(pair[which, kt][:, 1, :], 3, which, kt)
-        scatter(1, DX, 0, True)
+        for which in (DP, DX):
+            second_product(pair[which, 1][:, 1, :], 3, which, 1)
         scatter(1, DX, 1, True)
+        nc.vector.tensor_copy(window[0][DX][:].indirect(entries(DX, 3, 4)), staged[1, (DX, 0)][:, P:])
         nc.scalar.activation(window[0][DP][:].indirect(entries(DP, 4, 6)), both[DP, 0][:, 0:C], ACT.Copy)
-        nc.scalar.copy(both[DP, 0][:, C:], last[:])
         nc.scalar.copy(both[DX, 0][:], pair[DX, 0][:].rearrange("p e c -> p (e c)"))
+        nc.scalar.copy(both[DP, 0][:, C:], last[:])
         nc.scalar.copy(both[DP, 1][:], pair[DP, 1][:].rearrange("p e c -> p (e c)"))
-        nc.scalar.copy(both[DX, 1][:], pair[DX, 1][:].rearrange("p e c -> p (e c)"))
         nc.scalar.activation(window[0][DP][:].indirect(entries(DP, 6, 8)), both[DP, 0][:, C:], ACT.Copy)
         nc.scalar.activation(window[1][DP][:].indirect(entries(DP, HALF, GROUPS)), both[DP, 1][:], ACT.Copy, scale=one[:])
+        nc.vector.tensor_copy(both[DX, 1][:], pair[DX, 1][:].rearrange("p e c -> p (e c)"))
         for kt in range(ROW_TILES):
             nc.vector.tensor_copy(window[kt][DX][:].indirect(entries(DX, HALF, GROUPS)), both[DX, kt][:])
         for lo in range(0, T, 512):

from contextlib import ExitStack

import concourse.mybir as mybir
from concourse.masks import make_identity

K, T, E, C, H, N = 256, 1024, 4, 256, 512, 1024
FLOPS = 2 * E * C * (N * H + 2 * H * K)

F32 = mybir.dt.float32
BF16 = mybir.dt.bfloat16
I32 = mybir.dt.int32
U32 = mybir.dt.uint32
U16 = mybir.dt.uint16
U8 = mybir.dt.uint8
FP8X4 = mybir.dt.float8_e4m3fn_x4
FP4X4 = mybir.dt.float4_e2m1fn_x4
ACT = mybir.ActivationFunctionType
ALU = mybir.AluOpType
WIDTH = {F32: 4, I32: 4, U32: 4, BF16: 2, U8: 1}

P = 128
PASSES = N // 512
SLOTS = E * C
GROUPS = SLOTS // P
PER_EXPERT = C // P
PER_COLUMN = 16
QUADRANTS = 4
MOVED_ROWS = 112
DX, DP = 0, 1
HALF = GROUPS // 2
ROW_TILES = K // P
OWN, PARTNER = ((DX, 0), (DX, 1)), ((DP, 0), (DP, 1))
UPPER, LOWER = ((DX, 0), (DP, 0)), ((DX, 1), (DP, 1))
ALIGN = 64
FAR = 208 * 1024


def load_scale_rows(nc, plane, rows):
    m = rows.shape[0]
    for r in range(4):
        nc.sync.dma_start(
            out=plane[r:P:32, :].bitcast(I32).rearrange("q (m w) -> q m w", m=m),
            in_=rows.bitcast(I32)[:, r:16:4, :].rearrange("m q w -> q m w"),
        )


def tile_moe_dub_silu_kernel(
    tc, dy_words, dy_scales, w2t_words, w2t_scales, w1t_words, w1t_scales, wpt_words, wpt_scales, a, gate, offs, offs2, out
):
    nc = tc.nc
    with ExitStack() as ctx:
        lists = ctx.enter_context(tc.tile_pool(name="lists", bufs=1))
        keep = ctx.enter_context(tc.tile_pool(name="keep", bufs=1))
        psum = ctx.enter_context(tc.psum_pool(name="psum", bufs=1))

        place = {"free": 0}

        def held(shape, dtype, name, over=None, at=0, room=0, lead=0):
            size = WIDTH[dtype]
            for n in shape[1:]:
                size = size * n
            if over is None:
                start = place["free"] + lead
                place["free"] = start + (size + room + ALIGN - 1) // ALIGN * ALIGN
                place[name] = (start, size + room, lead)
            else:
                start = place[over][0] + at
                assert at + size <= place[over][1] and -at <= place[over][2]
                place[name] = (start, place[over][1] - at, place[over][2] + at)
            return keep.tile(shape, dtype, name=name, align_bytes=ALIGN, offset=start)

        def bank(shape, name, number):
            return psum.tile(shape, F32, name=name, tag=f"bank{number}")

        token_list = lists.tile([P, SLOTS // PER_COLUMN], U16, name="token_list")
        partner_list = lists.tile([P, SLOTS // PER_COLUMN], U16, name="partner_list")

        def entries(which, lo, hi):
            return (token_list, partner_list)[which][:, lo * P // PER_COLUMN : hi * P // PER_COLUMN]

        dy_sc = held([P, T], U8, "dy_sc")
        w2_sc = [held([P, 2 * PASSES * H], U8, f"w2_sc{h}") for h in range(2)]
        w1_sc = held([P, E * K], U8, "w1_sc")
        wp_sc = held([P, E * K], U8, "wp_sc")
        slot_sc = [[held([P, HALF * P], U8, f"slot_sc{h}{s}") for s in range(PASSES)] for h in range(2)]
        nc.gpsimd.memset(dy_sc[:].bitcast(I32), 0)
        gate_rows = held([P, P], F32, "gate_rows")
        nc.vector.memset(gate_rows[:], 0.0)
        for plane in (slot_sc[0][1], w2_sc[0], wp_sc, w1_sc, slot_sc[1][1], w2_sc[1]):
            nc.vector.memset(plane[:].bitcast(I32), 0)

        one = held([P, 1], F32, "one")
        nc.gpsimd.memset(one[:], 1.0)
        ident = held([P, P], F32, "ident")
        make_identity(nc, ident[:])

        dy_w = [held([P, T], I32, f"dy_w{s}") for s in range(PASSES)]
        a_sb, w2_w, second_w = {}, {}, {}

        def load_a(e):
            a_sb[e] = held([P, 4, C], F32, f"a_sb{e}")
            nc.sync.dma_start(out=a_sb[e][:], in_=a[:, e * C : (e + 1) * C].rearrange("(c p) j -> p c j", c=4))

        def load_w2(lo, hi):
            part = held([P, (hi - lo) * PASSES, 2 * H], U8, f"w2_w{lo}")
            nc.sync.dma_start(
                out=part[:].bitcast(I32), in_=w2t_words[lo:hi].bitcast(I32).rearrange("e s p w -> p (e s) w")
            )
            for e in range(lo, hi):
                w2_w[e] = part[:, (e - lo) * PASSES : (e - lo + 1) * PASSES, :]

        def load_second(which, lo, hi):
            if which == DX:
                part = held([P, hi - lo, 2 * K], U8, f"w1_w{lo}")
                source = w1t_words[lo:hi].bitcast(I32).rearrange("e s p w -> p (e s) w")
            else:
                part = held([P, hi - lo, 4 * K], U8, f"wp_w{lo}")
                source = wpt_words[lo:hi].bitcast(I32).rearrange("e s p k d -> p (e s) (k d)")
            nc.sync.dma_start(out=part[:].bitcast(I32), in_=source)
            for e in range(lo, hi):
                second_w[which, e] = part[:, e - lo, :]

        def move_scale_rows(h):
            nc.sync.dma_start(
                out=slot_sc[h][1][0:MOVED_ROWS, :].bitcast(I32), in_=slot_sc[h][0][4 : 4 + MOVED_ROWS, :].bitcast(I32)
            )

        w2_rows = w2t_scales.rearrange("e s b w -> (e s) b w")
        load_a(0)
        nc.sync.dma_start(token_list[:], offs)
        for q in range(QUADRANTS):
            nc.sync.dma_start(
                out=dy_sc[32 * q : 32 * q + 4 * PASSES, :].bitcast(I32),
                in_=dy_scales[:, 4 * q : 4 * q + 4, :].bitcast(I32),
            )
        nc.sync.dma_start(out=gate_rows[0:GROUPS, :], in_=gate[0:1, :].rearrange("o (t c) -> (o t) c", c=P))
        nc.sync.dma_start(out=dy_w[0][:], in_=dy_words[0].rearrange("p n t -> p (n t)").bitcast(I32))
        load_a(1)
        nc.sync.dma_start(out=dy_w[1][:], in_=dy_words[1].rearrange("p n t -> p (n t)").bitcast(I32))
        for h in range(2):
            nc.vector.tensor_copy(slot_sc[h][0][:], dy_sc[:].indirect(entries(DX, h * HALF, (h + 1) * HALF)))
        load_w2(0, 1)
        load_scale_rows(nc, w2_sc[0], w2_rows[0 : 2 * PASSES])
        move_scale_rows(0)
        load_a(2)
        load_w2(1, 2)
        load_scale_rows(nc, wp_sc, wpt_scales.rearrange("e s b w -> (e s) b w"))
        load_second(DP, 0, 1)
        load_a(3)
        load_scale_rows(nc, w1_sc, w1t_scales.rearrange("e s b w -> (e s) b w"))
        load_second(DX, 0, 1)
        nc.sync.dma_start(partner_list[:], offs2)
        move_scale_rows(1)
        load_scale_rows(nc, w2_sc[1], w2_rows[2 * PASSES :])
        load_w2(2, 3)
        load_w2(3, 4)
        load_second(DP, 1, 4)
        load_second(DX, 1, 4)

        slot_w, tanh_half, silu_neg, gated, part_dh, dh_t, sums, dh, dq, products, staged, a_turned, back, sig = ({} for n in range(14))
        place["far"] = (FAR, ROW_TILES * T * 4, 0)
        window = [[None, held([P, T], F32, f"window{kt}{DP}", "far", kt * T * 4)] for kt in range(ROW_TILES)]
        window[0][DX] = held([P, T], F32, "window00")

        def gather_words(lo, hi, s, over=None, at=0):
            part = held([P, (hi - lo) * P], U32, f"slot_w{lo}{s}", over, at)
            nc.vector.tensor_copy(part[:], dy_w[s][:].bitcast(U32).indirect(entries(DX, lo, hi)))
            for t in range(lo, hi):
                slot_w[t, s] = part[:, (t - lo) * P : (t - lo + 1) * P]

        def turn_a(t, number):
            e, u = divmod(t, PER_EXPERT)
            turned = bank([P, H], "a_turned", number)
            for c in range(H // P):
                nc.tensor.transpose(turned[:, c * P : (c + 1) * P], a_sb[e][:, c, u * P : (u + 1) * P], ident[:])
            a_turned[t] = turned

        def activations(t):
            turned = a_turned[t]
            silu_neg[t] = held([P, H], F32, f"silu{t}")
            nc.scalar.activation(silu_neg[t][:], turned[:], ACT.Silu, scale=-1.0)
            tanh_half[t] = held([P, H], F32, f"tanh{t}", room=2048 if t == 6 else 0)
            nc.scalar.activation(tanh_half[t][:], turned[:], ACT.Tanh, scale=0.5)

        def gate_factor(t, over=None):
            gated[t] = held([P, H], F32, f"gated{t}", over)
            nc.gpsimd.tensor_scalar(gated[t][:], silu_neg[t][:], neg_gate[:, t : t + 1], pos_gate[:, t : t + 1], ALU.mult, ALU.add)

        def whole_factor(t):
            less = held([P, H], F32, f"less{t}")
            nc.scalar.activation(less[:], silu_neg[t][:], ACT.Copy, bias=-1.0)
            more = held([P, H], F32, f"more{t}")
            nc.scalar.activation(more[:], tanh_half[t][:], ACT.Copy, bias=1.0)
            gated[t] = held([P, H], F32, f"factor{t}")
            nc.gpsimd.tensor_tensor(gated[t][:], less[:], more[:], ALU.mult)

        def whole_dh(t, over=None):
            dh_t[t] = held([P, H], BF16, f"dh_t{t}", over)
            nc.vector.scalar_tensor_tensor(dh_t[t][:], sums[t][:], neg_gate[:, t : t + 1], gated[t][:], ALU.mult, ALU.mult)

        def first_product(t, number):
            e = t // PER_EXPERT
            sums[t] = bank([P, H], "sums", number)
            for s in range(PASSES):
                m = e % 2 * PASSES + s
                nc.tensor.matmul_mx(
                    out=sums[t][:],
                    lhsT=slot_w[t, s].bitcast(FP8X4),
                    lhsT_scale=slot_sc[t // HALF][s][:, t % HALF * P : (t % HALF + 1) * P],
                    rhs=w2_w[e][:, s, :].bitcast(FP4X4),
                    rhs_scale=w2_sc[t // HALF][:, m * H : (m + 1) * H],
                    start=(s == 0),
                    stop=(s == PASSES - 1),
                )

        def begin_dh(t, over=None, at=0):
            part_dh[t] = held([P, H], F32, f"part{t}", over, at, room=1024, lead=1024)
            nc.vector.scalar_tensor_tensor(part_dh[t][:], tanh_half[t][:], 1.0, sums[t][:], ALU.add, ALU.mult)

        def finish_dh(engine, t, over=None, at=0):
            dh_t[t] = held([P, H], BF16, f"dh_t{t}", over, at, room=1024)
            engine.tensor_tensor(dh_t[t][:], part_dh[t][:], gated[t][:], ALU.mult)

        def turn_back(lo, hi, number):
            back[lo] = bank([P, hi - lo, 2, P], "back", number)
            for t in range(lo, hi):
                pairs = dh_t[t][:].bitcast(F32)
                for v in range(2):
                    nc.tensor.transpose(back[lo][:, t - lo, v, :], pairs[:, v : H // 2 : 2], ident[:])

        def copy_back(lo, hi, on_vector, over=None, at=0):
            dh[lo] = held([P, (hi - lo) * H], BF16, f"dh{lo}", over, at, room=1024)
            target = dh[lo][:].bitcast(F32).rearrange("p (u j v) -> p u j v", u=hi - lo, v=2)
            if on_vector:
                nc.vector.tensor_copy(target, back[lo][:].rearrange("p u v j -> p u j v"))
            else:
                nc.scalar.copy(target, back[lo][:].rearrange("p u v j -> p u j v"))

        def quantise(lo, hi, over=None, also=None):
            codes = held([P, (hi - lo) * P], U32, f"dq_w{lo}", over, room=1024)
            scales = held([P, (hi - lo) * P], U8, f"dq_sc{lo}", also)
            nc.vector.quantize_mx(out=codes[:].bitcast(FP8X4), scales=scales[:], in_=dh[lo][:])
            dq[lo] = (codes, scales)

        def second_product(target, e, which, kt):
            codes, scales = dq[PER_EXPERT * e]
            if which == DX:
                words, plane = second_w[DX, e][:, 2 * kt * P : 2 * (kt + 1) * P].bitcast(FP4X4), w1_sc
            else:
                words, plane = second_w[DP, e][:, 4 * kt * P : 4 * (kt + 1) * P].bitcast(FP8X4), wp_sc
            nc.tensor.matmul_mx(
                out=target,
                lhsT=words,
                lhsT_scale=plane[:, e * K + kt * P : e * K + (kt + 1) * P],
                rhs=codes[:].bitcast(FP8X4),
                rhs_scale=scales[:],
                start=True,
                stop=True,
            )

        def second_products(e, parts, number):
            products[e, parts] = bank([P, len(parts), C], "products", number)
            for n, (which, kt) in enumerate(parts):
                second_product(products[e, parts][:, n, :], e, which, kt)

        def stage(e, parts, lo, hi, on_vector, over=None, at=0):
            part = held([P, hi - lo, C], F32, f"staged{e}{parts[lo][0]}{parts[lo][1]}", over, at, room=1024)
            if on_vector:
                nc.vector.tensor_copy(part[:], products[e, parts][:, lo:hi, :])
            else:
                nc.scalar.copy(part[:], products[e, parts][:, lo:hi, :])
            for n in range(lo, hi):
                staged[e, parts[n]] = part[:, n - lo, :]

        def scatter(e, which, kt, on_vector):
            target = window[kt][which][:].indirect(entries(which, PER_EXPERT * e, PER_EXPERT * (e + 1)))
            if on_vector:
                nc.vector.tensor_copy(target, staged[e, (which, kt)])
            else:
                nc.scalar.activation(target, staged[e, (which, kt)], ACT.Copy)

        def add_and_store(adder, kt, lo, hi, over=None, at=0):
            total = held([P, hi - lo], F32, f"total{kt}_{lo}", over, at)
            adder.tensor_tensor(total[:], window[kt][DX][:, lo:hi], window[kt][DP][:, lo:hi], ALU.add)
            nc.sync.dma_start(out=out[kt * P : (kt + 1) * P, lo:hi], in_=total[:])

        turn_a(0, 0)
        turn_a(1, 1)
        gate_turned = bank([P, P], "gate_turned", 4)
        nc.tensor.transpose(gate_turned[:], gate_rows[:], ident[:])
        for t in range(2):
            activations(t)
            whole_factor(t)
        neg_gate = held([P, GROUPS], F32, "neg_gate")
        pos_gate = held([P, GROUPS], F32, "pos_gate")
        nc.vector.tensor_scalar(neg_gate[:], gate_turned[:, 0:GROUPS], -0.5, None, ALU.mult)
        nc.gpsimd.tensor_scalar(pos_gate[:], neg_gate[:], -1.0, 0.0, ALU.mult, ALU.add)
        turn_a(2, 7)
        turn_a(3, 0)
        activations(2)
        activations(3)
        gather_words(0, HALF, 0)
        gather_words(HALF, GROUPS, 0)
        gather_words(0, 2, 1)
        gather_words(2, HALF, 1)
        gate_factor(2)
        gate_factor(3)
        first_product(0, 2)
        first_product(1, 3)
        turn_a(4, 1)
        turn_a(5, 7)
        first_product(2, 5)
        first_product(3, 6)
        whole_dh(0)
        whole_dh(1)
        gather_words(4, 6, 1, over="factor0")
        begin_dh(2)
        activations(4)
        gate_factor(4)
        activations(5)
        turn_back(0, 2, 1)
        turn_a(6, 0)
        turn_a(7, 5)
        copy_back(0, 2, False)
        begin_dh(3)
        gather_words(6, 8, 1, over="factor1")
        finish_dh(nc.vector, 2)
        quantise(0, 2, also="a_sb3")
        finish_dh(nc.vector, 3, over="dh0")
        activations(6)
        activations(7)
        second_products(0, OWN[:1], 2)
        second_products(0, OWN[1:], 3)
        second_products(0, PARTNER, 4)
        stage(0, OWN[:1], 0, 1, True)
        stage(0, OWN[1:], 0, 1, True)
        turn_back(2, 4, 2)
        first_product(4, 5)
        first_product(5, 6)
        first_product(6, 7)
        first_product(7, 0)
        gate_factor(5, over="gated3")
        gate_factor(6, over="part3")
        gate_factor(7, over="silu5")
        scatter(0, DX, 0, True)
        stage(0, PARTNER, 0, 1, False)
        stage(0, PARTNER, 1, 2, False)
        scatter(0, DP, 0, False)
        scatter(0, DP, 1, False)
        copy_back(2, 4, True)
        begin_dh(4, over="staged000")
        quantise(2, 4)
        begin_dh(5)
        begin_dh(6)
        begin_dh(7)
        window[1][DX] = held([P, T], F32, "window10", "tanh6")
        scatter(0, DX, 1, True)
        second_products(1, PARTNER, 5)
        second_products(1, OWN, 6)
        finish_dh(nc.gpsimd, 4, over="dh2")
        finish_dh(nc.gpsimd, 5, over="dh2", at=1024)
        stage(1, PARTNER, 0, 1, False)
        stage(1, PARTNER, 1, 2, False)
        scatter(1, DP, 0, False)
        scatter(1, DP, 1, False)
        finish_dh(nc.vector, 6, over="part5")
        finish_dh(nc.vector, 7, over="part5", at=1024)
        turn_back(4, 6, 5)
        turn_back(6, 8, 0)
        copy_back(4, 6, True)
        stage(1, OWN, 0, 1, True, over="dh_t5")
        nc.scalar.activation(window[0][DX][:].indirect(entries(DX, 2, 3)), staged[1, (DX, 0)][:, 0:P], ACT.Copy)
        quantise(4, 6)
        pair = {(which, kt): bank([P, 2, C], "pair", 1 + 2 * kt + which) for kt in range(ROW_TILES) for which in (DP, DX)}
        for which, kt in pair:
            second_product(pair[which, kt][:, 0, :], 2, which, kt)
        copy_back(6, 8, True)
        stage(1, OWN, 1, 2, True, over="dh_t7")
        both = {key: held([P, 2 * C], F32, f"both{key[0]}{key[1]}") for key in pair}
        nc.scalar.copy(both[DP, 0][:, 0:C], pair[DP, 0][:, 0, :])
        quantise(6, 8)
        last = bank([P, C], "last", 7)
        second_product(pair[DX, 0][:, 1, :], 3, DX, 0)
        second_product(last[:], 3, DP, 0)
        for which in (DP, DX):
            second_product(pair[which, 1][:, 1, :], 3, which, 1)
        scatter(1, DX, 1, True)
        nc.vector.tensor_copy(window[0][DX][:].indirect(entries(DX, 3, 4)), staged[1, (DX, 0)][:, P:])
        nc.scalar.activation(window[0][DP][:].indirect(entries(DP, 4, 6)), both[DP, 0][:, 0:C], ACT.Copy)
        nc.scalar.copy(both[DX, 0][:], pair[DX, 0][:].rearrange("p e c -> p (e c)"))
        nc.scalar.copy(both[DP, 0][:, C:], last[:])
        nc.scalar.copy(both[DP, 1][:], pair[DP, 1][:].rearrange("p e c -> p (e c)"))
        nc.scalar.activation(window[0][DP][:].indirect(entries(DP, 6, 8)), both[DP, 0][:, C:], ACT.Copy)
        nc.scalar.activation(window[1][DP][:].indirect(entries(DP, HALF, GROUPS)), both[DP, 1][:], ACT.Copy, scale=one[:])
        nc.vector.tensor_copy(both[DX, 1][:], pair[DX, 1][:].rearrange("p e c -> p (e c)"))
        for kt in range(ROW_TILES):
            nc.vector.tensor_copy(window[kt][DX][:].indirect(entries(DX, HALF, GROUPS)), both[DX, kt][:])
        for lo in range(0, T, 512):
            add_and_store(nc.gpsimd, 0, lo, lo + 512)
        for lo, hi in ((0, 128), (128, 384), (384, 704), (704, T)):
            add_and_store(nc.vector, 1, lo, hi, "window00", 4 * lo)
